import numpy as np
import ml_dtypes


def mxq(x, axis, fmt="e4m3"):
    dtype, down = {"e4m3": (ml_dtypes.float8_e4m3fn, 7), "e5m2": (ml_dtypes.float8_e5m2, 14)}[fmt]
    v = np.moveaxis(np.asarray(x, np.float32).astype(ml_dtypes.bfloat16).astype(np.float64), axis, -1)
    blocks = v.reshape(v.shape[:-1] + (-1, 32))
    amax = np.abs(blocks).max(-1, keepdims=True)
    byte = np.maximum(np.where(amax > 0, np.frexp(amax)[1] - 1 + 127, 0) - down, 1)
    scale = np.exp2(byte - 127.0)
    codes = (blocks / scale).astype(np.float32).astype(dtype).astype(np.float64)
    return np.moveaxis((codes * scale).reshape(v.shape), -1, axis)


WIDE = False


def mx_kscale(k):
    if not WIDE:
        return np.ones(k)
    levels = np.array([10, -10, 5, -5, 0])
    if k % 512:
        return np.exp2(np.random.permutation(np.resize(levels, k // 32))).repeat(32)
    a = np.empty((k // 512, 16))
    for p in range(k // 512):
        a[p, :8] = np.random.permutation(np.resize(levels, 8))
        for g in range(8):
            far = levels[np.abs(levels - a[p, g]) >= 10]
            a[p, g + 8] = far[np.random.randint(len(far))]
    return np.exp2(a.ravel()).repeat(32)


def f64(x):
    return np.asarray(x).astype(np.float64)


def striped(idx):
    return np.tile(np.asarray(idx).reshape(-1, 16).T, (8, 1)).astype(np.uint16)


def unstriped(offs):
    return offs[:16].T.reshape(-1).astype(np.int64)


E2M1 = np.array([0.0, 0.5, 1.0, 1.5, 2.0, 3.0, 4.0, 6.0, -0.0, -0.5, -1.0, -1.5, -2.0, -3.0, -4.0, -6.0])


def pack_weight(w, fmt):
    k, n = w.shape
    w = f64(np.asarray(w, np.float32).astype(ml_dtypes.bfloat16)).reshape(k // 32, 32, n)
    amax = np.abs(w).max(1)
    if fmt == "e4m3":
        byte = np.frexp(amax)[1] - 1 + 127 - 7
    else:
        mant, ex = np.frexp(amax / 6.0)
        byte = np.where(mant > 0.5, ex, ex - 1) + 127
    byte = np.clip(np.where(amax > 0, byte, 1), 1, 254)
    scaled = (w * np.exp2(127.0 - byte)[:, None, :]).reshape(k, n).astype(np.float32)
    by_word = np.ascontiguousarray(scaled.reshape(k // 512, 128, 4, n).transpose(0, 1, 3, 2))
    if fmt == "e4m3":
        words = by_word.astype(ml_dtypes.float8_e4m3fn).view(np.uint8)
    else:
        c = by_word.astype(ml_dtypes.float4_e2m1fn).view(np.uint8) & 0xF
        words = (c[..., 0::2] | (c[..., 1::2] << 4)).reshape(k // 512, 128, 2 * n)
    return np.ascontiguousarray(words), np.ascontiguousarray(byte.astype(np.uint8).reshape(k // 512, 16, n))


def unpack_weight(words, scales, fmt):
    g, _, n = scales.shape
    words = np.ascontiguousarray(words).reshape(g, 128, n, -1)
    if fmt == "e4m3":
        vals = words.view(ml_dtypes.float8_e4m3fn).astype(np.float64)
    else:
        nib = np.empty((g, 128, n, 4), np.uint8)
        nib[..., 0::2] = words & 0xF
        nib[..., 1::2] = words >> 4
        vals = E2M1[nib]
    vals = vals * np.repeat(np.exp2(scales.astype(np.float64) - 127.0), 8, axis=1)[..., None]
    return vals.transpose(0, 1, 3, 2).reshape(g * 512, n)


B, N, T, D, DV, NQ = 2, 512, 2048, 1024, 256, 128
PAGE = 64
DRAFT = 128


def setup_inputs():
    n = np.random.standard_normal
    pages = np.random.permutation(T // PAGE)[:B * N // PAGE]
    idx = (pages[:, None] * PAGE + np.arange(PAGE)[None, :]).reshape(-1)
    s = mx_kscale(D)[:, None]
    u = np.ones(T)
    u[idx] = mx_kscale(B * N)
    r = np.random.uniform(0.5, 2.0, T)
    k = n((D, T)) / s
    v = n((DV, T)) / (u * r)
    kp = pack_weight(k, "e2m1")
    when = np.zeros(T)
    when[idx] = np.concatenate([np.concatenate([np.arange(N - DRAFT), N - DRAFT + np.random.randint(0, 16, DRAFT)]) for b in range(B)])
    return {
        "qT": (n((B, D, NQ)) * s * (1.00 / np.sqrt(D))).astype(np.float32),
        "k_words": np.ascontiguousarray(kp[0].reshape(D // 1024, 2, 128, T, 2).transpose(0, 2, 3, 1, 4)).reshape(D // 1024, 128, T, 4),
        "k_scales": kp[1],
        "vT": v.astype(np.float32),
        "vs": np.tile(u * r, (128, 1)).astype(np.float32),
        "pos": np.tile(when, (128, 1)).astype(np.float32),
        "qpos": np.random.randint(N - DRAFT, N - DRAFT + 16, (B, NQ, 1)).astype(np.float32),
        "offs": striped(idx),
    }


def reference(qT, k_words, k_scales, vT, vs, pos, qpos, offs):
    idx = unstriped(offs)
    k = unpack_weight(k_words.reshape(D // 1024, 128, T, 2, 2).transpose(0, 3, 1, 2, 4).reshape(D // 512, 128, 2 * T), k_scales, "e2m1")
    v = f64(vT)
    pick = lambda x: x[:, idx].reshape(x.shape[0], B, N).transpose(1, 0, 2)
    q = f64(qT)
    score = mxq(q, 1, "e4m3").transpose(0, 2, 1) @ pick(k)
    score = np.where(pick(f64(pos))[:, :1, :] <= f64(qpos), score, -30000.0)
    m = score.max(-1, keepdims=True)
    p = np.exp(score - m)
    total = p.sum(-1, keepdims=True)
    w = p * pick(f64(vs))[:, :1, :]
    y = mxq(w, 2, "e4m3") @ mxq(pick(v).transpose(0, 2, 1), 1, "e4m3")
    y = y / total
    return y

@@ -1,0 +1,185 @@
+from contextlib import ExitStack
+
+import concourse.mybir as mybir
+from concourse.masks import make_identity
+
+B, N, T, D, DV, NQ = 2, 512, 2048, 1024, 256, 128
+FLOPS = 2 * B * NQ * N * (D + DV)
+
+F32 = mybir.dt.float32
+BF16 = mybir.dt.bfloat16
+I32 = mybir.dt.int32
+U32 = mybir.dt.uint32
+U16 = mybir.dt.uint16
+U8 = mybir.dt.uint8
+FP8X4 = mybir.dt.float8_e4m3fn_x4
+FP4X4 = mybir.dt.float4_e2m1fn_x4
+ALU = mybir.AluOpType
+ACT = mybir.ActivationFunctionType
+
+P = 128
+PACK = 4
+PASSES = D // (P * PACK)
+COLS = N // 16
+MASKED = 30000.0
+FAR = float(2 ** 60)
+
+
+def tile_attend_draft_kernel(tc, qT, k_words, k_scales, vT, vs, pos, qpos, offs, out):
+    nc = tc.nc
+    with ExitStack() as ctx:
+        lists = ctx.enter_context(tc.tile_pool(name="lists", bufs=1))
+        sb = ctx.enter_context(tc.tile_pool(name="sb", bufs=1))
+        ps = ctx.enter_context(tc.psum_pool(name="ps", bufs=1))
+
+        def bank(tag, shape):
+            return ps.tile(shape, F32, name=tag, tag=tag)
+
+        offs_t = lists.tile([P, B * COLS], U16)
+        nc.sync.dma_start(offs_t[:], offs)
+        seq_offs = [offs_t[:, b * COLS:(b + 1) * COLS] for b in range(B)]
+
+        kw_win = sb.tile([P, T], I32, tag="first")
+        nc.sync.dma_start(kw_win[:], k_words[0].rearrange("p t c -> p (t c)").bitcast(I32))
+        q_raw = sb.tile([P, B * PASSES, PACK, NQ], F32)
+        nc.sync.dma_start(q_raw[:].rearrange("p g j q -> p g (j q)"),
+                          qT.rearrange("b (o p j) q -> p (b o) (j q)", p=P, j=PACK))
+
+        warm = sb.tile([P, 1], F32)
+        nc.gpsimd.memset(warm[:], 0.0)
+        warm_out = sb.tile([P, 1], F32)
+        nc.scalar.activation(warm_out[:], warm[:], ACT.Exp)
+        qpos_t = sb.tile([P, B], F32)
+        with nc.allow_non_contiguous_dma(reason="one place a query row"):
+            nc.gpsimd.dma_start(qpos_t[:], qpos.rearrange("b q o -> q (b o)"))
+        ident = sb.tile([P, P], F32)
+        make_identity(nc, ident[:])
+
+        pos_win = sb.tile([P, T], F32, tag="second")
+        nc.vector.memset(pos_win[:], 0.0)
+        nc.scalar.dma_start(pos_win[0:1, :], pos[0:1, :])
+        ks_win = sb.tile([P, PASSES, T // 4], I32)
+        nc.vector.memset(ks_win[:], 0)
+        ks_rows = k_scales.bitcast(I32).rearrange("o f t -> f o t")
+        for r in range(4):
+            nc.scalar.dma_start(ks_win[r:P:32, :, :], ks_rows[r:16:4, :, :])
+        vs_win = sb.tile([P, T], F32)
+        nc.vector.memset(vs_win[:], 0.0)
+        nc.scalar.dma_start(vs_win[0:1, :], vs[0:1, :])
+
+        kw_g = sb.tile([P, B * N], U32)
+        nc.vector.tensor_copy(kw_g[:], kw_win[:].bitcast(U32).indirect(offs_t[:]))
+        v1_raw = sb.tile([P, T], F32, tag="first")
+        nc.sync.dma_start(v1_raw[:], vT[P:2 * P, :])
+        pos_g = sb.tile([P, B * N], F32)
+        nc.vector.tensor_copy(pos_g[:], pos_win[:].indirect(offs_t[:]))
+        v0_win = sb.tile([P, T], F32, tag="second")
+        nc.sync.dma_start(v0_win[:], vT[0:P, :])
+
+        qbias = sb.tile([P, B], F32)
+        nc.scalar.activation(qbias[:], qpos_t[:], ACT.Copy, scale=-FAR)
+        q_bf = sb.tile([P, B * PASSES, NQ, PACK], BF16, align_bytes=64)
+        pos_col = sb.tile([P, B, PACK], F32)
+        past = sb.tile([P, B, N], F32)
+        for b in range(B):
+            g = slice(b * PASSES, (b + 1) * PASSES)
+            nc.scalar.activation(q_bf[:, g], q_raw[:, g].rearrange("p g j q -> p g q j"), ACT.Copy)
+            turned = bank("a%d" % b, [P, PACK, P])
+            for c in range(PACK):
+                nc.tensor.transpose(turned[:, c, :], pos_g[:, b * N + c * P:b * N + (c + 1) * P], ident[:])
+            nc.scalar.copy(pos_col[:, b, :], turned[:, :, 0])
+        for b in range(B):
+            spread = bank("b%d" % b, [P, PACK, P])
+            for c in range(PACK):
+                nc.tensor.transpose(spread[:, c, :], pos_col[:, b, c:c + 1].to_broadcast([P, P]), ident[:])
+            nc.scalar.activation(past[:, b, :], spread[:].rearrange("q c s -> q (c s)"), ACT.Relu,
+                                 bias=qbias[:, b:b + 1], scale=FAR)
+
+        ks_g = sb.tile([P, B, PASSES, N], U8, align_bytes=64)
+        keys = sb.tile([P, B, PASSES, 2 * N], U8, align_bytes=64)
+        q_codes = sb.tile([P, B * PASSES * NQ], U32, align_bytes=64)
+        q_scales = sb.tile([P, B * PASSES * NQ], U8, align_bytes=64)
+        scores = []
+        for b in range(B):
+            g = slice(b * PASSES, (b + 1) * PASSES)
+            cols = slice(b * PASSES * NQ, (b + 1) * PASSES * NQ)
+            nc.vector.tensor_copy(keys[:, b].bitcast(U16),
+                                  kw_g[:, b * N:(b + 1) * N].bitcast(U16).rearrange("p (n o) -> p o n", o=PASSES))
+            for o in range(PASSES):
+                nc.vector.tensor_copy(ks_g[:, b, o, :], ks_win[:, o, :].bitcast(U8).indirect(seq_offs[b]))
+            nc.vector.quantize_mx(q_codes[:, cols].bitcast(FP8X4), q_scales[:, cols],
+                                  q_bf[:, g].rearrange("p g q j -> p (g q j)"))
+            acc = bank("c%d" % b, [P, N])
+            for o in range(PASSES):
+                qc = slice((b * PASSES + o) * NQ, (b * PASSES + o + 1) * NQ)
+                nc.tensor.matmul_mx(acc[:], lhsT=q_codes[:, qc].bitcast(FP8X4), lhsT_scale=q_scales[:, qc],
+                                    rhs=keys[:, b, o, :].bitcast(FP4X4), rhs_scale=ks_g[:, b, o, :],
+                                    start=(o == 0), stop=(o == PASSES - 1))
+            scores.append(acc)
+
+        v1_win = sb.tile([P, T], BF16)
+        nc.scalar.activation(v1_win[:], v1_raw[:], ACT.Copy)
+        v_g = [sb.tile([P, 2, B * P, 2], BF16, name="v_g%d" % c) for c in range(2)]
+        nc.scalar.activation(v_g[1][:].rearrange("e u p w -> e p u w"), v1_win[:].indirect(offs_t[:]), ACT.Copy)
+
+        neg = sb.tile([P, B, N], F32)
+        nc.vector.tensor_tensor(neg[:, 0, :], past[:, 0, :], scores[0][:], ALU.subtract)
+        vs_g = sb.tile([P, B * N], F32)
+        nc.vector.tensor_copy(vs_g[:], vs_win[:].indirect(offs_t[:]))
+        nc.vector.tensor_tensor(neg[:, 1, :], past[:, 1, :], scores[1][:], ALU.subtract)
+        vs_col = sb.tile([P, B, PACK], F32)
+        for b in range(B):
+            turned = bank("a%d" % b, [P, PACK, P])
+            for t in range(PACK):
+                nc.tensor.transpose(turned[:, t, :], vs_g[:, b * N + t:(b + 1) * N:PACK], ident[:])
+            nc.scalar.copy(vs_col[:, b, :], turned[:, :, 0])
+
+        clamped = sb.tile([P, B, N], F32)
+        neg_max = [sb.tile([P, 1], F32, name="neg_max%d" % b) for b in range(B)]
+        total = [sb.tile([P, 1], F32, name="total%d" % b) for b in range(B)]
+        prob = sb.tile([P, B, PACK, P], F32)
+        turned_p = []
+        for b in range(B):
+            nc.vector.tensor_scalar(clamped[:, b, :], neg[:, b, :], MASKED, None, ALU.min, ALU.min,
+                                    accum_out=neg_max[b][:])
+            nc.scalar.activation(prob[:, b].rearrange("q t s -> q s t"),
+                                 clamped[:, b, :].rearrange("q (s t) -> q s t", t=PACK), ACT.Exp,
+                                 bias=neg_max[b][:], scale=-1.0, accum_out=total[b][:])
+            tp = bank("b%d" % b, [P, PACK, NQ])
+            for t in range(PACK):
+                nc.tensor.transpose(tp[:, t, :], prob[:, b, t, :], ident[:])
+            turned_p.append(tp)
+
+        nc.vector.tensor_copy(v_g[0][:].rearrange("e u p w -> e p u w"), v0_win[:].indirect(offs_t[:]))
+        v_bf = sb.tile([P, B, DV, PACK], BF16, align_bytes=64)
+        for b in range(B):
+            tv = bank("d%d" % b, [P, 2, 2, P])
+            for c in (1, 0):
+                words = v_g[c][:].bitcast(F32)
+                for u in range(2):
+                    nc.tensor.transpose(tv[:, c, u, :], words[:, u, b * P:(b + 1) * P, 0], ident[:])
+            nc.scalar.copy(v_bf[:, b].bitcast(F32).rearrange("p (c e) u -> p c e u", c=2),
+                           tv[:].rearrange("p c u e -> p c e u"))
+
+        w_bf = sb.tile([P, B, NQ, PACK], BF16, align_bytes=64)
+        w_codes = sb.tile([P, B, NQ], U32, align_bytes=64)
+        w_scales = sb.tile([P, B, NQ], U8, align_bytes=64)
+        v_codes = sb.tile([P, B, DV], U32, align_bytes=64)
+        v_scales = sb.tile([P, B, DV], U8, align_bytes=64)
+        inv = [sb.tile([P, 1], F32, name="inv%d" % b) for b in range(B)]
+        y = sb.tile([P, B, DV], F32)
+        for b in range(B):
+            nc.vector.tensor_tensor(w_bf[:, b], turned_p[b][:].rearrange("p t q -> p q t"),
+                                    vs_col[:, b, :].unsqueeze(1).to_broadcast([P, NQ, PACK]), ALU.mult)
+            nc.vector.reciprocal(inv[b][:], total[b][:])
+        for b in range(B):
+            nc.vector.quantize_mx(v_codes[:, b, :].bitcast(FP8X4), v_scales[:, b, :],
+                                  v_bf[:, b].rearrange("p e t -> p (e t)"))
+            nc.vector.quantize_mx(w_codes[:, b, :].bitcast(FP8X4), w_scales[:, b, :],
+                                  w_bf[:, b].rearrange("p q t -> p (q t)"))
+            acc = bank("a%d" % b, [P, DV])
+            nc.tensor.matmul_mx(acc[:], lhsT=w_codes[:, b, :].bitcast(FP8X4), lhsT_scale=w_scales[:, b, :],
+                                rhs=v_codes[:, b, :].bitcast(FP8X4), rhs_scale=v_scales[:, b, :],
+                                start=True, stop=True)
+            nc.scalar.activation(y[:, b, :], acc[:], ACT.Copy, scale=inv[b][:])
+            nc.sync.dma_start(out[b], y[:, b, :])

@@ -39,51 +39,54 @@ def tile_attend_draft_kernel(tc, qT, k_words, k_scales, vT, vs, pos, qpos, offs,
         nc.sync.dma_start(offs_t[:], offs)
         seq_offs = [offs_t[:, b * COLS:(b + 1) * COLS] for b in range(B)]
 
-        kw_win = sb.tile([P, T], I32, tag="first")
-        nc.sync.dma_start(kw_win[:], k_words[0].rearrange("p t c -> p (t c)").bitcast(I32))
-        q_raw = sb.tile([P, B * PASSES, PACK, NQ], F32)
-        nc.sync.dma_start(q_raw[:].rearrange("p g j q -> p g (j q)"),
-                          qT.rearrange("b (o p j) q -> p (b o) (j q)", p=P, j=PACK))
-
-        warm = sb.tile([P, 1], F32)
-        nc.gpsimd.memset(warm[:], 0.0)
-        warm_out = sb.tile([P, 1], F32)
-        nc.scalar.activation(warm_out[:], warm[:], ACT.Exp)
-        qpos_t = sb.tile([P, B], F32)
+        qpos_t = sb.tile([P, B], F32, tag="qpos_then_q")
         with nc.allow_non_contiguous_dma(reason="one place a query row"):
-            nc.gpsimd.dma_start(qpos_t[:], qpos.rearrange("b q o -> q (b o)"))
+            nc.sync.dma_start(qpos_t[:], qpos.rearrange("b q o -> q (b o)"))
+        ks_rows = k_scales.bitcast(I32).rearrange("o f t -> f o t")
+        ks_win = sb.tile([P, T // 4], I32, tag="ks_then_kw")
+        nc.vector.memset(ks_win[:], 0)
+        for r in range(4):
+            nc.sync.dma_start(ks_win[r:P:16, :], ks_rows[r:16:4, :, :])
+        pos_win = sb.tile([P, T], F32, tag="pos_then_v1")
+        nc.vector.memset(pos_win[:], 0.0)
+        nc.sync.dma_start(pos_win[0:1, :], pos[0:1, :])
+        vs_win = sb.tile([P, T], F32, tag="vs_then_v0")
+        nc.vector.memset(vs_win[:], 0.0)
+        nc.sync.dma_start(vs_win[0:1, :], vs[0:1, :])
+        qbias = sb.tile([P, B], F32)
+        nc.vector.tensor_scalar(qbias[:], qpos_t[:], -FAR, None, ALU.mult)
+        q_raw = sb.tile([P, B, PASSES, PACK * NQ], F32, tag="qpos_then_q")
+        for b in range(B):
+            nc.sync.dma_start(q_raw[:, b], qT[b].rearrange("(o p j) q -> p o (j q)", p=P, j=PACK))
         ident = sb.tile([P, P], F32)
         make_identity(nc, ident[:])
+        ks_low = sb.tile([P, B * N // 4], I32, align_bytes=64)
+        nc.vector.memset(ks_low[96:P, :], 0)
 
-        pos_win = sb.tile([P, T], F32, tag="second")
-        nc.vector.memset(pos_win[:], 0.0)
-        nc.scalar.dma_start(pos_win[0:1, :], pos[0:1, :])
-        ks_win = sb.tile([P, PASSES, T // 4], I32)
-        nc.vector.memset(ks_win[:], 0)
-        ks_rows = k_scales.bitcast(I32).rearrange("o f t -> f o t")
-        for r in range(4):
-            nc.scalar.dma_start(ks_win[r:P:32, :, :], ks_rows[r:16:4, :, :])
-        vs_win = sb.tile([P, T], F32)
-        nc.vector.memset(vs_win[:], 0.0)
-        nc.scalar.dma_start(vs_win[0:1, :], vs[0:1, :])
-
-        kw_g = sb.tile([P, B * N], U32)
-        nc.vector.tensor_copy(kw_g[:], kw_win[:].bitcast(U32).indirect(offs_t[:]))
-        v1_raw = sb.tile([P, T], F32, tag="first")
-        nc.sync.dma_start(v1_raw[:], vT[P:2 * P, :])
+        ks_g = sb.tile([P, B * N], U8, align_bytes=64)
+        nc.vector.tensor_copy(ks_g[:], ks_win[:].bitcast(U8).indirect(offs_t[:]))
+        nc.sync.dma_start(ks_low[0:P - 16, :], ks_g[16:P, :].bitcast(I32))
+        ks_plane = [ks_g[:], ks_low[:].bitcast(U8)]
+        kw_win = sb.tile([P, T], I32, tag="ks_then_kw")
+        nc.sync.dma_start(kw_win[:], k_words[0].rearrange("p t c -> p (t c)").bitcast(I32))
         pos_g = sb.tile([P, B * N], F32)
         nc.vector.tensor_copy(pos_g[:], pos_win[:].indirect(offs_t[:]))
-        v0_win = sb.tile([P, T], F32, tag="second")
+        v1_raw = sb.tile([P, T], F32, tag="pos_then_v1")
+        for h in range(2):
+            nc.sync.dma_start(v1_raw[:, h * 1024:(h + 1) * 1024], vT[P:2 * P, h * 1024:(h + 1) * 1024])
+        vs_g = sb.tile([P, B * N], F32)
+        nc.vector.tensor_copy(vs_g[:], vs_win[:].indirect(offs_t[:]))
+        v0_win = sb.tile([P, T], F32, tag="vs_then_v0")
         nc.sync.dma_start(v0_win[:], vT[0:P, :])
+        kw_g = sb.tile([P, B * N], U32)
 
-        qbias = sb.tile([P, B], F32)
-        nc.scalar.activation(qbias[:], qpos_t[:], ACT.Copy, scale=-FAR)
         q_bf = sb.tile([P, B * PASSES, NQ, PACK], BF16, align_bytes=64)
-        pos_col = sb.tile([P, B, PACK], F32)
         past = sb.tile([P, B, N], F32)
         for b in range(B):
             g = slice(b * PASSES, (b + 1) * PASSES)
-            nc.scalar.activation(q_bf[:, g], q_raw[:, g].rearrange("p g j q -> p g q j"), ACT.Copy)
+            nc.scalar.activation(q_bf[:, g], q_raw[:, b].rearrange("p g (j q) -> p g q j", j=PACK), ACT.Copy)
+        pos_col = sb.tile([P, B, PACK], F32, tag="qpos_then_q")
+        for b in range(B):
             turned = bank("a%d" % b, [P, PACK, P])
             for c in range(PACK):
                 nc.tensor.transpose(turned[:, c, :], pos_g[:, b * N + c * P:b * N + (c + 1) * P], ident[:])
@@ -95,7 +98,6 @@ def tile_attend_draft_kernel(tc, qT, k_words, k_scales, vT, vs, pos, qpos, offs,
             nc.scalar.activation(past[:, b, :], spread[:].rearrange("q c s -> q (c s)"), ACT.Relu,
                                  bias=qbias[:, b:b + 1], scale=FAR)
 
-        ks_g = sb.tile([P, B, PASSES, N], U8, align_bytes=64)
         keys = sb.tile([P, B, PASSES, 2 * N], U8, align_bytes=64)
         q_codes = sb.tile([P, B * PASSES * NQ], U32, align_bytes=64)
         q_scales = sb.tile([P, B * PASSES * NQ], U8, align_bytes=64)
@@ -103,30 +105,28 @@ def tile_attend_draft_kernel(tc, qT, k_words, k_scales, vT, vs, pos, qpos, offs,
         for b in range(B):
             g = slice(b * PASSES, (b + 1) * PASSES)
             cols = slice(b * PASSES * NQ, (b + 1) * PASSES * NQ)
-            nc.vector.tensor_copy(keys[:, b].bitcast(U16),
-                                  kw_g[:, b * N:(b + 1) * N].bitcast(U16).rearrange("p (n o) -> p o n", o=PASSES))
-            for o in range(PASSES):
-                nc.vector.tensor_copy(ks_g[:, b, o, :], ks_win[:, o, :].bitcast(U8).indirect(seq_offs[b]))
+            nc.vector.tensor_copy(kw_g[:, b * N:(b + 1) * N], kw_win[:].bitcast(U32).indirect(seq_offs[b]))
             nc.vector.quantize_mx(q_codes[:, cols].bitcast(FP8X4), q_scales[:, cols],
                                   q_bf[:, g].rearrange("p g q j -> p (g q j)"))
+            nc.vector.tensor_copy(keys[:, b].bitcast(U16),
+                                  kw_g[:, b * N:(b + 1) * N].bitcast(U16).rearrange("p (n o) -> p o n", o=PASSES))
             acc = bank("c%d" % b, [P, N])
             for o in range(PASSES):
                 qc = slice((b * PASSES + o) * NQ, (b * PASSES + o + 1) * NQ)
                 nc.tensor.matmul_mx(acc[:], lhsT=q_codes[:, qc].bitcast(FP8X4), lhsT_scale=q_scales[:, qc],
-                                    rhs=keys[:, b, o, :].bitcast(FP4X4), rhs_scale=ks_g[:, b, o, :],
+                                    rhs=keys[:, b, o, :].bitcast(FP4X4), rhs_scale=ks_plane[o][:, b * N:(b + 1) * N],
                                     start=(o == 0), stop=(o == PASSES - 1))
             scores.append(acc)
 
         v1_win = sb.tile([P, T], BF16)
-        nc.scalar.activation(v1_win[:], v1_raw[:], ACT.Copy)
-        v_g = [sb.tile([P, 2, B * P, 2], BF16, name="v_g%d" % c) for c in range(2)]
-        nc.scalar.activation(v_g[1][:].rearrange("e u p w -> e p u w"), v1_win[:].indirect(offs_t[:]), ACT.Copy)
+        for h in range(4):
+            nc.scalar.activation(v1_win[:, h * N:(h + 1) * N], v1_raw[:, h * N:(h + 1) * N], ACT.Copy)
+        v_g1 = sb.tile([P, 2, B * P, 2], BF16)
+        for b in range(B):
+            nc.scalar.activation(v_g1[:, :, b * P:(b + 1) * P, :].rearrange("e u p w -> e p u w"),
+                                 v1_win[:].indirect(seq_offs[b]), ACT.Copy)
 
-        neg = sb.tile([P, B, N], F32)
-        nc.vector.tensor_tensor(neg[:, 0, :], past[:, 0, :], scores[0][:], ALU.subtract)
-        vs_g = sb.tile([P, B * N], F32)
-        nc.vector.tensor_copy(vs_g[:], vs_win[:].indirect(offs_t[:]))
-        nc.vector.tensor_tensor(neg[:, 1, :], past[:, 1, :], scores[1][:], ALU.subtract)
+        neg = sb.tile([P, B, N], F32, tag="neg_then_v_g0")
         vs_col = sb.tile([P, B, PACK], F32)
         for b in range(B):
             turned = bank("a%d" % b, [P, PACK, P])
@@ -140,6 +140,7 @@ def tile_attend_draft_kernel(tc, qT, k_words, k_scales, vT, vs, pos, qpos, offs,
         prob = sb.tile([P, B, PACK, P], F32)
         turned_p = []
         for b in range(B):
+            nc.vector.tensor_tensor(neg[:, b, :], past[:, b, :], scores[b][:], ALU.subtract)
             nc.vector.tensor_scalar(clamped[:, b, :], neg[:, b, :], MASKED, None, ALU.min, ALU.min,
                                     accum_out=neg_max[b][:])
             nc.scalar.activation(prob[:, b].rearrange("q t s -> q s t"),
@@ -150,7 +151,11 @@ def tile_attend_draft_kernel(tc, qT, k_words, k_scales, vT, vs, pos, qpos, offs,
                 nc.tensor.transpose(tp[:, t, :], prob[:, b, t, :], ident[:])
             turned_p.append(tp)
 
-        nc.vector.tensor_copy(v_g[0][:].rearrange("e u p w -> e p u w"), v0_win[:].indirect(offs_t[:]))
+        v_g0 = sb.tile([P, 2, B * P, 2], BF16, tag="neg_then_v_g0")
+        v_g = [v_g0, v_g1]
+        for b in range(B):
+            nc.vector.tensor_copy(v_g0[:, :, b * P:(b + 1) * P, :].rearrange("e u p w -> e p u w"),
+                                  v0_win[:].indirect(seq_offs[b]))
         v_bf = sb.tile([P, B, DV, PACK], BF16, align_bytes=64)
         for b in range(B):
             tv = bank("d%d" % b, [P, 2, 2, P])

@@ -1,7 +1,6 @@
 from contextlib import ExitStack
 
 import concourse.mybir as mybir
-from concourse.masks import make_identity
 
 B, N, T, D, DV, NQ = 2, 512, 2048, 1024, 256, 128
 FLOPS = 2 * B * NQ * N * (D + DV)
@@ -30,6 +29,7 @@ def tile_attend_draft_kernel(tc, qT, k_words, k_scales, vT, vs, pos, qpos, offs,
     with ExitStack() as ctx:
         lists = ctx.enter_context(tc.tile_pool(name="lists", bufs=1))
         sb = ctx.enter_context(tc.tile_pool(name="sb", bufs=1))
+        arena = ctx.enter_context(tc.tile_pool(name="arena", bufs=1))
         ps = ctx.enter_context(tc.psum_pool(name="ps", bufs=1))
 
         def bank(tag, shape):
@@ -43,14 +43,21 @@ def tile_attend_draft_kernel(tc, qT, k_words, k_scales, vT, vs, pos, qpos, offs,
         with nc.allow_non_contiguous_dma(reason="one place a query row"):
             nc.sync.dma_start(qpos_t[:], qpos.rearrange("b q o -> q (b o)"))
         ks_rows = k_scales.bitcast(I32).rearrange("o f t -> f o t")
-        ks_win = sb.tile([P, T // 4], I32, tag="ks_then_kw")
+        ks_win = arena.tile([P, T // 4], I32, offset=7168)
         nc.vector.memset(ks_win[:], 0)
         for r in range(4):
             nc.sync.dma_start(ks_win[r:P:16, :], ks_rows[r:16:4, :, :])
-        pos_win = sb.tile([P, T], F32, tag="pos_then_v1")
+        zeros = sb.tile([P, P], F32, tag="zeros_then_kw")
+        nc.gpsimd.memset(zeros[:], 0.0)
+        ident = sb.tile([P, P], F32)
+        nc.gpsimd.affine_select(out=ident[:], in_=zeros[:], compare_op=ALU.not_equal, fill=1.0, base=0,
+                                pattern=[[-1, P]], channel_multiplier=1)
+        kw_win = sb.tile([P, T], I32, tag="zeros_then_kw")
+        nc.sync.dma_start(kw_win[:], k_words[0].rearrange("p t c -> p (t c)").bitcast(I32))
+        pos_win = arena.tile([P, T], F32, offset=19456)
         nc.vector.memset(pos_win[:], 0.0)
         nc.sync.dma_start(pos_win[0:1, :], pos[0:1, :])
-        vs_win = sb.tile([P, T], F32, tag="vs_then_v0")
+        vs_win = sb.tile([P, T], F32, tag="vs_then_v_g0")
         nc.vector.memset(vs_win[:], 0.0)
         nc.sync.dma_start(vs_win[0:1, :], vs[0:1, :])
         qbias = sb.tile([P, B], F32)
@@ -58,30 +65,24 @@ def tile_attend_draft_kernel(tc, qT, k_words, k_scales, vT, vs, pos, qpos, offs,
         q_raw = sb.tile([P, B, PASSES, PACK * NQ], F32, tag="qpos_then_q")
         for b in range(B):
             nc.sync.dma_start(q_raw[:, b], qT[b].rearrange("(o p j) q -> p o (j q)", p=P, j=PACK))
-        ident = sb.tile([P, P], F32)
-        make_identity(nc, ident[:])
         ks_low = sb.tile([P, B * N // 4], I32, align_bytes=64)
         nc.vector.memset(ks_low[96:P, :], 0)
 
         ks_g = sb.tile([P, B * N], U8, align_bytes=64)
         nc.vector.tensor_copy(ks_g[:], ks_win[:].bitcast(U8).indirect(offs_t[:]))
-        nc.sync.dma_start(ks_low[0:P - 16, :], ks_g[16:P, :].bitcast(I32))
+        for lo, hi in ((0, 64), (64, 96), (96, 112)):
+            nc.sync.dma_start(ks_low[lo:hi, :], ks_g[lo + 16:hi + 16, :].bitcast(I32))
         ks_plane = [ks_g[:], ks_low[:].bitcast(U8)]
-        kw_win = sb.tile([P, T], I32, tag="ks_then_kw")
-        nc.sync.dma_start(kw_win[:], k_words[0].rearrange("p t c -> p (t c)").bitcast(I32))
-        pos_g = sb.tile([P, B * N], F32)
-        nc.vector.tensor_copy(pos_g[:], pos_win[:].indirect(offs_t[:]))
-        v1_raw = sb.tile([P, T], F32, tag="pos_then_v1")
+        v1_raw = arena.tile([P, T], F32, offset=0)
         for h in range(2):
             nc.sync.dma_start(v1_raw[:, h * 1024:(h + 1) * 1024], vT[P:2 * P, h * 1024:(h + 1) * 1024])
-        vs_g = sb.tile([P, B * N], F32)
-        nc.vector.tensor_copy(vs_g[:], vs_win[:].indirect(offs_t[:]))
-        v0_win = sb.tile([P, T], F32, tag="vs_then_v0")
+        pos_g = arena.tile([P, B * N], F32, offset=8192)
+        nc.vector.tensor_copy(pos_g[:], pos_win[:].indirect(offs_t[:]))
+        v0_win = arena.tile([P, T], F32, offset=12288)
         nc.sync.dma_start(v0_win[:], vT[0:P, :])
-        kw_g = sb.tile([P, B * N], U32)
 
-        q_bf = sb.tile([P, B * PASSES, NQ, PACK], BF16, align_bytes=64)
-        past = sb.tile([P, B, N], F32)
+        q_bf = sb.tile([P, B * PASSES, NQ, PACK], BF16, align_bytes=64, tag="q_bf_then_vs_g")
+        past = sb.tile([P, B, PACK, P], F32)
         for b in range(B):
             g = slice(b * PASSES, (b + 1) * PASSES)
             nc.scalar.activation(q_bf[:, g], q_raw[:, b].rearrange("p g (j q) -> p g q j", j=PACK), ACT.Copy)
@@ -92,12 +93,13 @@ def tile_attend_draft_kernel(tc, qT, k_words, k_scales, vT, vs, pos, qpos, offs,
                 nc.tensor.transpose(turned[:, c, :], pos_g[:, b * N + c * P:b * N + (c + 1) * P], ident[:])
             nc.scalar.copy(pos_col[:, b, :], turned[:, :, 0])
         for b in range(B):
-            spread = bank("b%d" % b, [P, PACK, P])
+            spread = bank("b%d" % b, [P, N])
             for c in range(PACK):
-                nc.tensor.transpose(spread[:, c, :], pos_col[:, b, c:c + 1].to_broadcast([P, P]), ident[:])
-            nc.scalar.activation(past[:, b, :], spread[:].rearrange("q c s -> q (c s)"), ACT.Relu,
+                nc.tensor.transpose(spread[:, c * P:(c + 1) * P], pos_col[:, b, c:c + 1].to_broadcast([P, P]), ident[:])
+            nc.scalar.activation(past[:, b], spread[:].rearrange("q (s t) -> q t s", t=PACK), ACT.Relu,
                                  bias=qbias[:, b:b + 1], scale=FAR)
 
+        kw_g = arena.tile([P, B * N], U32, offset=20480)
         keys = sb.tile([P, B, PASSES, 2 * N], U8, align_bytes=64)
         q_codes = sb.tile([P, B * PASSES * NQ], U32, align_bytes=64)
         q_scales = sb.tile([P, B * PASSES * NQ], U8, align_bytes=64)
@@ -118,53 +120,56 @@ def tile_attend_draft_kernel(tc, qT, k_words, k_scales, vT, vs, pos, qpos, offs,
                                     start=(o == 0), stop=(o == PASSES - 1))
             scores.append(acc)
 
-        v1_win = sb.tile([P, T], BF16)
+        vs_g = sb.tile([P, B * N], F32, align_bytes=64, tag="q_bf_then_vs_g")
+        nc.vector.tensor_copy(vs_g[:], vs_win[:].indirect(offs_t[:]))
+
+        v_bf = sb.tile([P, B, DV, PACK], BF16, align_bytes=64)
+        turned_v = [bank("d%d" % b, [P, 2, 2, P]) for b in range(B)]
+
+        def turn_values(c, gathered):
+            words = gathered[:].bitcast(F32)
+            for b in range(B):
+                for u in range(2):
+                    nc.tensor.transpose(turned_v[b][:, c, u, :], words[:, b * 256 + u:(b + 1) * 256:2], ident[:])
+                nc.scalar.copy(v_bf[:, b, c * P:(c + 1) * P, :].bitcast(F32),
+                               turned_v[b][:, c].rearrange("p u e -> p e u"))
+
+        v1_win = sb.tile([P, T], BF16, tag="v1_then_vs_col")
         for h in range(4):
             nc.scalar.activation(v1_win[:, h * N:(h + 1) * N], v1_raw[:, h * N:(h + 1) * N], ACT.Copy)
-        v_g1 = sb.tile([P, 2, B * P, 2], BF16)
+        v_g1 = sb.tile([P, B * N], BF16)
         for b in range(B):
-            nc.scalar.activation(v_g1[:, :, b * P:(b + 1) * P, :].rearrange("e u p w -> e p u w"),
-                                 v1_win[:].indirect(seq_offs[b]), ACT.Copy)
+            nc.scalar.activation(v_g1[:, b * N:(b + 1) * N], v1_win[:].indirect(seq_offs[b]), ACT.Copy)
 
-        neg = sb.tile([P, B, N], F32, tag="neg_then_v_g0")
-        vs_col = sb.tile([P, B, PACK], F32)
+        vs_col = sb.tile([P, B, PACK], F32, tag="v1_then_vs_col")
         for b in range(B):
             turned = bank("a%d" % b, [P, PACK, P])
             for t in range(PACK):
                 nc.tensor.transpose(turned[:, t, :], vs_g[:, b * N + t:(b + 1) * N:PACK], ident[:])
             nc.scalar.copy(vs_col[:, b, :], turned[:, :, 0])
+        turn_values(1, v_g1)
 
+        v_g0 = sb.tile([P, B * N], BF16, tag="vs_then_v_g0")
+        nc.vector.tensor_copy(v_g0[:], v0_win[:].indirect(offs_t[:]))
+        turn_values(0, v_g0)
+
+        neg = arena.tile([P, B, PACK, P], F32, offset=12288)
         clamped = sb.tile([P, B, N], F32)
         neg_max = [sb.tile([P, 1], F32, name="neg_max%d" % b) for b in range(B)]
         total = [sb.tile([P, 1], F32, name="total%d" % b) for b in range(B)]
-        prob = sb.tile([P, B, PACK, P], F32)
+        prob = sb.tile([P, B, N], F32)
         turned_p = []
         for b in range(B):
-            nc.vector.tensor_tensor(neg[:, b, :], past[:, b, :], scores[b][:], ALU.subtract)
-            nc.vector.tensor_scalar(clamped[:, b, :], neg[:, b, :], MASKED, None, ALU.min, ALU.min,
-                                    accum_out=neg_max[b][:])
-            nc.scalar.activation(prob[:, b].rearrange("q t s -> q s t"),
-                                 clamped[:, b, :].rearrange("q (s t) -> q s t", t=PACK), ACT.Exp,
+            nc.vector.tensor_tensor(neg[:, b], past[:, b], scores[b][:].rearrange("q (s t) -> q t s", t=PACK),
+                                    ALU.subtract)
+            nc.vector.tensor_scalar(clamped[:, b, :], neg[:, b].rearrange("q t s -> q (t s)"), MASKED, None,
+                                    ALU.min, ALU.min, accum_out=neg_max[b][:])
+            nc.scalar.activation(prob[:, b, :], clamped[:, b, :], ACT.Exp,
                                  bias=neg_max[b][:], scale=-1.0, accum_out=total[b][:])
             tp = bank("b%d" % b, [P, PACK, NQ])
             for t in range(PACK):
-                nc.tensor.transpose(tp[:, t, :], prob[:, b, t, :], ident[:])
+                nc.tensor.transpose(tp[:, t, :], prob[:, b, t * P:(t + 1) * P], ident[:])
             turned_p.append(tp)
-
-        v_g0 = sb.tile([P, 2, B * P, 2], BF16, tag="neg_then_v_g0")
-        v_g = [v_g0, v_g1]
-        for b in range(B):
-            nc.vector.tensor_copy(v_g0[:, :, b * P:(b + 1) * P, :].rearrange("e u p w -> e p u w"),
-                                  v0_win[:].indirect(seq_offs[b]))
-        v_bf = sb.tile([P, B, DV, PACK], BF16, align_bytes=64)
-        for b in range(B):
-            tv = bank("d%d" % b, [P, 2, 2, P])
-            for c in (1, 0):
-                words = v_g[c][:].bitcast(F32)
-                for u in range(2):
-                    nc.tensor.transpose(tv[:, c, u, :], words[:, u, b * P:(b + 1) * P, 0], ident[:])
-            nc.scalar.copy(v_bf[:, b].bitcast(F32).rearrange("p (c e) u -> p c e u", c=2),
-                           tv[:].rearrange("p c u e -> p c e u"))
 
         w_bf = sb.tile([P, B, NQ, PACK], BF16, align_bytes=64)
         w_codes = sb.tile([P, B, NQ], U32, align_bytes=64)
@@ -174,12 +179,12 @@ def tile_attend_draft_kernel(tc, qT, k_words, k_scales, vT, vs, pos, qpos, offs,
         inv = [sb.tile([P, 1], F32, name="inv%d" % b) for b in range(B)]
         y = sb.tile([P, B, DV], F32)
         for b in range(B):
+            nc.vector.quantize_mx(v_codes[:, b, :].bitcast(FP8X4), v_scales[:, b, :],
+                                  v_bf[:, b].rearrange("p e t -> p (e t)"))
+        for b in range(B):
             nc.vector.tensor_tensor(w_bf[:, b], turned_p[b][:].rearrange("p t q -> p q t"),
                                     vs_col[:, b, :].unsqueeze(1).to_broadcast([P, NQ, PACK]), ALU.mult)
             nc.vector.reciprocal(inv[b][:], total[b][:])
-        for b in range(B):
-            nc.vector.quantize_mx(v_codes[:, b, :].bitcast(FP8X4), v_scales[:, b, :],
-                                  v_bf[:, b].rearrange("p e t -> p (e t)"))
             nc.vector.quantize_mx(w_codes[:, b, :].bitcast(FP8X4), w_scales[:, b, :],
                                   w_bf[:, b].rearrange("p q t -> p (q t)"))
             acc = bank("a%d" % b, [P, DV])

@@ -1,6 +1,7 @@
 from contextlib import ExitStack
 
 import concourse.mybir as mybir
+from concourse.masks import make_identity
 
 B, N, T, D, DV, NQ = 2, 512, 2048, 1024, 256, 128
 FLOPS = 2 * B * NQ * N * (D + DV)
@@ -39,30 +40,27 @@ def tile_attend_draft_kernel(tc, qT, k_words, k_scales, vT, vs, pos, qpos, offs,
         nc.sync.dma_start(offs_t[:], offs)
         seq_offs = [offs_t[:, b * COLS:(b + 1) * COLS] for b in range(B)]
 
-        qpos_t = sb.tile([P, B], F32, tag="qpos_then_q")
+        qpos_t = arena.tile([P, 16], F32, offset=36832)
         with nc.allow_non_contiguous_dma(reason="one place a query row"):
-            nc.sync.dma_start(qpos_t[:], qpos.rearrange("b q o -> q (b o)"))
+            nc.sync.dma_start(qpos_t[:, 0:B], qpos.rearrange("b q o -> q (b o)"))
         ks_rows = k_scales.bitcast(I32).rearrange("o f t -> f o t")
         ks_win = arena.tile([P, T // 4], I32, offset=7168)
         nc.vector.memset(ks_win[:], 0)
         for r in range(4):
             nc.sync.dma_start(ks_win[r:P:16, :], ks_rows[r:16:4, :, :])
-        zeros = sb.tile([P, P], F32, tag="zeros_then_kw")
-        nc.gpsimd.memset(zeros[:], 0.0)
         ident = sb.tile([P, P], F32)
-        nc.gpsimd.affine_select(out=ident[:], in_=zeros[:], compare_op=ALU.not_equal, fill=1.0, base=0,
-                                pattern=[[-1, P]], channel_multiplier=1)
-        kw_win = sb.tile([P, T], I32, tag="zeros_then_kw")
-        nc.sync.dma_start(kw_win[:], k_words[0].rearrange("p t c -> p (t c)").bitcast(I32))
+        make_identity(nc, ident[:])
         pos_win = arena.tile([P, T], F32, offset=19456)
         nc.vector.memset(pos_win[:], 0.0)
         nc.sync.dma_start(pos_win[0:1, :], pos[0:1, :])
+        qbias = sb.tile([P, B], F32)
+        nc.vector.tensor_scalar(qbias[:], qpos_t[:, 0:B], -FAR, None, ALU.mult)
         vs_win = sb.tile([P, T], F32, tag="vs_then_v_g0")
         nc.vector.memset(vs_win[:], 0.0)
         nc.sync.dma_start(vs_win[0:1, :], vs[0:1, :])
-        qbias = sb.tile([P, B], F32)
-        nc.vector.tensor_scalar(qbias[:], qpos_t[:], -FAR, None, ALU.mult)
-        q_raw = sb.tile([P, B, PASSES, PACK * NQ], F32, tag="qpos_then_q")
+        kw_win = arena.tile([P, T], I32, offset=28672)
+        nc.sync.dma_start(kw_win[:], k_words[0].rearrange("p t c -> p (t c)").bitcast(I32))
+        q_raw = arena.tile([P, B, PASSES, PACK * NQ], F32, offset=36864)
         for b in range(B):
             nc.sync.dma_start(q_raw[:, b], qT[b].rearrange("(o p j) q -> p o (j q)", p=P, j=PACK))
         ks_low = sb.tile([P, B * N // 4], I32, align_bytes=64)
@@ -86,7 +84,7 @@ def tile_attend_draft_kernel(tc, qT, k_words, k_scales, vT, vs, pos, qpos, offs,
         for b in range(B):
             g = slice(b * PASSES, (b + 1) * PASSES)
             nc.scalar.activation(q_bf[:, g], q_raw[:, b].rearrange("p g (j q) -> p g q j", j=PACK), ACT.Copy)
-        pos_col = sb.tile([P, B, PACK], F32, tag="qpos_then_q")
+        pos_col = arena.tile([P, B, PACK], F32, offset=36928)
         for b in range(B):
             turned = bank("a%d" % b, [P, PACK, P])
             for c in range(PACK):
@@ -100,19 +98,19 @@ def tile_attend_draft_kernel(tc, qT, k_words, k_scales, vT, vs, pos, qpos, offs,
                                  bias=qbias[:, b:b + 1], scale=FAR)
 
         kw_g = arena.tile([P, B * N], U32, offset=20480)
+        nc.vector.tensor_copy(kw_g[:], kw_win[:].bitcast(U32).indirect(offs_t[:]))
         keys = sb.tile([P, B, PASSES, 2 * N], U8, align_bytes=64)
-        q_codes = sb.tile([P, B * PASSES * NQ], U32, align_bytes=64)
+        q_codes = arena.tile([P, B * PASSES * NQ], U32, align_bytes=64, offset=29696)
         q_scales = sb.tile([P, B * PASSES * NQ], U8, align_bytes=64)
         scores = []
         for b in range(B):
             g = slice(b * PASSES, (b + 1) * PASSES)
             cols = slice(b * PASSES * NQ, (b + 1) * PASSES * NQ)
-            nc.vector.tensor_copy(kw_g[:, b * N:(b + 1) * N], kw_win[:].bitcast(U32).indirect(seq_offs[b]))
-            nc.vector.quantize_mx(q_codes[:, cols].bitcast(FP8X4), q_scales[:, cols],
-                                  q_bf[:, g].rearrange("p g q j -> p (g q j)"))
             nc.vector.tensor_copy(keys[:, b].bitcast(U16),
                                   kw_g[:, b * N:(b + 1) * N].bitcast(U16).rearrange("p (n o) -> p o n", o=PASSES))
-            acc = bank("c%d" % b, [P, N])
+            nc.vector.quantize_mx(q_codes[:, cols].bitcast(FP8X4), q_scales[:, cols],
+                                  q_bf[:, g].rearrange("p g q j -> p (g q j)"))
+            acc = bank("a%d" % b, [P, N])
             for o in range(PASSES):
                 qc = slice((b * PASSES + o) * NQ, (b * PASSES + o + 1) * NQ)
                 nc.tensor.matmul_mx(acc[:], lhsT=q_codes[:, qc].bitcast(FP8X4), lhsT_scale=q_scales[:, qc],
@@ -135,15 +133,15 @@ def tile_attend_draft_kernel(tc, qT, k_words, k_scales, vT, vs, pos, qpos, offs,
                                turned_v[b][:, c].rearrange("p u e -> p e u"))
 
         v1_win = sb.tile([P, T], BF16, tag="v1_then_vs_col")
-        for h in range(4):
-            nc.scalar.activation(v1_win[:, h * N:(h + 1) * N], v1_raw[:, h * N:(h + 1) * N], ACT.Copy)
+        for h in range(2):
+            nc.scalar.activation(v1_win[:, h * 1024:(h + 1) * 1024], v1_raw[:, h * 1024:(h + 1) * 1024], ACT.Copy)
         v_g1 = sb.tile([P, B * N], BF16)
         for b in range(B):
             nc.scalar.activation(v_g1[:, b * N:(b + 1) * N], v1_win[:].indirect(seq_offs[b]), ACT.Copy)
 
         vs_col = sb.tile([P, B, PACK], F32, tag="v1_then_vs_col")
         for b in range(B):
-            turned = bank("a%d" % b, [P, PACK, P])
+            turned = bank("c%d" % b, [P, PACK, P])
             for t in range(PACK):
                 nc.tensor.transpose(turned[:, t, :], vs_g[:, b * N + t:(b + 1) * N:PACK], ident[:])
             nc.scalar.copy(vs_col[:, b, :], turned[:, :, 0])
@@ -187,7 +185,7 @@ def tile_attend_draft_kernel(tc, qT, k_words, k_scales, vT, vs, pos, qpos, offs,
             nc.vector.reciprocal(inv[b][:], total[b][:])
             nc.vector.quantize_mx(w_codes[:, b, :].bitcast(FP8X4), w_scales[:, b, :],
                                   w_bf[:, b].rearrange("p q t -> p (q t)"))
-            acc = bank("a%d" % b, [P, DV])
+            acc = bank("c%d" % b, [P, DV])
             nc.tensor.matmul_mx(acc[:], lhsT=w_codes[:, b, :].bitcast(FP8X4), lhsT_scale=w_scales[:, b, :],
                                 rhs=v_codes[:, b, :].bitcast(FP8X4), rhs_scale=v_scales[:, b, :],
                                 start=True, stop=True)

@@ -40,29 +40,33 @@ def tile_attend_draft_kernel(tc, qT, k_words, k_scales, vT, vs, pos, qpos, offs,
         nc.sync.dma_start(offs_t[:], offs)
         seq_offs = [offs_t[:, b * COLS:(b + 1) * COLS] for b in range(B)]
 
-        qpos_t = arena.tile([P, 16], F32, offset=36832)
+        qpos_t = arena.tile([P, 2064], F32, offset=36832)
         with nc.allow_non_contiguous_dma(reason="one place a query row"):
             nc.sync.dma_start(qpos_t[:, 0:B], qpos.rearrange("b q o -> q (b o)"))
+        v1_raw = [arena.tile([P, T // 2], F32, offset=0, name="v1_first"),
+                  arena.tile([P, T // 2], F32, offset=32768, name="v1_second")]
+        nc.sync.dma_start(v1_raw[0][:], vT[P:2 * P, 0:T // 2])
         ks_rows = k_scales.bitcast(I32).rearrange("o f t -> f o t")
-        ks_win = arena.tile([P, T // 4], I32, offset=7168)
+        ks_win = arena.tile([P, T // 4], I32, offset=4096)
         nc.vector.memset(ks_win[:], 0)
         for r in range(4):
             nc.sync.dma_start(ks_win[r:P:16, :], ks_rows[r:16:4, :, :])
         ident = sb.tile([P, P], F32)
         make_identity(nc, ident[:])
-        pos_win = arena.tile([P, T], F32, offset=19456)
+        pos_win = arena.tile([P, T], F32, offset=15360)
         nc.vector.memset(pos_win[:], 0.0)
         nc.sync.dma_start(pos_win[0:1, :], pos[0:1, :])
         qbias = sb.tile([P, B], F32)
         nc.vector.tensor_scalar(qbias[:], qpos_t[:, 0:B], -FAR, None, ALU.mult)
-        vs_win = sb.tile([P, T], F32, tag="vs_then_v_g0")
+        nc.sync.dma_start(v1_raw[1][:], vT[P:2 * P, T // 2:T])
+        vs_win = arena.tile([P, T], F32, offset=24576)
         nc.vector.memset(vs_win[:], 0.0)
         nc.sync.dma_start(vs_win[0:1, :], vs[0:1, :])
-        kw_win = arena.tile([P, T], I32, offset=28672)
-        nc.sync.dma_start(kw_win[:], k_words[0].rearrange("p t c -> p (t c)").bitcast(I32))
         q_raw = arena.tile([P, B, PASSES, PACK * NQ], F32, offset=36864)
         for b in range(B):
             nc.sync.dma_start(q_raw[:, b], qT[b].rearrange("(o p j) q -> p o (j q)", p=P, j=PACK))
+        kw_win = arena.tile([P, T], I32, offset=45056)
+        nc.sync.dma_start(kw_win[:], k_words[0].rearrange("p t c -> p (t c)").bitcast(I32))
         ks_low = sb.tile([P, B * N // 4], I32, align_bytes=64)
         nc.vector.memset(ks_low[96:P, :], 0)
 
@@ -71,15 +75,21 @@ def tile_attend_draft_kernel(tc, qT, k_words, k_scales, vT, vs, pos, qpos, offs,
         for lo, hi in ((0, 64), (64, 96), (96, 112)):
             nc.sync.dma_start(ks_low[lo:hi, :], ks_g[lo + 16:hi + 16, :].bitcast(I32))
         ks_plane = [ks_g[:], ks_low[:].bitcast(U8)]
-        v1_raw = arena.tile([P, T], F32, offset=0)
-        for h in range(2):
-            nc.sync.dma_start(v1_raw[:, h * 1024:(h + 1) * 1024], vT[P:2 * P, h * 1024:(h + 1) * 1024])
-        pos_g = arena.tile([P, B * N], F32, offset=8192)
+        pos_g = arena.tile([P, B * N], F32, offset=4096)
         nc.vector.tensor_copy(pos_g[:], pos_win[:].indirect(offs_t[:]))
-        v0_win = arena.tile([P, T], F32, offset=12288)
+        v0_win = arena.tile([P, T], F32, offset=8192)
         nc.sync.dma_start(v0_win[:], vT[0:P, :])
+        vs_g = arena.tile([P, B * N], F32, offset=16384)
+        nc.vector.tensor_copy(vs_g[:], vs_win[:].indirect(offs_t[:]))
 
-        q_bf = sb.tile([P, B * PASSES, NQ, PACK], BF16, align_bytes=64, tag="q_bf_then_vs_g")
+        v1_win = sb.tile([P, T], BF16)
+        for h in range(2):
+            nc.scalar.activation(v1_win[:, h * 1024:(h + 1) * 1024], v1_raw[h][:], ACT.Copy)
+        v_g1 = sb.tile([P, B * N], BF16)
+        for b in range(B):
+            nc.scalar.activation(v_g1[:, b * N:(b + 1) * N], v1_win[:].indirect(seq_offs[b]), ACT.Copy)
+
+        q_bf = sb.tile([P, B * PASSES, NQ, PACK], BF16, align_bytes=64, tag="q_bf_then_v_g0")
         past = sb.tile([P, B, PACK, P], F32)
         for b in range(B):
             g = slice(b * PASSES, (b + 1) * PASSES)
@@ -96,32 +106,14 @@ def tile_attend_draft_kernel(tc, qT, k_words, k_scales, vT, vs, pos, qpos, offs,
                 nc.tensor.transpose(spread[:, c * P:(c + 1) * P], pos_col[:, b, c:c + 1].to_broadcast([P, P]), ident[:])
             nc.scalar.activation(past[:, b], spread[:].rearrange("q (s t) -> q t s", t=PACK), ACT.Relu,
                                  bias=qbias[:, b:b + 1], scale=FAR)
-
-        kw_g = arena.tile([P, B * N], U32, offset=20480)
-        nc.vector.tensor_copy(kw_g[:], kw_win[:].bitcast(U32).indirect(offs_t[:]))
-        keys = sb.tile([P, B, PASSES, 2 * N], U8, align_bytes=64)
-        q_codes = arena.tile([P, B * PASSES * NQ], U32, align_bytes=64, offset=29696)
-        q_scales = sb.tile([P, B * PASSES * NQ], U8, align_bytes=64)
-        scores = []
+        vs_col = arena.tile([P, B, PACK], F32, offset=36992)
         for b in range(B):
-            g = slice(b * PASSES, (b + 1) * PASSES)
-            cols = slice(b * PASSES * NQ, (b + 1) * PASSES * NQ)
-            nc.vector.tensor_copy(keys[:, b].bitcast(U16),
-                                  kw_g[:, b * N:(b + 1) * N].bitcast(U16).rearrange("p (n o) -> p o n", o=PASSES))
-            nc.vector.quantize_mx(q_codes[:, cols].bitcast(FP8X4), q_scales[:, cols],
-                                  q_bf[:, g].rearrange("p g q j -> p (g q j)"))
-            acc = bank("a%d" % b, [P, N])
-            for o in range(PASSES):
-                qc = slice((b * PASSES + o) * NQ, (b * PASSES + o + 1) * NQ)
-                nc.tensor.matmul_mx(acc[:], lhsT=q_codes[:, qc].bitcast(FP8X4), lhsT_scale=q_scales[:, qc],
-                                    rhs=keys[:, b, o, :].bitcast(FP4X4), rhs_scale=ks_plane[o][:, b * N:(b + 1) * N],
-                                    start=(o == 0), stop=(o == PASSES - 1))
-            scores.append(acc)
+            turned = bank("c%d" % b, [P, PACK, P])
+            for t in range(PACK):
+                nc.tensor.transpose(turned[:, t, :], vs_g[:, b * N + t:(b + 1) * N:PACK], ident[:])
+            nc.scalar.copy(vs_col[:, b, :], turned[:, :, 0])
 
-        vs_g = sb.tile([P, B * N], F32, align_bytes=64, tag="q_bf_then_vs_g")
-        nc.vector.tensor_copy(vs_g[:], vs_win[:].indirect(offs_t[:]))
-
-        v_bf = sb.tile([P, B, DV, PACK], BF16, align_bytes=64)
+        v_bf = arena.tile([P, B, DV, PACK], BF16, align_bytes=64, offset=37888)
         turned_v = [bank("d%d" % b, [P, 2, 2, P]) for b in range(B)]
 
         def turn_values(c, gathered):
@@ -132,26 +124,34 @@ def tile_attend_draft_kernel(tc, qT, k_words, k_scales, vT, vs, pos, qpos, offs,
                 nc.scalar.copy(v_bf[:, b, c * P:(c + 1) * P, :].bitcast(F32),
                                turned_v[b][:, c].rearrange("p u e -> p e u"))
 
-        v1_win = sb.tile([P, T], BF16, tag="v1_then_vs_col")
-        for h in range(2):
-            nc.scalar.activation(v1_win[:, h * 1024:(h + 1) * 1024], v1_raw[:, h * 1024:(h + 1) * 1024], ACT.Copy)
-        v_g1 = sb.tile([P, B * N], BF16)
-        for b in range(B):
-            nc.scalar.activation(v_g1[:, b * N:(b + 1) * N], v1_win[:].indirect(seq_offs[b]), ACT.Copy)
-
-        vs_col = sb.tile([P, B, PACK], F32, tag="v1_then_vs_col")
-        for b in range(B):
-            turned = bank("c%d" % b, [P, PACK, P])
-            for t in range(PACK):
-                nc.tensor.transpose(turned[:, t, :], vs_g[:, b * N + t:(b + 1) * N:PACK], ident[:])
-            nc.scalar.copy(vs_col[:, b, :], turned[:, :, 0])
         turn_values(1, v_g1)
 
-        v_g0 = sb.tile([P, B * N], BF16, tag="vs_then_v_g0")
+        kw_g = arena.tile([P, B * N], U32, offset=24576)
+        nc.vector.tensor_copy(kw_g[:], kw_win[:].bitcast(U32).indirect(offs_t[:]))
+        keys = sb.tile([P, B, PASSES, 2 * N], U8, align_bytes=64)
+        q_codes = arena.tile([P, B * PASSES * NQ], U32, align_bytes=64, offset=46080)
+        q_scales = sb.tile([P, B * PASSES * NQ], U8, align_bytes=64)
+        scores = []
+        for b in range(B):
+            g = slice(b * PASSES, (b + 1) * PASSES)
+            cols = slice(b * PASSES * NQ, (b + 1) * PASSES * NQ)
+            nc.vector.quantize_mx(q_codes[:, cols].bitcast(FP8X4), q_scales[:, cols],
+                                  q_bf[:, g].rearrange("p g q j -> p (g q j)"))
+            nc.vector.tensor_copy(keys[:, b].bitcast(U16),
+                                  kw_g[:, b * N:(b + 1) * N].bitcast(U16).rearrange("p (n o) -> p o n", o=PASSES))
+            acc = bank("a%d" % b, [P, N])
+            for o in range(PASSES):
+                qc = slice((b * PASSES + o) * NQ, (b * PASSES + o + 1) * NQ)
+                nc.tensor.matmul_mx(acc[:], lhsT=q_codes[:, qc].bitcast(FP8X4), lhsT_scale=q_scales[:, qc],
+                                    rhs=keys[:, b, o, :].bitcast(FP4X4), rhs_scale=ks_plane[o][:, b * N:(b + 1) * N],
+                                    start=(o == 0), stop=(o == PASSES - 1))
+            scores.append(acc)
+
+        v_g0 = sb.tile([P, B * N], BF16, align_bytes=64, tag="q_bf_then_v_g0")
         nc.vector.tensor_copy(v_g0[:], v0_win[:].indirect(offs_t[:]))
         turn_values(0, v_g0)
 
-        neg = arena.tile([P, B, PACK, P], F32, offset=12288)
+        neg = arena.tile([P, B, PACK, P], F32, offset=8192)
         clamped = sb.tile([P, B, N], F32)
         neg_max = [sb.tile([P, 1], F32, name="neg_max%d" % b) for b in range(B)]
         total = [sb.tile([P, 1], F32, name="total%d" % b) for b in range(B)]
@@ -160,6 +160,7 @@ def tile_attend_draft_kernel(tc, qT, k_words, k_scales, vT, vs, pos, qpos, offs,
         for b in range(B):
             nc.vector.tensor_tensor(neg[:, b], past[:, b], scores[b][:].rearrange("q (s t) -> q t s", t=PACK),
                                     ALU.subtract)
+        for b in range(B):
             nc.vector.tensor_scalar(clamped[:, b, :], neg[:, b].rearrange("q t s -> q (t s)"), MASKED, None,
                                     ALU.min, ALU.min, accum_out=neg_max[b][:])
             nc.scalar.activation(prob[:, b, :], clamped[:, b, :], ACT.Exp,
@@ -182,12 +183,18 @@ def tile_attend_draft_kernel(tc, qT, k_words, k_scales, vT, vs, pos, qpos, offs,
         for b in range(B):
             nc.vector.tensor_tensor(w_bf[:, b], turned_p[b][:].rearrange("p t q -> p q t"),
                                     vs_col[:, b, :].unsqueeze(1).to_broadcast([P, NQ, PACK]), ALU.mult)
-            nc.vector.reciprocal(inv[b][:], total[b][:])
+        sums = []
+        for b in range(B):
             nc.vector.quantize_mx(w_codes[:, b, :].bitcast(FP8X4), w_scales[:, b, :],
                                   w_bf[:, b].rearrange("p q t -> p (q t)"))
             acc = bank("c%d" % b, [P, DV])
             nc.tensor.matmul_mx(acc[:], lhsT=w_codes[:, b, :].bitcast(FP8X4), lhsT_scale=w_scales[:, b, :],
                                 rhs=v_codes[:, b, :].bitcast(FP8X4), rhs_scale=v_scales[:, b, :],
                                 start=True, stop=True)
-            nc.scalar.activation(y[:, b, :], acc[:], ACT.Copy, scale=inv[b][:])
-            nc.sync.dma_start(out[b], y[:, b, :])
+            sums.append(acc)
+        for b in range(B):
+            nc.vector.reciprocal(inv[b][:], total[b][:])
+        nc.scalar.activation(y[:, 0, :], sums[0][:], ACT.Copy, scale=inv[0][:])
+        nc.sync.dma_start(out[0], y[:, 0, :])
+        nc.vector.tensor_scalar(y[:, 1, :], sums[1][:], inv[1][:], None, ALU.mult)
+        nc.sync.dma_start(out[1], y[:, 1, :])

@@ -40,33 +40,34 @@ def tile_attend_draft_kernel(tc, qT, k_words, k_scales, vT, vs, pos, qpos, offs,
         nc.sync.dma_start(offs_t[:], offs)
         seq_offs = [offs_t[:, b * COLS:(b + 1) * COLS] for b in range(B)]
 
-        qpos_t = arena.tile([P, 2064], F32, offset=36832)
+        qpos_t = arena.tile([P, 2064], F32, offset=45024)
         with nc.allow_non_contiguous_dma(reason="one place a query row"):
             nc.sync.dma_start(qpos_t[:, 0:B], qpos.rearrange("b q o -> q (b o)"))
-        v1_raw = [arena.tile([P, T // 2], F32, offset=0, name="v1_first"),
-                  arena.tile([P, T // 2], F32, offset=32768, name="v1_second")]
-        nc.sync.dma_start(v1_raw[0][:], vT[P:2 * P, 0:T // 2])
         ks_rows = k_scales.bitcast(I32).rearrange("o f t -> f o t")
         ks_win = arena.tile([P, T // 4], I32, offset=4096)
         nc.vector.memset(ks_win[:], 0)
         for r in range(4):
             nc.sync.dma_start(ks_win[r:P:16, :], ks_rows[r:16:4, :, :])
+        v1_raw = sb.tile([P, T], F32)
+        for h in range(2):
+            nc.sync.dma_start(v1_raw[:, h * 1024:(h + 1) * 1024], vT[P:2 * P, h * 1024:(h + 1) * 1024])
         ident = sb.tile([P, P], F32)
         make_identity(nc, ident[:])
         pos_win = arena.tile([P, T], F32, offset=15360)
         nc.vector.memset(pos_win[:], 0.0)
         nc.sync.dma_start(pos_win[0:1, :], pos[0:1, :])
-        qbias = sb.tile([P, B], F32)
-        nc.vector.tensor_scalar(qbias[:], qpos_t[:, 0:B], -FAR, None, ALU.mult)
-        nc.sync.dma_start(v1_raw[1][:], vT[P:2 * P, T // 2:T])
         vs_win = arena.tile([P, T], F32, offset=24576)
         nc.vector.memset(vs_win[:], 0.0)
         nc.sync.dma_start(vs_win[0:1, :], vs[0:1, :])
+        qbias = sb.tile([P, B], F32)
+        nc.vector.tensor_scalar(qbias[:], qpos_t[:, 0:B], -FAR, None, ALU.mult)
+        kw_win = arena.tile([P, T], I32, offset=45056)
+        nc.sync.dma_start(kw_win[:], k_words[0].rearrange("p t c -> p (t c)").bitcast(I32))
+        v0_win = arena.tile([P, T], F32, offset=53248)
+        nc.sync.dma_start(v0_win[:], vT[0:P, :])
         q_raw = arena.tile([P, B, PASSES, PACK * NQ], F32, offset=36864)
         for b in range(B):
             nc.sync.dma_start(q_raw[:, b], qT[b].rearrange("(o p j) q -> p o (j q)", p=P, j=PACK))
-        kw_win = arena.tile([P, T], I32, offset=45056)
-        nc.sync.dma_start(kw_win[:], k_words[0].rearrange("p t c -> p (t c)").bitcast(I32))
         ks_low = sb.tile([P, B * N // 4], I32, align_bytes=64)
         nc.vector.memset(ks_low[96:P, :], 0)
 
@@ -77,29 +78,27 @@ def tile_attend_draft_kernel(tc, qT, k_words, k_scales, vT, vs, pos, qpos, offs,
         ks_plane = [ks_g[:], ks_low[:].bitcast(U8)]
         pos_g = arena.tile([P, B * N], F32, offset=4096)
         nc.vector.tensor_copy(pos_g[:], pos_win[:].indirect(offs_t[:]))
-        v0_win = arena.tile([P, T], F32, offset=8192)
-        nc.sync.dma_start(v0_win[:], vT[0:P, :])
         vs_g = arena.tile([P, B * N], F32, offset=16384)
         nc.vector.tensor_copy(vs_g[:], vs_win[:].indirect(offs_t[:]))
 
         v1_win = sb.tile([P, T], BF16)
         for h in range(2):
-            nc.scalar.activation(v1_win[:, h * 1024:(h + 1) * 1024], v1_raw[h][:], ACT.Copy)
+            nc.scalar.activation(v1_win[:, h * 1024:(h + 1) * 1024], v1_raw[:, h * 1024:(h + 1) * 1024], ACT.Copy)
         v_g1 = sb.tile([P, B * N], BF16)
         for b in range(B):
             nc.scalar.activation(v_g1[:, b * N:(b + 1) * N], v1_win[:].indirect(seq_offs[b]), ACT.Copy)
 
         q_bf = sb.tile([P, B * PASSES, NQ, PACK], BF16, align_bytes=64, tag="q_bf_then_v_g0")
-        past = sb.tile([P, B, PACK, P], F32)
         for b in range(B):
             g = slice(b * PASSES, (b + 1) * PASSES)
             nc.scalar.activation(q_bf[:, g], q_raw[:, b].rearrange("p g (j q) -> p g q j", j=PACK), ACT.Copy)
-        pos_col = arena.tile([P, B, PACK], F32, offset=36928)
+        pos_col = sb.tile([P, B, PACK], F32)
         for b in range(B):
             turned = bank("a%d" % b, [P, PACK, P])
             for c in range(PACK):
                 nc.tensor.transpose(turned[:, c, :], pos_g[:, b * N + c * P:b * N + (c + 1) * P], ident[:])
             nc.scalar.copy(pos_col[:, b, :], turned[:, :, 0])
+        past = arena.tile([P, B, PACK, P], F32, offset=8192)
         for b in range(B):
             spread = bank("b%d" % b, [P, N])
             for c in range(PACK):
@@ -113,18 +112,21 @@ def tile_attend_draft_kernel(tc, qT, k_words, k_scales, vT, vs, pos, qpos, offs,
                 nc.tensor.transpose(turned[:, t, :], vs_g[:, b * N + t:(b + 1) * N:PACK], ident[:])
             nc.scalar.copy(vs_col[:, b, :], turned[:, :, 0])
 
-        v_bf = arena.tile([P, B, DV, PACK], BF16, align_bytes=64, offset=37888)
+        v_bf = [arena.tile([P, DV, PACK], BF16, align_bytes=64, offset=37888, name="v_bf_first")]
         turned_v = [bank("d%d" % b, [P, 2, 2, P]) for b in range(B)]
 
-        def turn_values(c, gathered):
-            words = gathered[:].bitcast(F32)
-            for b in range(B):
-                for u in range(2):
-                    nc.tensor.transpose(turned_v[b][:, c, u, :], words[:, b * 256 + u:(b + 1) * 256:2], ident[:])
-                nc.scalar.copy(v_bf[:, b, c * P:(c + 1) * P, :].bitcast(F32),
-                               turned_v[b][:, c].rearrange("p u e -> p e u"))
+        def turn_values(c, b, gathered):
+            words = gathered.bitcast(F32)
+            for u in range(2):
+                nc.tensor.transpose(turned_v[b][:, c, u, :], words[:, u:256:2], ident[:])
 
-        turn_values(1, v_g1)
+        def copy_values(c, b):
+            nc.scalar.copy(v_bf[b][:, c * P:(c + 1) * P, :].bitcast(F32),
+                           turned_v[b][:, c].rearrange("p u e -> p e u"))
+
+        for b in range(B):
+            turn_values(1, b, v_g1[:, b * N:(b + 1) * N])
+        copy_values(1, 0)
 
         kw_g = arena.tile([P, B * N], U32, offset=24576)
         nc.vector.tensor_copy(kw_g[:], kw_win[:].bitcast(U32).indirect(offs_t[:]))
@@ -147,12 +149,13 @@ def tile_attend_draft_kernel(tc, qT, k_words, k_scales, vT, vs, pos, qpos, offs,
                                     start=(o == 0), stop=(o == PASSES - 1))
             scores.append(acc)
 
-        v_g0 = sb.tile([P, B * N], BF16, align_bytes=64, tag="q_bf_then_v_g0")
-        nc.vector.tensor_copy(v_g0[:], v0_win[:].indirect(offs_t[:]))
-        turn_values(0, v_g0)
+        v_g0 = sb.tile([P, N], BF16, align_bytes=64, tag="q_bf_then_v_g0")
+        nc.vector.tensor_copy(v_g0[:], v0_win[:].indirect(seq_offs[0]))
+        turn_values(0, 0, v_g0[:])
+        copy_values(0, 0)
 
-        neg = arena.tile([P, B, PACK, P], F32, offset=8192)
-        clamped = sb.tile([P, B, N], F32)
+        neg = sb.tile([P, B, PACK, P], F32)
+        clamped = [arena.tile([P, N], F32, offset=61440 + 2048 * b, name="clamped%d" % b) for b in range(B)]
         neg_max = [sb.tile([P, 1], F32, name="neg_max%d" % b) for b in range(B)]
         total = [sb.tile([P, 1], F32, name="total%d" % b) for b in range(B)]
         prob = sb.tile([P, B, N], F32)
@@ -161,14 +164,21 @@ def tile_attend_draft_kernel(tc, qT, k_words, k_scales, vT, vs, pos, qpos, offs,
             nc.vector.tensor_tensor(neg[:, b], past[:, b], scores[b][:].rearrange("q (s t) -> q t s", t=PACK),
                                     ALU.subtract)
         for b in range(B):
-            nc.vector.tensor_scalar(clamped[:, b, :], neg[:, b].rearrange("q t s -> q (t s)"), MASKED, None,
+            nc.vector.tensor_scalar(clamped[b][:], neg[:, b].rearrange("q t s -> q (t s)"), MASKED, None,
                                     ALU.min, ALU.min, accum_out=neg_max[b][:])
-            nc.scalar.activation(prob[:, b, :], clamped[:, b, :], ACT.Exp,
+            nc.scalar.activation(prob[:, b, :], clamped[b][:], ACT.Exp,
                                  bias=neg_max[b][:], scale=-1.0, accum_out=total[b][:])
             tp = bank("b%d" % b, [P, PACK, NQ])
             for t in range(PACK):
                 nc.tensor.transpose(tp[:, t, :], prob[:, b, t * P:(t + 1) * P], ident[:])
             turned_p.append(tp)
+
+        v_g0_last = arena.tile([P, N], BF16, offset=10240)
+        nc.vector.tensor_copy(v_g0_last[:], v0_win[:].indirect(seq_offs[1]))
+        v_bf.append(arena.tile([P, DV, PACK], BF16, align_bytes=64, offset=63488, name="v_bf_second"))
+        copy_values(1, 1)
+        turn_values(0, 1, v_g0_last[:])
+        copy_values(0, 1)
 
         w_bf = sb.tile([P, B, NQ, PACK], BF16, align_bytes=64)
         w_codes = sb.tile([P, B, NQ], U32, align_bytes=64)
@@ -178,13 +188,12 @@ def tile_attend_draft_kernel(tc, qT, k_words, k_scales, vT, vs, pos, qpos, offs,
         inv = [sb.tile([P, 1], F32, name="inv%d" % b) for b in range(B)]
         y = sb.tile([P, B, DV], F32)
         for b in range(B):
-            nc.vector.quantize_mx(v_codes[:, b, :].bitcast(FP8X4), v_scales[:, b, :],
-                                  v_bf[:, b].rearrange("p e t -> p (e t)"))
-        for b in range(B):
             nc.vector.tensor_tensor(w_bf[:, b], turned_p[b][:].rearrange("p t q -> p q t"),
                                     vs_col[:, b, :].unsqueeze(1).to_broadcast([P, NQ, PACK]), ALU.mult)
         sums = []
         for b in range(B):
+            nc.vector.quantize_mx(v_codes[:, b, :].bitcast(FP8X4), v_scales[:, b, :],
+                                  v_bf[b][:].rearrange("p e t -> p (e t)"))
             nc.vector.quantize_mx(w_codes[:, b, :].bitcast(FP8X4), w_scales[:, b, :],
                                   w_bf[:, b].rearrange("p q t -> p (q t)"))
             acc = bank("c%d" % b, [P, DV])

@@ -40,17 +40,16 @@ def tile_attend_draft_kernel(tc, qT, k_words, k_scales, vT, vs, pos, qpos, offs,
         nc.sync.dma_start(offs_t[:], offs)
         seq_offs = [offs_t[:, b * COLS:(b + 1) * COLS] for b in range(B)]
 
-        qpos_t = arena.tile([P, 2064], F32, offset=45024)
+        qpos_t = arena.tile([P, 16], F32, offset=40928)
         with nc.allow_non_contiguous_dma(reason="one place a query row"):
             nc.sync.dma_start(qpos_t[:, 0:B], qpos.rearrange("b q o -> q (b o)"))
         ks_rows = k_scales.bitcast(I32).rearrange("o f t -> f o t")
-        ks_win = arena.tile([P, T // 4], I32, offset=4096)
+        ks_win = arena.tile([P, T // 4], I32, offset=3072)
         nc.vector.memset(ks_win[:], 0)
         for r in range(4):
             nc.sync.dma_start(ks_win[r:P:16, :], ks_rows[r:16:4, :, :])
-        v1_raw = sb.tile([P, T], F32)
-        for h in range(2):
-            nc.sync.dma_start(v1_raw[:, h * 1024:(h + 1) * 1024], vT[P:2 * P, h * 1024:(h + 1) * 1024])
+        q_first = sb.tile([P, PASSES, PACK * NQ], F32)
+        nc.sync.dma_start(q_first[:], qT[0].rearrange("(o p j) q -> p o (j q)", p=P, j=PACK))
         ident = sb.tile([P, P], F32)
         make_identity(nc, ident[:])
         pos_win = arena.tile([P, T], F32, offset=15360)
@@ -61,13 +60,10 @@ def tile_attend_draft_kernel(tc, qT, k_words, k_scales, vT, vs, pos, qpos, offs,
         nc.sync.dma_start(vs_win[0:1, :], vs[0:1, :])
         qbias = sb.tile([P, B], F32)
         nc.vector.tensor_scalar(qbias[:], qpos_t[:, 0:B], -FAR, None, ALU.mult)
-        kw_win = arena.tile([P, T], I32, offset=45056)
+        kw_win = arena.tile([P, T], I32, offset=32768)
         nc.sync.dma_start(kw_win[:], k_words[0].rearrange("p t c -> p (t c)").bitcast(I32))
-        v0_win = arena.tile([P, T], F32, offset=53248)
-        nc.sync.dma_start(v0_win[:], vT[0:P, :])
-        q_raw = arena.tile([P, B, PASSES, PACK * NQ], F32, offset=36864)
-        for b in range(B):
-            nc.sync.dma_start(q_raw[:, b], qT[b].rearrange("(o p j) q -> p o (j q)", p=P, j=PACK))
+        q_second = arena.tile([P, PASSES, PACK * NQ], F32, offset=40960)
+        nc.sync.dma_start(q_second[:], qT[1].rearrange("(o p j) q -> p o (j q)", p=P, j=PACK))
         ks_low = sb.tile([P, B * N // 4], I32, align_bytes=64)
         nc.vector.memset(ks_low[96:P, :], 0)
 
@@ -76,62 +72,36 @@ def tile_attend_draft_kernel(tc, qT, k_words, k_scales, vT, vs, pos, qpos, offs,
         for lo, hi in ((0, 64), (64, 96), (96, 112)):
             nc.sync.dma_start(ks_low[lo:hi, :], ks_g[lo + 16:hi + 16, :].bitcast(I32))
         ks_plane = [ks_g[:], ks_low[:].bitcast(U8)]
-        pos_g = arena.tile([P, B * N], F32, offset=4096)
-        nc.vector.tensor_copy(pos_g[:], pos_win[:].indirect(offs_t[:]))
-        vs_g = arena.tile([P, B * N], F32, offset=16384)
-        nc.vector.tensor_copy(vs_g[:], vs_win[:].indirect(offs_t[:]))
-
-        v1_win = sb.tile([P, T], BF16)
+        v1_raw = arena.tile([P, T], F32, offset=4096)
         for h in range(2):
-            nc.scalar.activation(v1_win[:, h * 1024:(h + 1) * 1024], v1_raw[:, h * 1024:(h + 1) * 1024], ACT.Copy)
-        v_g1 = sb.tile([P, B * N], BF16)
-        for b in range(B):
-            nc.scalar.activation(v_g1[:, b * N:(b + 1) * N], v1_win[:].indirect(seq_offs[b]), ACT.Copy)
+            nc.sync.dma_start(v1_raw[:, h * 1024:(h + 1) * 1024], vT[P:2 * P, h * 1024:(h + 1) * 1024])
+        pos_g = arena.tile([P, B * N], F32, offset=0)
+        nc.vector.tensor_copy(pos_g[:], pos_win[:].indirect(offs_t[:]))
+        v0_win = arena.tile([P, T], F32, offset=16384)
+        nc.sync.dma_start(v0_win[:], vT[0:P, :])
 
-        q_bf = sb.tile([P, B * PASSES, NQ, PACK], BF16, align_bytes=64, tag="q_bf_then_v_g0")
-        for b in range(B):
-            g = slice(b * PASSES, (b + 1) * PASSES)
-            nc.scalar.activation(q_bf[:, g], q_raw[:, b].rearrange("p g (j q) -> p g q j", j=PACK), ACT.Copy)
-        pos_col = sb.tile([P, B, PACK], F32)
+        q_bf = sb.tile([P, B * PASSES, NQ, PACK], BF16, align_bytes=64, tag="q_bf_then_vs_g")
+        for b, q_raw in enumerate((q_first, q_second)):
+            nc.scalar.activation(q_bf[:, b * PASSES:(b + 1) * PASSES],
+                                 q_raw[:].rearrange("p g (j q) -> p g q j", j=PACK), ACT.Copy)
+        pos_col = arena.tile([P, B, PACK], F32, offset=41024)
         for b in range(B):
             turned = bank("a%d" % b, [P, PACK, P])
             for c in range(PACK):
                 nc.tensor.transpose(turned[:, c, :], pos_g[:, b * N + c * P:b * N + (c + 1) * P], ident[:])
             nc.scalar.copy(pos_col[:, b, :], turned[:, :, 0])
-        past = arena.tile([P, B, PACK, P], F32, offset=8192)
+        past = arena.tile([P, B, PACK, P], F32, offset=45056)
         for b in range(B):
             spread = bank("b%d" % b, [P, N])
             for c in range(PACK):
                 nc.tensor.transpose(spread[:, c * P:(c + 1) * P], pos_col[:, b, c:c + 1].to_broadcast([P, P]), ident[:])
             nc.scalar.activation(past[:, b], spread[:].rearrange("q (s t) -> q t s", t=PACK), ACT.Relu,
                                  bias=qbias[:, b:b + 1], scale=FAR)
-        vs_col = arena.tile([P, B, PACK], F32, offset=36992)
-        for b in range(B):
-            turned = bank("c%d" % b, [P, PACK, P])
-            for t in range(PACK):
-                nc.tensor.transpose(turned[:, t, :], vs_g[:, b * N + t:(b + 1) * N:PACK], ident[:])
-            nc.scalar.copy(vs_col[:, b, :], turned[:, :, 0])
 
-        v_bf = [arena.tile([P, DV, PACK], BF16, align_bytes=64, offset=37888, name="v_bf_first")]
-        turned_v = [bank("d%d" % b, [P, 2, 2, P]) for b in range(B)]
-
-        def turn_values(c, b, gathered):
-            words = gathered.bitcast(F32)
-            for u in range(2):
-                nc.tensor.transpose(turned_v[b][:, c, u, :], words[:, u:256:2], ident[:])
-
-        def copy_values(c, b):
-            nc.scalar.copy(v_bf[b][:, c * P:(c + 1) * P, :].bitcast(F32),
-                           turned_v[b][:, c].rearrange("p u e -> p e u"))
-
-        for b in range(B):
-            turn_values(1, b, v_g1[:, b * N:(b + 1) * N])
-        copy_values(1, 0)
-
-        kw_g = arena.tile([P, B * N], U32, offset=24576)
+        kw_g = arena.tile([P, B * N], U32, offset=12288)
         nc.vector.tensor_copy(kw_g[:], kw_win[:].bitcast(U32).indirect(offs_t[:]))
         keys = sb.tile([P, B, PASSES, 2 * N], U8, align_bytes=64)
-        q_codes = arena.tile([P, B * PASSES * NQ], U32, align_bytes=64, offset=46080)
+        q_codes = arena.tile([P, B * PASSES * NQ], U32, align_bytes=64, offset=33792)
         q_scales = sb.tile([P, B * PASSES * NQ], U8, align_bytes=64)
         scores = []
         for b in range(B):
@@ -149,16 +119,34 @@ def tile_attend_draft_kernel(tc, qT, k_words, k_scales, vT, vs, pos, qpos, offs,
                                     start=(o == 0), stop=(o == PASSES - 1))
             scores.append(acc)
 
-        v_g0 = sb.tile([P, N], BF16, align_bytes=64, tag="q_bf_then_v_g0")
-        nc.vector.tensor_copy(v_g0[:], v0_win[:].indirect(seq_offs[0]))
-        turn_values(0, 0, v_g0[:])
-        copy_values(0, 0)
+        vs_g = sb.tile([P, B * N], F32, align_bytes=64, tag="q_bf_then_vs_g")
+        nc.vector.tensor_copy(vs_g[:], vs_win[:].indirect(offs_t[:]))
+        turned_vs = [bank("c%d" % b, [P, PACK, P]) for b in range(B)]
+        for b in range(B):
+            for t in range(PACK):
+                nc.tensor.transpose(turned_vs[b][:, t, :], vs_g[:, b * N + t:(b + 1) * N:PACK], ident[:])
 
-        neg = sb.tile([P, B, PACK, P], F32)
-        clamped = [arena.tile([P, N], F32, offset=61440 + 2048 * b, name="clamped%d" % b) for b in range(B)]
+        v1_win = sb.tile([P, T], BF16)
+        for h in range(2):
+            nc.scalar.activation(v1_win[:, h * 1024:(h + 1) * 1024], v1_raw[:, h * 1024:(h + 1) * 1024], ACT.Copy)
+
+        v_bf = sb.tile([P, B, DV, PACK], BF16, align_bytes=64)
+
+        def turn_values(c, b, gathered, tag):
+            words = gathered[:, b * N:(b + 1) * N].bitcast(F32)
+            turned = bank(tag, [P, 2, P])
+            for u in range(2):
+                nc.tensor.transpose(turned[:, u, :], words[:, u:N // 2:2], ident[:])
+            nc.scalar.copy(v_bf[:, b, c * P:(c + 1) * P, :].bitcast(F32), turned[:].rearrange("p u e -> p e u"))
+
+        v_g1 = sb.tile([P, B * N], BF16)
+        nc.scalar.activation(v_g1[:, 0:N], v1_win[:].indirect(seq_offs[0]), ACT.Copy)
+
+        neg = arena.tile([P, B, PACK, P], F32, offset=24576)
+        clamped = [arena.tile([P, N], F32, offset=49152 + 2048 * b, name="clamped%d" % b) for b in range(B)]
         neg_max = [sb.tile([P, 1], F32, name="neg_max%d" % b) for b in range(B)]
         total = [sb.tile([P, 1], F32, name="total%d" % b) for b in range(B)]
-        prob = sb.tile([P, B, N], F32)
+        prob = arena.tile([P, B, N], F32, offset=8192)
         turned_p = []
         for b in range(B):
             nc.vector.tensor_tensor(neg[:, b], past[:, b], scores[b][:].rearrange("q (s t) -> q t s", t=PACK),
@@ -173,14 +161,19 @@ def tile_attend_draft_kernel(tc, qT, k_words, k_scales, vT, vs, pos, qpos, offs,
                 nc.tensor.transpose(tp[:, t, :], prob[:, b, t * P:(t + 1) * P], ident[:])
             turned_p.append(tp)
 
-        v_g0_last = arena.tile([P, N], BF16, offset=10240)
-        nc.vector.tensor_copy(v_g0_last[:], v0_win[:].indirect(seq_offs[1]))
-        v_bf.append(arena.tile([P, DV, PACK], BF16, align_bytes=64, offset=63488, name="v_bf_second"))
-        copy_values(1, 1)
-        turn_values(0, 1, v_g0_last[:])
-        copy_values(0, 1)
+        vs_col = arena.tile([P, B, PACK], F32, offset=51200)
+        for b in range(B):
+            nc.scalar.copy(vs_col[:, b, :], turned_vs[b][:, :, 0])
+        nc.scalar.activation(v_g1[:, N:2 * N], v1_win[:].indirect(seq_offs[1]), ACT.Copy)
+        for b in range(B):
+            turn_values(1, b, v_g1, "d%d" % b)
 
-        w_bf = sb.tile([P, B, NQ, PACK], BF16, align_bytes=64)
+        v_g0 = arena.tile([P, B * N], BF16, offset=47104)
+        nc.vector.tensor_copy(v_g0[:], v0_win[:].indirect(offs_t[:]))
+        for b in range(B):
+            turn_values(0, b, v_g0, "a%d" % b)
+
+        w_bf = arena.tile([P, B, NQ, PACK], BF16, align_bytes=64, offset=16384)
         w_codes = sb.tile([P, B, NQ], U32, align_bytes=64)
         w_scales = sb.tile([P, B, NQ], U8, align_bytes=64)
         v_codes = sb.tile([P, B, DV], U32, align_bytes=64)
@@ -190,19 +183,20 @@ def tile_attend_draft_kernel(tc, qT, k_words, k_scales, vT, vs, pos, qpos, offs,
         for b in range(B):
             nc.vector.tensor_tensor(w_bf[:, b], turned_p[b][:].rearrange("p t q -> p q t"),
                                     vs_col[:, b, :].unsqueeze(1).to_broadcast([P, NQ, PACK]), ALU.mult)
+        for b in range(B):
+            nc.vector.reciprocal(inv[b][:], total[b][:])
+        for b in range(B):
+            nc.vector.quantize_mx(w_codes[:, b, :].bitcast(FP8X4), w_scales[:, b, :],
+                                  w_bf[:, b].rearrange("p q t -> p (q t)"))
         sums = []
         for b in range(B):
             nc.vector.quantize_mx(v_codes[:, b, :].bitcast(FP8X4), v_scales[:, b, :],
-                                  v_bf[b][:].rearrange("p e t -> p (e t)"))
-            nc.vector.quantize_mx(w_codes[:, b, :].bitcast(FP8X4), w_scales[:, b, :],
-                                  w_bf[:, b].rearrange("p q t -> p (q t)"))
+                                  v_bf[:, b].rearrange("p e t -> p (e t)"))
             acc = bank("c%d" % b, [P, DV])
             nc.tensor.matmul_mx(acc[:], lhsT=w_codes[:, b, :].bitcast(FP8X4), lhsT_scale=w_scales[:, b, :],
                                 rhs=v_codes[:, b, :].bitcast(FP8X4), rhs_scale=v_scales[:, b, :],
                                 start=True, stop=True)
             sums.append(acc)
-        for b in range(B):
-            nc.vector.reciprocal(inv[b][:], total[b][:])
         nc.scalar.activation(y[:, 0, :], sums[0][:], ACT.Copy, scale=inv[0][:])
         nc.sync.dma_start(out[0], y[:, 0, :])
         nc.vector.tensor_scalar(y[:, 1, :], sums[1][:], inv[1][:], None, ALU.mult)

@@ -48,7 +48,7 @@ def tile_attend_draft_kernel(tc, qT, k_words, k_scales, vT, vs, pos, qpos, offs,
         nc.vector.memset(ks_win[:], 0)
         for r in range(4):
             nc.sync.dma_start(ks_win[r:P:16, :], ks_rows[r:16:4, :, :])
-        q_first = sb.tile([P, PASSES, PACK * NQ], F32)
+        q_first = arena.tile([P, PASSES, PACK * NQ], F32, offset=45056)
         nc.sync.dma_start(q_first[:], qT[0].rearrange("(o p j) q -> p o (j q)", p=P, j=PACK))
         ident = sb.tile([P, P], F32)
         make_identity(nc, ident[:])
@@ -84,13 +84,13 @@ def tile_attend_draft_kernel(tc, qT, k_words, k_scales, vT, vs, pos, qpos, offs,
         for b, q_raw in enumerate((q_first, q_second)):
             nc.scalar.activation(q_bf[:, b * PASSES:(b + 1) * PASSES],
                                  q_raw[:].rearrange("p g (j q) -> p g q j", j=PACK), ACT.Copy)
-        pos_col = arena.tile([P, B, PACK], F32, offset=41024)
+        pos_col = arena.tile([P, B, PACK], F32, offset=45056)
         for b in range(B):
             turned = bank("a%d" % b, [P, PACK, P])
             for c in range(PACK):
                 nc.tensor.transpose(turned[:, c, :], pos_g[:, b * N + c * P:b * N + (c + 1) * P], ident[:])
             nc.scalar.copy(pos_col[:, b, :], turned[:, :, 0])
-        past = arena.tile([P, B, PACK, P], F32, offset=45056)
+        past = arena.tile([P, B, PACK, P], F32, offset=40960)
         for b in range(B):
             spread = bank("b%d" % b, [P, N])
             for c in range(PACK):
@@ -121,16 +121,13 @@ def tile_attend_draft_kernel(tc, qT, k_words, k_scales, vT, vs, pos, qpos, offs,
 
         vs_g = sb.tile([P, B * N], F32, align_bytes=64, tag="q_bf_then_vs_g")
         nc.vector.tensor_copy(vs_g[:], vs_win[:].indirect(offs_t[:]))
-        turned_vs = [bank("c%d" % b, [P, PACK, P]) for b in range(B)]
+        vs_col = [arena.tile([P, PACK], F32, offset=53248 + 1024 * b, name="vs_col%d" % b) for b in range(B)]
         for b in range(B):
-            for t in range(PACK):
-                nc.tensor.transpose(turned_vs[b][:, t, :], vs_g[:, b * N + t:(b + 1) * N:PACK], ident[:])
+            nc.sync.dma_start(vs_col[b][:], vs_g[0:1, b * N:(b + 1) * N])
 
         v1_win = sb.tile([P, T], BF16)
         for h in range(2):
             nc.scalar.activation(v1_win[:, h * 1024:(h + 1) * 1024], v1_raw[:, h * 1024:(h + 1) * 1024], ACT.Copy)
-
-        v_bf = sb.tile([P, B, DV, PACK], BF16, align_bytes=64)
 
         def turn_values(c, b, gathered, tag):
             words = gathered[:, b * N:(b + 1) * N].bitcast(F32)
@@ -140,10 +137,11 @@ def tile_attend_draft_kernel(tc, qT, k_words, k_scales, vT, vs, pos, qpos, offs,
             nc.scalar.copy(v_bf[:, b, c * P:(c + 1) * P, :].bitcast(F32), turned[:].rearrange("p u e -> p e u"))
 
         v_g1 = sb.tile([P, B * N], BF16)
-        nc.scalar.activation(v_g1[:, 0:N], v1_win[:].indirect(seq_offs[0]), ACT.Copy)
+        for b in range(B):
+            nc.scalar.activation(v_g1[:, b * N:(b + 1) * N], v1_win[:].indirect(seq_offs[b]), ACT.Copy)
 
         neg = arena.tile([P, B, PACK, P], F32, offset=24576)
-        clamped = [arena.tile([P, N], F32, offset=49152 + 2048 * b, name="clamped%d" % b) for b in range(B)]
+        clamped = [arena.tile([P, N], F32, offset=55296 + 2048 * b, name="clamped%d" % b) for b in range(B)]
         neg_max = [sb.tile([P, 1], F32, name="neg_max%d" % b) for b in range(B)]
         total = [sb.tile([P, 1], F32, name="total%d" % b) for b in range(B)]
         prob = arena.tile([P, B, N], F32, offset=8192)
@@ -161,28 +159,25 @@ def tile_attend_draft_kernel(tc, qT, k_words, k_scales, vT, vs, pos, qpos, offs,
                 nc.tensor.transpose(tp[:, t, :], prob[:, b, t * P:(t + 1) * P], ident[:])
             turned_p.append(tp)
 
-        vs_col = arena.tile([P, B, PACK], F32, offset=51200)
-        for b in range(B):
-            nc.scalar.copy(vs_col[:, b, :], turned_vs[b][:, :, 0])
-        nc.scalar.activation(v_g1[:, N:2 * N], v1_win[:].indirect(seq_offs[1]), ACT.Copy)
+        v_bf = arena.tile([P, B, DV, PACK], BF16, align_bytes=64, offset=55296)
         for b in range(B):
             turn_values(1, b, v_g1, "d%d" % b)
 
-        v_g0 = arena.tile([P, B * N], BF16, offset=47104)
+        v_g0 = arena.tile([P, B * N], BF16, offset=43008)
         nc.vector.tensor_copy(v_g0[:], v0_win[:].indirect(offs_t[:]))
         for b in range(B):
-            turn_values(0, b, v_g0, "a%d" % b)
+            turn_values(0, b, v_g0, "d%d" % b)
 
         w_bf = arena.tile([P, B, NQ, PACK], BF16, align_bytes=64, offset=16384)
         w_codes = sb.tile([P, B, NQ], U32, align_bytes=64)
         w_scales = sb.tile([P, B, NQ], U8, align_bytes=64)
-        v_codes = sb.tile([P, B, DV], U32, align_bytes=64)
+        v_codes = arena.tile([P, B, DV], U32, align_bytes=64, offset=53248)
         v_scales = sb.tile([P, B, DV], U8, align_bytes=64)
         inv = [sb.tile([P, 1], F32, name="inv%d" % b) for b in range(B)]
         y = sb.tile([P, B, DV], F32)
         for b in range(B):
             nc.vector.tensor_tensor(w_bf[:, b], turned_p[b][:].rearrange("p t q -> p q t"),
-                                    vs_col[:, b, :].unsqueeze(1).to_broadcast([P, NQ, PACK]), ALU.mult)
+                                    vs_col[b][:].unsqueeze(1).to_broadcast([P, NQ, PACK]), ALU.mult)
         for b in range(B):
             nc.vector.reciprocal(inv[b][:], total[b][:])
         for b in range(B):

@@ -23,6 +23,9 @@ PASSES = D // (P * PACK)
 COLS = N // 16
 MASKED = 30000.0
 FAR = float(2 ** 60)
+ULP = float(2 ** -23)
+NEAR = float(2 ** 30)
+ROW = P - 1
 
 
 def tile_attend_draft_kernel(tc, qT, k_words, k_scales, vT, vs, pos, qpos, offs, out):
@@ -40,138 +43,146 @@ def tile_attend_draft_kernel(tc, qT, k_words, k_scales, vT, vs, pos, qpos, offs,
         nc.sync.dma_start(offs_t[:], offs)
         seq_offs = [offs_t[:, b * COLS:(b + 1) * COLS] for b in range(B)]
 
-        qpos_t = arena.tile([P, 16], F32, offset=40928)
-        with nc.allow_non_contiguous_dma(reason="one place a query row"):
-            nc.sync.dma_start(qpos_t[:, 0:B], qpos.rearrange("b q o -> q (b o)"))
-        ks_rows = k_scales.bitcast(I32).rearrange("o f t -> f o t")
-        ks_win = arena.tile([P, T // 4], I32, offset=3072)
+        ks_win = arena.tile([P, T // 4], I32, offset=8192)
         nc.vector.memset(ks_win[:], 0)
+        vs_win = sb.tile([P, T], F32)
+        nc.sync.dma_start(vs_win[ROW:P, :], vs[0:1, :])
+        pos_cols = sb.tile([P, T // P], F32)
+        nc.sync.dma_start(pos_cols[:], pos[0].rearrange("(p j) -> p j", p=P))
+        ks_rows = k_scales.bitcast(I32).rearrange("o f t -> f o t")
         for r in range(4):
             nc.sync.dma_start(ks_win[r:P:16, :], ks_rows[r:16:4, :, :])
-        q_first = arena.tile([P, PASSES, PACK * NQ], F32, offset=45056)
-        nc.sync.dma_start(q_first[:], qT[0].rearrange("(o p j) q -> p o (j q)", p=P, j=PACK))
-        ident = sb.tile([P, P], F32)
-        make_identity(nc, ident[:])
-        pos_win = arena.tile([P, T], F32, offset=15360)
-        nc.vector.memset(pos_win[:], 0.0)
-        nc.sync.dma_start(pos_win[0:1, :], pos[0:1, :])
-        vs_win = arena.tile([P, T], F32, offset=24576)
-        nc.vector.memset(vs_win[:], 0.0)
-        nc.sync.dma_start(vs_win[0:1, :], vs[0:1, :])
-        qbias = sb.tile([P, B], F32)
-        nc.vector.tensor_scalar(qbias[:], qpos_t[:, 0:B], -FAR, None, ALU.mult)
-        kw_win = arena.tile([P, T], I32, offset=32768)
-        nc.sync.dma_start(kw_win[:], k_words[0].rearrange("p t c -> p (t c)").bitcast(I32))
-        q_second = arena.tile([P, PASSES, PACK * NQ], F32, offset=40960)
-        nc.sync.dma_start(q_second[:], qT[1].rearrange("(o p j) q -> p o (j q)", p=P, j=PACK))
+        nc.vector.memset(vs_win[0:ROW, :], 0.0)
         ks_low = sb.tile([P, B * N // 4], I32, align_bytes=64)
         nc.vector.memset(ks_low[96:P, :], 0)
+        kw_win = arena.tile([P, T], I32, offset=24576)
+        nc.sync.dma_start(kw_win[:], k_words[0].rearrange("p t c -> p (t c)").bitcast(I32))
+        q_raw = [sb.tile([P, PASSES, PACK * NQ], F32, name="q_raw%d" % b) for b in range(B)]
+        for b in range(B):
+            nc.sync.dma_start(q_raw[b][:], qT[b].rearrange("(o p j) q -> p o (j q)", p=P, j=PACK))
+        qpos_t = sb.tile([P, B], F32)
+        with nc.allow_non_contiguous_dma(reason="one place a query row"):
+            nc.sync.dma_start(qpos_t[:], qpos.rearrange("b q o -> q (b o)"))
 
+        ident = sb.tile([P, P], F32)
+        make_identity(nc, ident[:])
+        pos_win = sb.tile([P, T], F32)
+        for a, tag in enumerate(("a0", "a1", "b0", "b1")):
+            spread = bank(tag, [P, PACK, P])
+            for j in range(PACK):
+                nc.tensor.transpose(spread[:, j, :], pos_cols[:, PACK * a + j:PACK * a + j + 1].to_broadcast([P, P]),
+                                    ident[:])
+            nc.scalar.activation(pos_win[:].rearrange("q (n j) -> q n j", j=T // P)[:, :, PACK * a:PACK * (a + 1)],
+                                 spread[:].rearrange("q j n -> q n j"), ACT.Copy)
+
+        vs_g = sb.tile([P, B * N], F32)
+        nc.vector.tensor_copy(vs_g[:], vs_win[:].indirect(offs_t[:]))
         ks_g = sb.tile([P, B * N], U8, align_bytes=64)
         nc.vector.tensor_copy(ks_g[:], ks_win[:].bitcast(U8).indirect(offs_t[:]))
         for lo, hi in ((0, 64), (64, 96), (96, 112)):
             nc.sync.dma_start(ks_low[lo:hi, :], ks_g[lo + 16:hi + 16, :].bitcast(I32))
         ks_plane = [ks_g[:], ks_low[:].bitcast(U8)]
-        v1_raw = arena.tile([P, T], F32, offset=4096)
+        vs_col = [arena.tile([P, PACK], F32, offset=36864 + 1024 * b, name="vs_col%d" % b) for b in range(B)]
+        for b in range(B):
+            nc.sync.dma_start(vs_col[b][:], vs_g[ROW:P, b * N:(b + 1) * N])
+        v1_raw = arena.tile([P, T], F32, offset=1024)
         for h in range(2):
             nc.sync.dma_start(v1_raw[:, h * 1024:(h + 1) * 1024], vT[P:2 * P, h * 1024:(h + 1) * 1024])
-        pos_g = arena.tile([P, B * N], F32, offset=0)
-        nc.vector.tensor_copy(pos_g[:], pos_win[:].indirect(offs_t[:]))
-        v0_win = arena.tile([P, T], F32, offset=16384)
+        v0_win = arena.tile([P, T], F32, offset=9216)
         nc.sync.dma_start(v0_win[:], vT[0:P, :])
 
-        q_bf = sb.tile([P, B * PASSES, NQ, PACK], BF16, align_bytes=64, tag="q_bf_then_vs_g")
-        for b, q_raw in enumerate((q_first, q_second)):
+        q_bf = sb.tile([P, B * PASSES, NQ, PACK], BF16, align_bytes=64)
+        for b in range(B):
             nc.scalar.activation(q_bf[:, b * PASSES:(b + 1) * PASSES],
-                                 q_raw[:].rearrange("p g (j q) -> p g q j", j=PACK), ACT.Copy)
-        pos_col = arena.tile([P, B, PACK], F32, offset=45056)
-        for b in range(B):
-            turned = bank("a%d" % b, [P, PACK, P])
-            for c in range(PACK):
-                nc.tensor.transpose(turned[:, c, :], pos_g[:, b * N + c * P:b * N + (c + 1) * P], ident[:])
-            nc.scalar.copy(pos_col[:, b, :], turned[:, :, 0])
-        past = arena.tile([P, B, PACK, P], F32, offset=40960)
-        for b in range(B):
-            spread = bank("b%d" % b, [P, N])
-            for c in range(PACK):
-                nc.tensor.transpose(spread[:, c * P:(c + 1) * P], pos_col[:, b, c:c + 1].to_broadcast([P, P]), ident[:])
-            nc.scalar.activation(past[:, b], spread[:].rearrange("q (s t) -> q t s", t=PACK), ACT.Relu,
-                                 bias=qbias[:, b:b + 1], scale=FAR)
+                                 q_raw[b][:].rearrange("p g (j q) -> p g q j", j=PACK), ACT.Copy, scale=-1.0)
+        q_up = sb.tile([P, B], F32)
+        nc.scalar.activation(q_up[:], qpos_t[:], ACT.Copy, scale=FAR * (1.0 + ULP))
 
-        kw_g = arena.tile([P, B * N], U32, offset=12288)
-        nc.vector.tensor_copy(kw_g[:], kw_win[:].bitcast(U32).indirect(offs_t[:]))
-        keys = sb.tile([P, B, PASSES, 2 * N], U8, align_bytes=64)
-        q_codes = arena.tile([P, B * PASSES * NQ], U32, align_bytes=64, offset=33792)
-        q_scales = sb.tile([P, B * PASSES * NQ], U8, align_bytes=64)
-        scores = []
+        kw_g = [arena.tile([P, N], U32, offset=32768, name="kw_g0"), sb.tile([P, N], U32, name="kw_g1")]
         for b in range(B):
-            g = slice(b * PASSES, (b + 1) * PASSES)
+            nc.vector.tensor_copy(kw_g[b][:], kw_win[:].bitcast(U32).indirect(seq_offs[b]))
+        keys = sb.tile([P, B, PASSES, 2 * N], U8, align_bytes=64)
+        q_scales = sb.tile([P, B * PASSES * NQ], U8, align_bytes=64)
+        pos_g = [arena.tile([P, N], F32, offset=24576 + 2048 * b, name="pos_g%d" % b) for b in range(B)]
+        scores = []
+
+        def split(b):
+            nc.vector.tensor_copy(keys[:, b].bitcast(U16), kw_g[b][:].bitcast(U16).rearrange("p (n o) -> p o n", o=PASSES))
+
+        def places(b):
+            nc.vector.tensor_scalar(pos_g[b][:], pos_win[:].indirect(seq_offs[b]), FAR, -NEAR, ALU.mult, ALU.add)
+
+        def score(b):
+            q_codes = arena.tile([P, PASSES * NQ], U32, align_bytes=64, offset=32768 + 1024 * b, name="q_codes%d" % b)
             cols = slice(b * PASSES * NQ, (b + 1) * PASSES * NQ)
-            nc.vector.quantize_mx(q_codes[:, cols].bitcast(FP8X4), q_scales[:, cols],
-                                  q_bf[:, g].rearrange("p g q j -> p (g q j)"))
-            nc.vector.tensor_copy(keys[:, b].bitcast(U16),
-                                  kw_g[:, b * N:(b + 1) * N].bitcast(U16).rearrange("p (n o) -> p o n", o=PASSES))
+            nc.vector.quantize_mx(q_codes[:].bitcast(FP8X4), q_scales[:, cols],
+                                  q_bf[:, b * PASSES:(b + 1) * PASSES].rearrange("p g q j -> p (g q j)"))
             acc = bank("a%d" % b, [P, N])
             for o in range(PASSES):
                 qc = slice((b * PASSES + o) * NQ, (b * PASSES + o + 1) * NQ)
-                nc.tensor.matmul_mx(acc[:], lhsT=q_codes[:, qc].bitcast(FP8X4), lhsT_scale=q_scales[:, qc],
+                nc.tensor.matmul_mx(acc[:], lhsT=q_codes[:, o * NQ:(o + 1) * NQ].bitcast(FP8X4), lhsT_scale=q_scales[:, qc],
                                     rhs=keys[:, b, o, :].bitcast(FP4X4), rhs_scale=ks_plane[o][:, b * N:(b + 1) * N],
                                     start=(o == 0), stop=(o == PASSES - 1))
             scores.append(acc)
 
-        vs_g = sb.tile([P, B * N], F32, align_bytes=64, tag="q_bf_then_vs_g")
-        nc.vector.tensor_copy(vs_g[:], vs_win[:].indirect(offs_t[:]))
-        vs_col = [arena.tile([P, PACK], F32, offset=53248 + 1024 * b, name="vs_col%d" % b) for b in range(B)]
-        for b in range(B):
-            nc.sync.dma_start(vs_col[b][:], vs_g[0:1, b * N:(b + 1) * N])
+        split(0)
+        places(0)
+        score(0)
+        split(1)
+        score(1)
+        places(1)
+        q_far = sb.tile([P, B], F32)
+        nc.vector.scalar_tensor_tensor(q_far[:], qpos_t[:], FAR * (1.0 - ULP), q_up[:], ALU.mult, ALU.max)
 
-        v1_win = sb.tile([P, T], BF16)
+        v1_win = arena.tile([P, T], BF16, offset=20480)
         for h in range(2):
             nc.scalar.activation(v1_win[:, h * 1024:(h + 1) * 1024], v1_raw[:, h * 1024:(h + 1) * 1024], ACT.Copy)
-
-        def turn_values(c, b, gathered, tag):
-            words = gathered[:, b * N:(b + 1) * N].bitcast(F32)
-            turned = bank(tag, [P, 2, P])
-            for u in range(2):
-                nc.tensor.transpose(turned[:, u, :], words[:, u:N // 2:2], ident[:])
-            nc.scalar.copy(v_bf[:, b, c * P:(c + 1) * P, :].bitcast(F32), turned[:].rearrange("p u e -> p e u"))
-
         v_g1 = sb.tile([P, B * N], BF16)
         for b in range(B):
             nc.scalar.activation(v_g1[:, b * N:(b + 1) * N], v1_win[:].indirect(seq_offs[b]), ACT.Copy)
 
-        neg = arena.tile([P, B, PACK, P], F32, offset=24576)
-        clamped = [arena.tile([P, N], F32, offset=55296 + 2048 * b, name="clamped%d" % b) for b in range(B)]
+        v_bf = sb.tile([P, B, DV, PACK], BF16, align_bytes=64)
+
+        def turn_values(gathered, b, tag):
+            words = gathered[:, b * N:(b + 1) * N].bitcast(F32)
+            turned = bank(tag, [P, 2, P])
+            for u in range(2):
+                nc.tensor.transpose(turned[:, u, :], words[:, u:N // 2:2], ident[:])
+            return turned
+
+        def lay_values(c, b, turned):
+            nc.scalar.copy(v_bf[:, b, c * P:(c + 1) * P, :].bitcast(F32), turned[:].rearrange("p u e -> p e u"))
+
+        turned_v1 = [turn_values(v_g1, b, "d%d" % b) for b in range(B)]
+
+        neg = sb.tile([P, B, N], F32)
+        clamped = sb.tile([P, B, N], F32)
         neg_max = [sb.tile([P, 1], F32, name="neg_max%d" % b) for b in range(B)]
         total = [sb.tile([P, 1], F32, name="total%d" % b) for b in range(B)]
-        prob = arena.tile([P, B, N], F32, offset=8192)
+        prob = [arena.tile([P, PACK, P], F32, offset=off, name="prob%d" % b) for b, off in enumerate((2048, 20480))]
         turned_p = []
         for b in range(B):
-            nc.vector.tensor_tensor(neg[:, b], past[:, b], scores[b][:].rearrange("q (s t) -> q t s", t=PACK),
-                                    ALU.subtract)
+            nc.vector.scalar_tensor_tensor(neg[:, b], pos_g[b][:], q_far[:, b:b + 1], scores[b][:], ALU.subtract, ALU.max)
         for b in range(B):
-            nc.vector.tensor_scalar(clamped[b][:], neg[:, b].rearrange("q t s -> q (t s)"), MASKED, None,
-                                    ALU.min, ALU.min, accum_out=neg_max[b][:])
-            nc.scalar.activation(prob[:, b, :], clamped[b][:], ACT.Exp,
-                                 bias=neg_max[b][:], scale=-1.0, accum_out=total[b][:])
+            nc.vector.tensor_scalar(clamped[:, b], neg[:, b], MASKED, None, ALU.min, ALU.min, accum_out=neg_max[b][:])
+            nc.scalar.activation(prob[b][:].rearrange("q t s -> q s t"), clamped[:, b].rearrange("q (s t) -> q s t", t=PACK),
+                                 ACT.Exp, bias=neg_max[b][:], scale=-1.0, accum_out=total[b][:])
             tp = bank("b%d" % b, [P, PACK, NQ])
             for t in range(PACK):
-                nc.tensor.transpose(tp[:, t, :], prob[:, b, t * P:(t + 1) * P], ident[:])
+                nc.tensor.transpose(tp[:, t, :], prob[b][:, t, :], ident[:])
             turned_p.append(tp)
-
-        v_bf = arena.tile([P, B, DV, PACK], BF16, align_bytes=64, offset=55296)
         for b in range(B):
-            turn_values(1, b, v_g1, "d%d" % b)
+            lay_values(1, b, turned_v1[b])
 
-        v_g0 = arena.tile([P, B * N], BF16, offset=43008)
+        v_g0 = arena.tile([P, B * N], BF16, offset=26624)
         nc.vector.tensor_copy(v_g0[:], v0_win[:].indirect(offs_t[:]))
         for b in range(B):
-            turn_values(0, b, v_g0, "d%d" % b)
+            lay_values(0, b, turn_values(v_g0, b, "a%d" % b))
 
-        w_bf = arena.tile([P, B, NQ, PACK], BF16, align_bytes=64, offset=16384)
+        w_bf = arena.tile([P, B, NQ, PACK], BF16, align_bytes=64, offset=12288)
         w_codes = sb.tile([P, B, NQ], U32, align_bytes=64)
         w_scales = sb.tile([P, B, NQ], U8, align_bytes=64)
-        v_codes = arena.tile([P, B, DV], U32, align_bytes=64, offset=53248)
+        v_codes = arena.tile([P, B, DV], U32, align_bytes=64, offset=36864)
         v_scales = sb.tile([P, B, DV], U8, align_bytes=64)
         inv = [sb.tile([P, 1], F32, name="inv%d" % b) for b in range(B)]
         y = sb.tile([P, B, DV], F32)
@@ -180,11 +191,10 @@ def tile_attend_draft_kernel(tc, qT, k_words, k_scales, vT, vs, pos, qpos, offs,
                                     vs_col[b][:].unsqueeze(1).to_broadcast([P, NQ, PACK]), ALU.mult)
         for b in range(B):
             nc.vector.reciprocal(inv[b][:], total[b][:])
+        sums = []
         for b in range(B):
             nc.vector.quantize_mx(w_codes[:, b, :].bitcast(FP8X4), w_scales[:, b, :],
                                   w_bf[:, b].rearrange("p q t -> p (q t)"))
-        sums = []
-        for b in range(B):
             nc.vector.quantize_mx(v_codes[:, b, :].bitcast(FP8X4), v_scales[:, b, :],
                                   v_bf[:, b].rearrange("p e t -> p (e t)"))
             acc = bank("c%d" % b, [P, DV])

@@ -91,9 +91,10 @@ def tile_attend_draft_kernel(tc, qT, k_words, k_scales, vT, vs, pos, qpos, offs,
         v0_win = arena.tile([P, T], F32, offset=9216)
         nc.sync.dma_start(v0_win[:], vT[0:P, :])
 
-        q_bf = sb.tile([P, B * PASSES, NQ, PACK], BF16, align_bytes=64)
+        q_bf = [arena.tile([P, PASSES, NQ, PACK], BF16, align_bytes=64, offset=40960 + 4096 * b, name="q_bf%d" % b)
+                for b in range(B)]
         for b in range(B):
-            nc.scalar.activation(q_bf[:, b * PASSES:(b + 1) * PASSES],
+            nc.scalar.activation(q_bf[b][:],
                                  q_raw[b][:].rearrange("p g (j q) -> p g q j", j=PACK), ACT.Copy, scale=-1.0)
         q_up = sb.tile([P, B], F32)
         nc.scalar.activation(q_up[:], qpos_t[:], ACT.Copy, scale=FAR * (1.0 + ULP))
@@ -101,13 +102,14 @@ def tile_attend_draft_kernel(tc, qT, k_words, k_scales, vT, vs, pos, qpos, offs,
         kw_g = [arena.tile([P, N], U32, offset=32768, name="kw_g0"), sb.tile([P, N], U32, name="kw_g1")]
         for b in range(B):
             nc.vector.tensor_copy(kw_g[b][:], kw_win[:].bitcast(U32).indirect(seq_offs[b]))
-        keys = sb.tile([P, B, PASSES, 2 * N], U8, align_bytes=64)
+        keys = [sb.tile([P, PASSES, 2 * N], U8, align_bytes=64, name="keys0"),
+                arena.tile([P, PASSES, 2 * N], U8, align_bytes=64, offset=41984, name="keys1")]
         q_scales = sb.tile([P, B * PASSES * NQ], U8, align_bytes=64)
-        pos_g = [arena.tile([P, N], F32, offset=24576 + 2048 * b, name="pos_g%d" % b) for b in range(B)]
+        pos_g = [arena.tile([P, N], F32, offset=off, name="pos_g%d" % b) for b, off in enumerate((39936, 45056))]
         scores = []
 
         def split(b):
-            nc.vector.tensor_copy(keys[:, b].bitcast(U16), kw_g[b][:].bitcast(U16).rearrange("p (n o) -> p o n", o=PASSES))
+            nc.vector.tensor_copy(keys[b][:].bitcast(U16), kw_g[b][:].bitcast(U16).rearrange("p (n o) -> p o n", o=PASSES))
 
         def places(b):
             nc.vector.tensor_scalar(pos_g[b][:], pos_win[:].indirect(seq_offs[b]), FAR, -NEAR, ALU.mult, ALU.add)
@@ -116,23 +118,22 @@ def tile_attend_draft_kernel(tc, qT, k_words, k_scales, vT, vs, pos, qpos, offs,
             q_codes = arena.tile([P, PASSES * NQ], U32, align_bytes=64, offset=32768 + 1024 * b, name="q_codes%d" % b)
             cols = slice(b * PASSES * NQ, (b + 1) * PASSES * NQ)
             nc.vector.quantize_mx(q_codes[:].bitcast(FP8X4), q_scales[:, cols],
-                                  q_bf[:, b * PASSES:(b + 1) * PASSES].rearrange("p g q j -> p (g q j)"))
+                                  q_bf[b][:].rearrange("p g q j -> p (g q j)"))
             acc = bank("a%d" % b, [P, N])
             for o in range(PASSES):
                 qc = slice((b * PASSES + o) * NQ, (b * PASSES + o + 1) * NQ)
                 nc.tensor.matmul_mx(acc[:], lhsT=q_codes[:, o * NQ:(o + 1) * NQ].bitcast(FP8X4), lhsT_scale=q_scales[:, qc],
-                                    rhs=keys[:, b, o, :].bitcast(FP4X4), rhs_scale=ks_plane[o][:, b * N:(b + 1) * N],
+                                    rhs=keys[b][:, o, :].bitcast(FP4X4), rhs_scale=ks_plane[o][:, b * N:(b + 1) * N],
                                     start=(o == 0), stop=(o == PASSES - 1))
             scores.append(acc)
 
-        split(0)
-        places(0)
-        score(0)
-        split(1)
-        score(1)
-        places(1)
+        for b in range(B):
+            split(b)
+            score(b)
         q_far = sb.tile([P, B], F32)
         nc.vector.scalar_tensor_tensor(q_far[:], qpos_t[:], FAR * (1.0 - ULP), q_up[:], ALU.mult, ALU.max)
+        for b in range(B):
+            places(b)
 
         v1_win = arena.tile([P, T], BF16, offset=20480)
         for h in range(2):
@@ -174,7 +175,7 @@ def tile_attend_draft_kernel(tc, qT, k_words, k_scales, vT, vs, pos, qpos, offs,
         for b in range(B):
             lay_values(1, b, turned_v1[b])
 
-        v_g0 = arena.tile([P, B * N], BF16, offset=26624)
+        v_g0 = arena.tile([P, B * N], BF16, offset=45056)
         nc.vector.tensor_copy(v_g0[:], v0_win[:].indirect(offs_t[:]))
         for b in range(B):
             lay_values(0, b, turn_values(v_g0, b, "a%d" % b))
@@ -184,7 +185,7 @@ def tile_attend_draft_kernel(tc, qT, k_words, k_scales, vT, vs, pos, qpos, offs,
         w_scales = sb.tile([P, B, NQ], U8, align_bytes=64)
         v_codes = arena.tile([P, B, DV], U32, align_bytes=64, offset=36864)
         v_scales = sb.tile([P, B, DV], U8, align_bytes=64)
-        inv = [sb.tile([P, 1], F32, name="inv%d" % b) for b in range(B)]
+        inv = [arena.tile([P, 1], F32, offset=16384 + 32 * b, name="inv%d" % b) for b in range(B)]
         y = sb.tile([P, B, DV], F32)
         for b in range(B):
             nc.vector.tensor_tensor(w_bf[:, b], turned_p[b][:].rearrange("p t q -> p q t"),

@@ -49,20 +49,23 @@ def tile_attend_draft_kernel(tc, qT, k_words, k_scales, vT, vs, pos, qpos, offs,
         nc.sync.dma_start(vs_win[ROW:P, :], vs[0:1, :])
         pos_cols = sb.tile([P, T // P], F32)
         nc.sync.dma_start(pos_cols[:], pos[0].rearrange("(p j) -> p j", p=P))
+        kw_win = arena.tile([P, T], I32, offset=24576)
+        nc.sync.dma_start(kw_win[:], k_words[0].rearrange("p t c -> p (t c)").bitcast(I32))
         ks_rows = k_scales.bitcast(I32).rearrange("o f t -> f o t")
         for r in range(4):
             nc.sync.dma_start(ks_win[r:P:16, :], ks_rows[r:16:4, :, :])
         nc.vector.memset(vs_win[0:ROW, :], 0.0)
         ks_low = sb.tile([P, B * N // 4], I32, align_bytes=64)
         nc.vector.memset(ks_low[96:P, :], 0)
-        kw_win = arena.tile([P, T], I32, offset=24576)
-        nc.sync.dma_start(kw_win[:], k_words[0].rearrange("p t c -> p (t c)").bitcast(I32))
         q_raw = [sb.tile([P, PASSES, PACK * NQ], F32, name="q_raw%d" % b) for b in range(B)]
         for b in range(B):
             nc.sync.dma_start(q_raw[b][:], qT[b].rearrange("(o p j) q -> p o (j q)", p=P, j=PACK))
         qpos_t = sb.tile([P, B], F32)
         with nc.allow_non_contiguous_dma(reason="one place a query row"):
             nc.sync.dma_start(qpos_t[:], qpos.rearrange("b q o -> q (b o)"))
+
+        v1_raw = [sb.tile([P, T // 2], F32, name="v1_raw0"), arena.tile([P, T // 2], F32, offset=5120, name="v1_raw1")]
+        nc.sync.dma_start(v1_raw[0][:], vT[P:2 * P, 0:T // 2])
 
         ident = sb.tile([P, P], F32)
         make_identity(nc, ident[:])
@@ -77,6 +80,9 @@ def tile_attend_draft_kernel(tc, qT, k_words, k_scales, vT, vs, pos, qpos, offs,
 
         vs_g = sb.tile([P, B * N], F32)
         nc.vector.tensor_copy(vs_g[:], vs_win[:].indirect(offs_t[:]))
+        kw_g = [arena.tile([P, N], U32, offset=32768, name="kw_g0"), sb.tile([P, N], U32, name="kw_g1")]
+        for b in range(B):
+            nc.vector.tensor_copy(kw_g[b][:], kw_win[:].bitcast(U32).indirect(seq_offs[b]))
         ks_g = sb.tile([P, B * N], U8, align_bytes=64)
         nc.vector.tensor_copy(ks_g[:], ks_win[:].bitcast(U8).indirect(offs_t[:]))
         for lo, hi in ((0, 64), (64, 96), (96, 112)):
@@ -85,9 +91,7 @@ def tile_attend_draft_kernel(tc, qT, k_words, k_scales, vT, vs, pos, qpos, offs,
         vs_col = [arena.tile([P, PACK], F32, offset=36864 + 1024 * b, name="vs_col%d" % b) for b in range(B)]
         for b in range(B):
             nc.sync.dma_start(vs_col[b][:], vs_g[ROW:P, b * N:(b + 1) * N])
-        v1_raw = arena.tile([P, T], F32, offset=1024)
-        for h in range(2):
-            nc.sync.dma_start(v1_raw[:, h * 1024:(h + 1) * 1024], vT[P:2 * P, h * 1024:(h + 1) * 1024])
+        nc.sync.dma_start(v1_raw[1][:], vT[P:2 * P, T // 2:T])
         v0_win = arena.tile([P, T], F32, offset=9216)
         nc.sync.dma_start(v0_win[:], vT[0:P, :])
 
@@ -99,9 +103,6 @@ def tile_attend_draft_kernel(tc, qT, k_words, k_scales, vT, vs, pos, qpos, offs,
         q_up = sb.tile([P, B], F32)
         nc.scalar.activation(q_up[:], qpos_t[:], ACT.Copy, scale=FAR * (1.0 + ULP))
 
-        kw_g = [arena.tile([P, N], U32, offset=32768, name="kw_g0"), sb.tile([P, N], U32, name="kw_g1")]
-        for b in range(B):
-            nc.vector.tensor_copy(kw_g[b][:], kw_win[:].bitcast(U32).indirect(seq_offs[b]))
         keys = [sb.tile([P, PASSES, 2 * N], U8, align_bytes=64, name="keys0"),
                 arena.tile([P, PASSES, 2 * N], U8, align_bytes=64, offset=41984, name="keys1")]
         q_scales = sb.tile([P, B * PASSES * NQ], U8, align_bytes=64)
@@ -137,12 +138,11 @@ def tile_attend_draft_kernel(tc, qT, k_words, k_scales, vT, vs, pos, qpos, offs,
 
         v1_win = arena.tile([P, T], BF16, offset=20480)
         for h in range(2):
-            nc.scalar.activation(v1_win[:, h * 1024:(h + 1) * 1024], v1_raw[:, h * 1024:(h + 1) * 1024], ACT.Copy)
+            nc.scalar.activation(v1_win[:, h * 1024:(h + 1) * 1024], v1_raw[h][:], ACT.Copy)
         v_g1 = sb.tile([P, B * N], BF16)
         for b in range(B):
             nc.scalar.activation(v_g1[:, b * N:(b + 1) * N], v1_win[:].indirect(seq_offs[b]), ACT.Copy)
 
-        v_bf = sb.tile([P, B, DV, PACK], BF16, align_bytes=64)
 
         def turn_values(gathered, b, tag):
             words = gathered[:, b * N:(b + 1) * N].bitcast(F32)
@@ -157,10 +157,10 @@ def tile_attend_draft_kernel(tc, qT, k_words, k_scales, vT, vs, pos, qpos, offs,
         turned_v1 = [turn_values(v_g1, b, "d%d" % b) for b in range(B)]
 
         neg = sb.tile([P, B, N], F32)
-        clamped = sb.tile([P, B, N], F32)
+        clamped = arena.tile([P, B, N], F32, offset=49152)
         neg_max = [sb.tile([P, 1], F32, name="neg_max%d" % b) for b in range(B)]
         total = [sb.tile([P, 1], F32, name="total%d" % b) for b in range(B)]
-        prob = [arena.tile([P, PACK, P], F32, offset=off, name="prob%d" % b) for b, off in enumerate((2048, 20480))]
+        prob = [arena.tile([P, PACK, P], F32, offset=off, name="prob%d" % b) for b, off in enumerate((6144, 20480))]
         turned_p = []
         for b in range(B):
             nc.vector.scalar_tensor_tensor(neg[:, b], pos_g[b][:], q_far[:, b:b + 1], scores[b][:], ALU.subtract, ALU.max)
@@ -172,13 +172,14 @@ def tile_attend_draft_kernel(tc, qT, k_words, k_scales, vT, vs, pos, qpos, offs,
             for t in range(PACK):
                 nc.tensor.transpose(tp[:, t, :], prob[b][:, t, :], ident[:])
             turned_p.append(tp)
+        v_bf = arena.tile([P, B, DV, PACK], BF16, align_bytes=64, offset=49152)
         for b in range(B):
             lay_values(1, b, turned_v1[b])
 
         v_g0 = arena.tile([P, B * N], BF16, offset=45056)
         nc.vector.tensor_copy(v_g0[:], v0_win[:].indirect(offs_t[:]))
         for b in range(B):
-            lay_values(0, b, turn_values(v_g0, b, "a%d" % b))
+            lay_values(0, b, turn_values(v_g0, b, "d%d" % b))
 
         w_bf = arena.tile([P, B, NQ, PACK], BF16, align_bytes=64, offset=12288)
         w_codes = sb.tile([P, B, NQ], U32, align_bytes=64)

@@ -50,10 +50,12 @@ def tile_attend_draft_kernel(tc, qT, k_words, k_scales, vT, vs, pos, qpos, offs,
         pos_cols = sb.tile([P, T // P], F32)
         nc.sync.dma_start(pos_cols[:], pos[0].rearrange("(p j) -> p j", p=P))
         kw_win = arena.tile([P, T], I32, offset=24576)
-        nc.sync.dma_start(kw_win[:], k_words[0].rearrange("p t c -> p (t c)").bitcast(I32))
+        kw_rows = k_words[0].rearrange("p t c -> p (t c)").bitcast(I32)
+        nc.sync.dma_start(kw_win[:, 0:T // 2], kw_rows[:, 0:T // 2])
         ks_rows = k_scales.bitcast(I32).rearrange("o f t -> f o t")
         for r in range(4):
             nc.sync.dma_start(ks_win[r:P:16, :], ks_rows[r:16:4, :, :])
+        nc.sync.dma_start(kw_win[:, T // 2:T], kw_rows[:, T // 2:T])
         nc.vector.memset(vs_win[0:ROW, :], 0.0)
         ks_low = sb.tile([P, B * N // 4], I32, align_bytes=64)
         nc.vector.memset(ks_low[96:P, :], 0)
@@ -64,8 +66,11 @@ def tile_attend_draft_kernel(tc, qT, k_words, k_scales, vT, vs, pos, qpos, offs,
         with nc.allow_non_contiguous_dma(reason="one place a query row"):
             nc.sync.dma_start(qpos_t[:], qpos.rearrange("b q o -> q (b o)"))
 
-        v1_raw = [sb.tile([P, T // 2], F32, name="v1_raw0"), arena.tile([P, T // 2], F32, offset=5120, name="v1_raw1")]
-        nc.sync.dma_start(v1_raw[0][:], vT[P:2 * P, 0:T // 2])
+        v1_raw = [sb.tile([P, T // 2], F32, name="v1_raw0"), arena.tile([P, T // 2], F32, offset=4096, name="v1_raw1")]
+        for h in range(2):
+            nc.sync.dma_start(v1_raw[h][:], vT[P:2 * P, h * T // 2:(h + 1) * T // 2])
+        v0_win = arena.tile([P, T], F32, offset=10240)
+        nc.sync.dma_start(v0_win[:], vT[0:P, :])
 
         ident = sb.tile([P, P], F32)
         make_identity(nc, ident[:])
@@ -80,20 +85,13 @@ def tile_attend_draft_kernel(tc, qT, k_words, k_scales, vT, vs, pos, qpos, offs,
 
         vs_g = sb.tile([P, B * N], F32)
         nc.vector.tensor_copy(vs_g[:], vs_win[:].indirect(offs_t[:]))
-        kw_g = [arena.tile([P, N], U32, offset=32768, name="kw_g0"), sb.tile([P, N], U32, name="kw_g1")]
-        for b in range(B):
-            nc.vector.tensor_copy(kw_g[b][:], kw_win[:].bitcast(U32).indirect(seq_offs[b]))
         ks_g = sb.tile([P, B * N], U8, align_bytes=64)
         nc.vector.tensor_copy(ks_g[:], ks_win[:].bitcast(U8).indirect(offs_t[:]))
-        for lo, hi in ((0, 64), (64, 96), (96, 112)):
-            nc.sync.dma_start(ks_low[lo:hi, :], ks_g[lo + 16:hi + 16, :].bitcast(I32))
+        nc.gpsimd.dma_start(ks_low[0:P - 16, :], ks_g[16:P, :].bitcast(I32))
         ks_plane = [ks_g[:], ks_low[:].bitcast(U8)]
         vs_col = [arena.tile([P, PACK], F32, offset=36864 + 1024 * b, name="vs_col%d" % b) for b in range(B)]
         for b in range(B):
             nc.sync.dma_start(vs_col[b][:], vs_g[ROW:P, b * N:(b + 1) * N])
-        nc.sync.dma_start(v1_raw[1][:], vT[P:2 * P, T // 2:T])
-        v0_win = arena.tile([P, T], F32, offset=9216)
-        nc.sync.dma_start(v0_win[:], vT[0:P, :])
 
         q_bf = [arena.tile([P, PASSES, NQ, PACK], BF16, align_bytes=64, offset=40960 + 4096 * b, name="q_bf%d" % b)
                 for b in range(B)]
@@ -103,6 +101,9 @@ def tile_attend_draft_kernel(tc, qT, k_words, k_scales, vT, vs, pos, qpos, offs,
         q_up = sb.tile([P, B], F32)
         nc.scalar.activation(q_up[:], qpos_t[:], ACT.Copy, scale=FAR * (1.0 + ULP))
 
+        kw_g = [arena.tile([P, N], U32, offset=32768, name="kw_g0"), sb.tile([P, N], U32, name="kw_g1")]
+        for b in range(B):
+            nc.vector.tensor_copy(kw_g[b][:], kw_win[:].bitcast(U32).indirect(seq_offs[b]))
         keys = [sb.tile([P, PASSES, 2 * N], U8, align_bytes=64, name="keys0"),
                 arena.tile([P, PASSES, 2 * N], U8, align_bytes=64, offset=41984, name="keys1")]
         q_scales = sb.tile([P, B * PASSES * NQ], U8, align_bytes=64)

@@ -66,11 +66,6 @@ def tile_attend_draft_kernel(tc, qT, k_words, k_scales, vT, vs, pos, qpos, offs,
         with nc.allow_non_contiguous_dma(reason="one place a query row"):
             nc.sync.dma_start(qpos_t[:], qpos.rearrange("b q o -> q (b o)"))
 
-        v1_raw = [sb.tile([P, T // 2], F32, name="v1_raw0"), arena.tile([P, T // 2], F32, offset=4096, name="v1_raw1")]
-        for h in range(2):
-            nc.sync.dma_start(v1_raw[h][:], vT[P:2 * P, h * T // 2:(h + 1) * T // 2])
-        v0_win = arena.tile([P, T], F32, offset=10240)
-        nc.sync.dma_start(v0_win[:], vT[0:P, :])
 
         ident = sb.tile([P, P], F32)
         make_identity(nc, ident[:])
@@ -87,7 +82,13 @@ def tile_attend_draft_kernel(tc, qT, k_words, k_scales, vT, vs, pos, qpos, offs,
         nc.vector.tensor_copy(vs_g[:], vs_win[:].indirect(offs_t[:]))
         ks_g = sb.tile([P, B * N], U8, align_bytes=64)
         nc.vector.tensor_copy(ks_g[:], ks_win[:].bitcast(U8).indirect(offs_t[:]))
-        nc.gpsimd.dma_start(ks_low[0:P - 16, :], ks_g[16:P, :].bitcast(I32))
+        for lo, hi in ((0, 64), (64, 96), (96, 112)):
+            nc.sync.dma_start(ks_low[lo:hi, :], ks_g[lo + 16:hi + 16, :].bitcast(I32))
+        v1_raw = arena.tile([P, T], F32, offset=1024)
+        for h in range(2):
+            nc.sync.dma_start(v1_raw[:, h * T // 2:(h + 1) * T // 2], vT[P:2 * P, h * T // 2:(h + 1) * T // 2])
+        v0_win = arena.tile([P, T], F32, offset=9216)
+        nc.sync.dma_start(v0_win[:], vT[0:P, :])
         ks_plane = [ks_g[:], ks_low[:].bitcast(U8)]
         vs_col = [arena.tile([P, PACK], F32, offset=36864 + 1024 * b, name="vs_col%d" % b) for b in range(B)]
         for b in range(B):
@@ -139,14 +140,13 @@ def tile_attend_draft_kernel(tc, qT, k_words, k_scales, vT, vs, pos, qpos, offs,
 
         v1_win = arena.tile([P, T], BF16, offset=20480)
         for h in range(2):
-            nc.scalar.activation(v1_win[:, h * 1024:(h + 1) * 1024], v1_raw[h][:], ACT.Copy)
-        v_g1 = sb.tile([P, B * N], BF16)
-        for b in range(B):
-            nc.scalar.activation(v_g1[:, b * N:(b + 1) * N], v1_win[:].indirect(seq_offs[b]), ACT.Copy)
+            nc.scalar.activation(v1_win[:, h * 1024:(h + 1) * 1024], v1_raw[:, h * 1024:(h + 1) * 1024], ACT.Copy)
+        v_g1 = [sb.tile([P, N], BF16, name="v_g10"), arena.tile([P, N], BF16, offset=53248, name="v_g11")]
+        nc.scalar.activation(v_g1[0][:], v1_win[:].indirect(seq_offs[0]), ACT.Copy)
 
 
-        def turn_values(gathered, b, tag):
-            words = gathered[:, b * N:(b + 1) * N].bitcast(F32)
+        def turn_values(gathered, tag):
+            words = gathered.bitcast(F32)
             turned = bank(tag, [P, 2, P])
             for u in range(2):
                 nc.tensor.transpose(turned[:, u, :], words[:, u:N // 2:2], ident[:])
@@ -155,13 +155,13 @@ def tile_attend_draft_kernel(tc, qT, k_words, k_scales, vT, vs, pos, qpos, offs,
         def lay_values(c, b, turned):
             nc.scalar.copy(v_bf[:, b, c * P:(c + 1) * P, :].bitcast(F32), turned[:].rearrange("p u e -> p e u"))
 
-        turned_v1 = [turn_values(v_g1, b, "d%d" % b) for b in range(B)]
+        first_v1 = turn_values(v_g1[0][:], "d0")
 
         neg = sb.tile([P, B, N], F32)
-        clamped = arena.tile([P, B, N], F32, offset=49152)
+        clamped = arena.tile([P, B, N], F32, offset=51200)
         neg_max = [sb.tile([P, 1], F32, name="neg_max%d" % b) for b in range(B)]
         total = [sb.tile([P, 1], F32, name="total%d" % b) for b in range(B)]
-        prob = [arena.tile([P, PACK, P], F32, offset=off, name="prob%d" % b) for b, off in enumerate((6144, 20480))]
+        prob = [arena.tile([P, PACK, P], F32, offset=2048 + 2048 * b, name="prob%d" % b) for b in range(B)]
         turned_p = []
         for b in range(B):
             nc.vector.scalar_tensor_tensor(neg[:, b], pos_g[b][:], q_far[:, b:b + 1], scores[b][:], ALU.subtract, ALU.max)
@@ -174,13 +174,13 @@ def tile_attend_draft_kernel(tc, qT, k_words, k_scales, vT, vs, pos, qpos, offs,
                 nc.tensor.transpose(tp[:, t, :], prob[b][:, t, :], ident[:])
             turned_p.append(tp)
         v_bf = arena.tile([P, B, DV, PACK], BF16, align_bytes=64, offset=49152)
-        for b in range(B):
-            lay_values(1, b, turned_v1[b])
+        lay_values(1, 0, first_v1)
+        nc.scalar.activation(v_g1[1][:], v1_win[:].indirect(seq_offs[1]), ACT.Copy)
 
         v_g0 = arena.tile([P, B * N], BF16, offset=45056)
         nc.vector.tensor_copy(v_g0[:], v0_win[:].indirect(offs_t[:]))
-        for b in range(B):
-            lay_values(0, b, turn_values(v_g0, b, "d%d" % b))
+        lay_values(0, 0, turn_values(v_g0[:, 0:N], "d0"))
+        lay_values(1, 1, turn_values(v_g1[1][:], "d1"))
 
         w_bf = arena.tile([P, B, NQ, PACK], BF16, align_bytes=64, offset=12288)
         w_codes = sb.tile([P, B, NQ], U32, align_bytes=64)
@@ -192,6 +192,7 @@ def tile_attend_draft_kernel(tc, qT, k_words, k_scales, vT, vs, pos, qpos, offs,
         for b in range(B):
             nc.vector.tensor_tensor(w_bf[:, b], turned_p[b][:].rearrange("p t q -> p q t"),
                                     vs_col[b][:].unsqueeze(1).to_broadcast([P, NQ, PACK]), ALU.mult)
+        lay_values(0, 1, turn_values(v_g0[:, N:2 * N], "b0"))
         for b in range(B):
             nc.vector.reciprocal(inv[b][:], total[b][:])
         sums = []

@@ -102,11 +102,10 @@ def tile_attend_draft_kernel(tc, qT, k_words, k_scales, vT, vs, pos, qpos, offs,
         q_up = sb.tile([P, B], F32)
         nc.scalar.activation(q_up[:], qpos_t[:], ACT.Copy, scale=FAR * (1.0 + ULP))
 
-        kw_g = [arena.tile([P, N], U32, offset=32768, name="kw_g0"), sb.tile([P, N], U32, name="kw_g1")]
+        kw_g = [sb.tile([P, N], U32, name="kw_g%d" % b) for b in range(B)]
         for b in range(B):
             nc.vector.tensor_copy(kw_g[b][:], kw_win[:].bitcast(U32).indirect(seq_offs[b]))
-        keys = [sb.tile([P, PASSES, 2 * N], U8, align_bytes=64, name="keys0"),
-                arena.tile([P, PASSES, 2 * N], U8, align_bytes=64, offset=41984, name="keys1")]
+        keys = [sb.tile([P, PASSES, 2 * N], U8, align_bytes=64, name="keys%d" % b) for b in range(B)]
         q_scales = sb.tile([P, B * PASSES * NQ], U8, align_bytes=64)
         pos_g = [arena.tile([P, N], F32, offset=off, name="pos_g%d" % b) for b, off in enumerate((39936, 45056))]
         scores = []
@@ -118,7 +117,7 @@ def tile_attend_draft_kernel(tc, qT, k_words, k_scales, vT, vs, pos, qpos, offs,
             nc.vector.tensor_scalar(pos_g[b][:], pos_win[:].indirect(seq_offs[b]), FAR, -NEAR, ALU.mult, ALU.add)
 
         def score(b):
-            q_codes = arena.tile([P, PASSES * NQ], U32, align_bytes=64, offset=32768 + 1024 * b, name="q_codes%d" % b)
+            q_codes = sb.tile([P, PASSES * NQ], U32, align_bytes=64, name="q_codes%d" % b)
             cols = slice(b * PASSES * NQ, (b + 1) * PASSES * NQ)
             nc.vector.quantize_mx(q_codes[:].bitcast(FP8X4), q_scales[:, cols],
                                   q_bf[b][:].rearrange("p g q j -> p (g q j)"))
@@ -132,6 +131,7 @@ def tile_attend_draft_kernel(tc, qT, k_words, k_scales, vT, vs, pos, qpos, offs,
 
         for b in range(B):
             split(b)
+        for b in range(B):
             score(b)
         q_far = sb.tile([P, B], F32)
         nc.vector.scalar_tensor_tensor(q_far[:], qpos_t[:], FAR * (1.0 - ULP), q_up[:], ALU.mult, ALU.max)
@@ -152,15 +152,15 @@ def tile_attend_draft_kernel(tc, qT, k_words, k_scales, vT, vs, pos, qpos, offs,
                 nc.tensor.transpose(turned[:, u, :], words[:, u:N // 2:2], ident[:])
             return turned
 
-        def lay_values(c, b, turned):
-            nc.scalar.copy(v_bf[:, b, c * P:(c + 1) * P, :].bitcast(F32), turned[:].rearrange("p u e -> p e u"))
+        def lay_values(laid, turned):
+            nc.scalar.copy(laid.bitcast(F32), turned[:].rearrange("p u e -> p e u"))
 
         first_v1 = turn_values(v_g1[0][:], "d0")
 
         neg = sb.tile([P, B, N], F32)
         clamped = arena.tile([P, B, N], F32, offset=51200)
         neg_max = [sb.tile([P, 1], F32, name="neg_max%d" % b) for b in range(B)]
-        total = [sb.tile([P, 1], F32, name="total%d" % b) for b in range(B)]
+        total = sb.tile([P, B], F32)
         prob = [arena.tile([P, PACK, P], F32, offset=2048 + 2048 * b, name="prob%d" % b) for b in range(B)]
         turned_p = []
         for b in range(B):
@@ -168,45 +168,53 @@ def tile_attend_draft_kernel(tc, qT, k_words, k_scales, vT, vs, pos, qpos, offs,
         for b in range(B):
             nc.vector.tensor_scalar(clamped[:, b], neg[:, b], MASKED, None, ALU.min, ALU.min, accum_out=neg_max[b][:])
             nc.scalar.activation(prob[b][:].rearrange("q t s -> q s t"), clamped[:, b].rearrange("q (s t) -> q s t", t=PACK),
-                                 ACT.Exp, bias=neg_max[b][:], scale=-1.0, accum_out=total[b][:])
+                                 ACT.Exp, bias=neg_max[b][:], scale=-1.0, accum_out=total[:, b:b + 1])
             tp = bank("b%d" % b, [P, PACK, NQ])
             for t in range(PACK):
                 nc.tensor.transpose(tp[:, t, :], prob[b][:, t, :], ident[:])
             turned_p.append(tp)
-        v_bf = arena.tile([P, B, DV, PACK], BF16, align_bytes=64, offset=49152)
-        lay_values(1, 0, first_v1)
+        v_bf0 = arena.tile([P, DV, PACK], BF16, align_bytes=64, offset=51200)
+        v_bf11 = sb.tile([P, P, PACK], BF16, align_bytes=64)
+        v_bf01 = sb.tile([P, P, PACK], BF16, align_bytes=64)
+        lay_values(v_bf0[:, P:DV, :], first_v1)
         nc.scalar.activation(v_g1[1][:], v1_win[:].indirect(seq_offs[1]), ACT.Copy)
 
         v_g0 = arena.tile([P, B * N], BF16, offset=45056)
         nc.vector.tensor_copy(v_g0[:], v0_win[:].indirect(offs_t[:]))
-        lay_values(0, 0, turn_values(v_g0[:, 0:N], "d0"))
-        lay_values(1, 1, turn_values(v_g1[1][:], "d1"))
+        lay_values(v_bf0[:, 0:P, :], turn_values(v_g0[:, 0:N], "d0"))
+        lay_values(v_bf11[:], turn_values(v_g1[1][:], "d1"))
 
-        w_bf = arena.tile([P, B, NQ, PACK], BF16, align_bytes=64, offset=12288)
-        w_codes = sb.tile([P, B, NQ], U32, align_bytes=64)
-        w_scales = sb.tile([P, B, NQ], U8, align_bytes=64)
-        v_codes = arena.tile([P, B, DV], U32, align_bytes=64, offset=36864)
-        v_scales = sb.tile([P, B, DV], U8, align_bytes=64)
-        inv = [arena.tile([P, 1], F32, offset=16384 + 32 * b, name="inv%d" % b) for b in range(B)]
-        y = sb.tile([P, B, DV], F32)
+        w_bf = [arena.tile([P, NQ, PACK], BF16, align_bytes=64, offset=12288 + 1024 * b, name="w_bf%d" % b)
+                for b in range(B)]
         for b in range(B):
-            nc.vector.tensor_tensor(w_bf[:, b], turned_p[b][:].rearrange("p t q -> p q t"),
+            nc.vector.tensor_tensor(w_bf[b][:], turned_p[b][:].rearrange("p t q -> p q t"),
                                     vs_col[b][:].unsqueeze(1).to_broadcast([P, NQ, PACK]), ALU.mult)
-        lay_values(0, 1, turn_values(v_g0[:, N:2 * N], "b0"))
-        for b in range(B):
-            nc.vector.reciprocal(inv[b][:], total[b][:])
-        sums = []
-        for b in range(B):
-            nc.vector.quantize_mx(w_codes[:, b, :].bitcast(FP8X4), w_scales[:, b, :],
-                                  w_bf[:, b].rearrange("p q t -> p (q t)"))
-            nc.vector.quantize_mx(v_codes[:, b, :].bitcast(FP8X4), v_scales[:, b, :],
-                                  v_bf[:, b].rearrange("p e t -> p (e t)"))
-            acc = bank("c%d" % b, [P, DV])
-            nc.tensor.matmul_mx(acc[:], lhsT=w_codes[:, b, :].bitcast(FP8X4), lhsT_scale=w_scales[:, b, :],
-                                rhs=v_codes[:, b, :].bitcast(FP8X4), rhs_scale=v_scales[:, b, :],
-                                start=True, stop=True)
-            sums.append(acc)
-        nc.scalar.activation(y[:, 0, :], sums[0][:], ACT.Copy, scale=inv[0][:])
-        nc.sync.dma_start(out[0], y[:, 0, :])
-        nc.vector.tensor_scalar(y[:, 1, :], sums[1][:], inv[1][:], None, ALU.mult)
-        nc.sync.dma_start(out[1], y[:, 1, :])
+        lay_values(v_bf01[:], turn_values(v_g0[:, N:2 * N], "b0"))
+
+        def quantise(name, laid, offset=None):
+            width = laid.shape[1]
+            pool = sb if offset is None else arena
+            codes = pool.tile([P, width], U32, align_bytes=64, offset=offset, name=name + "_codes")
+            scales = sb.tile([P, width], U8, align_bytes=64, name=name + "_scales")
+            nc.vector.quantize_mx(codes[:].bitcast(FP8X4), scales[:], laid[:].rearrange("p c t -> p (c t)"))
+            return codes, scales
+
+        def product(weights, values, tag):
+            acc = bank(tag, [P, values[0].shape[1]])
+            nc.tensor.matmul_mx(acc[:], lhsT=weights[0][:].bitcast(FP8X4), lhsT_scale=weights[1][:],
+                                rhs=values[0][:].bitcast(FP8X4), rhs_scale=values[1][:], start=True, stop=True)
+            return acc
+
+        w0 = quantise("w0", w_bf[0])
+        sum0 = product(w0, quantise("v0", v_bf0, 37888), "c0")
+        inv = arena.tile([P, B], F32, offset=16384)
+        nc.vector.reciprocal(inv[:], total[:])
+        w1 = quantise("w1", w_bf[1])
+        sum11 = product(w1, quantise("v11", v_bf11, 36864), "c1")
+        sum01 = product(w1, quantise("v01", v_bf01), "a1")
+        y = [arena.tile([P, DV], F32, offset=45056, name="y0"), sb.tile([P, DV], F32, name="y1")]
+        nc.scalar.activation(y[0][:], sum0[:], ACT.Copy, scale=inv[:, 0:1])
+        nc.sync.dma_start(out[0], y[0][:])
+        nc.scalar.activation(y[1][:, P:DV], sum11[:], ACT.Copy, scale=inv[:, 1:2])
+        nc.vector.tensor_scalar(y[1][:, 0:P], sum01[:], inv[:, 1:2], None, ALU.mult)
+        nc.sync.dma_start(out[1], y[1][:])

@@ -97,8 +97,9 @@ def tile_attend_draft_kernel(tc, qT, k_words, k_scales, vT, vs, pos, qpos, offs,
         q_bf = [arena.tile([P, PASSES, NQ, PACK], BF16, align_bytes=64, offset=40960 + 4096 * b, name="q_bf%d" % b)
                 for b in range(B)]
         for b in range(B):
-            nc.scalar.activation(q_bf[b][:],
-                                 q_raw[b][:].rearrange("p g (j q) -> p g q j", j=PACK), ACT.Copy, scale=-1.0)
+            for g in range(PASSES):
+                nc.scalar.activation(q_bf[b][:, g].rearrange("p (c i) j -> p c j i", i=PACK),
+                                     q_raw[b][:, g].rearrange("p (j c i) -> p c j i", j=PACK, i=PACK), ACT.Copy, scale=-1.0)
         q_up = sb.tile([P, B], F32)
         nc.scalar.activation(q_up[:], qpos_t[:], ACT.Copy, scale=FAR * (1.0 + ULP))
 
@@ -142,14 +143,18 @@ def tile_attend_draft_kernel(tc, qT, k_words, k_scales, vT, vs, pos, qpos, offs,
         for h in range(2):
             nc.scalar.activation(v1_win[:, h * 1024:(h + 1) * 1024], v1_raw[:, h * 1024:(h + 1) * 1024], ACT.Copy)
         v_g1 = [sb.tile([P, N], BF16, name="v_g10"), arena.tile([P, N], BF16, offset=53248, name="v_g11")]
-        nc.scalar.activation(v_g1[0][:], v1_win[:].indirect(seq_offs[0]), ACT.Copy)
+
+        def dealt(gathered):
+            return gathered.rearrange("f (u p e) -> f p u e", u=2, e=2)
+
+        nc.scalar.activation(dealt(v_g1[0][:]), v1_win[:].indirect(seq_offs[0]), ACT.Copy)
 
 
         def turn_values(gathered, tag):
             words = gathered.bitcast(F32)
             turned = bank(tag, [P, 2, P])
             for u in range(2):
-                nc.tensor.transpose(turned[:, u, :], words[:, u:N // 2:2], ident[:])
+                nc.tensor.transpose(turned[:, u, :], words[:, u * P:(u + 1) * P], ident[:])
             return turned
 
         def lay_values(laid, turned):
@@ -177,10 +182,10 @@ def tile_attend_draft_kernel(tc, qT, k_words, k_scales, vT, vs, pos, qpos, offs,
         v_bf11 = sb.tile([P, P, PACK], BF16, align_bytes=64)
         v_bf01 = sb.tile([P, P, PACK], BF16, align_bytes=64)
         lay_values(v_bf0[:, P:DV, :], first_v1)
-        nc.scalar.activation(v_g1[1][:], v1_win[:].indirect(seq_offs[1]), ACT.Copy)
+        nc.scalar.activation(dealt(v_g1[1][:]), v1_win[:].indirect(seq_offs[1]), ACT.Copy)
 
         v_g0 = arena.tile([P, B * N], BF16, offset=45056)
-        nc.vector.tensor_copy(v_g0[:], v0_win[:].indirect(offs_t[:]))
+        nc.vector.tensor_copy(v_g0[:].rearrange("f (b u p e) -> f b p u e", b=B, u=2, e=2), v0_win[:].indirect(offs_t[:]))
         lay_values(v_bf0[:, 0:P, :], turn_values(v_g0[:, 0:N], "d0"))
         lay_values(v_bf11[:], turn_values(v_g1[1][:], "d1"))
 

@@ -26,6 +26,8 @@ FAR = float(2 ** 60)
 ULP = float(2 ** -23)
 NEAR = float(2 ** 30)
 ROW = P - 1
+HEAD = 512
+PIECE = (T - HEAD) // 2
 
 
 def tile_attend_draft_kernel(tc, qT, k_words, k_scales, vT, vs, pos, qpos, offs, out):
@@ -56,19 +58,22 @@ def tile_attend_draft_kernel(tc, qT, k_words, k_scales, vT, vs, pos, qpos, offs,
         for r in range(4):
             nc.sync.dma_start(ks_win[r:P:16, :], ks_rows[r:16:4, :, :])
         nc.sync.dma_start(kw_win[:, T // 2:T], kw_rows[:, T // 2:T])
+        q_rows = sb.tile([P, NQ], F32)
+        nc.sync.dma_start(q_rows[P - B:P, :], qpos.rearrange("b q o -> b (q o)"))
         nc.vector.memset(vs_win[0:ROW, :], 0.0)
         ks_low = sb.tile([P, B * N // 4], I32, align_bytes=64)
         nc.vector.memset(ks_low[96:P, :], 0)
-        q_raw = [sb.tile([P, PASSES, PACK * NQ], F32, name="q_raw%d" % b) for b in range(B)]
+        q_raw = [[arena.tile([P, PACK * NQ], F32, offset=57344 + 2048 * (PASSES * b + g), name="q_raw%d%d" % (b, g))
+                  for g in range(PASSES)] for b in range(B)]
         for b in range(B):
-            nc.sync.dma_start(q_raw[b][:], qT[b].rearrange("(o p j) q -> p o (j q)", p=P, j=PACK))
-        qpos_t = sb.tile([P, B], F32)
-        with nc.allow_non_contiguous_dma(reason="one place a query row"):
-            nc.sync.dma_start(qpos_t[:], qpos.rearrange("b q o -> q (b o)"))
-
+            for g in range(PASSES):
+                nc.sync.dma_start(q_raw[b][g][:], qT[b].rearrange("(o p j) q -> o p (j q)", p=P, j=PACK)[g])
+        v1_head = sb.tile([P, HEAD], F32)
+        nc.sync.dma_start(v1_head[:], vT[P:2 * P, 0:HEAD])
 
         ident = sb.tile([P, P], F32)
         make_identity(nc, ident[:])
+        nc.gpsimd.memset(q_rows[0:P - B, :], 0.0)
         pos_win = sb.tile([P, T], F32)
         for a, tag in enumerate(("a0", "a1", "b0", "b1")):
             spread = bank(tag, [P, PACK, P])
@@ -77,6 +82,8 @@ def tile_attend_draft_kernel(tc, qT, k_words, k_scales, vT, vs, pos, qpos, offs,
                                     ident[:])
             nc.scalar.activation(pos_win[:].rearrange("q (n j) -> q n j", j=T // P)[:, :, PACK * a:PACK * (a + 1)],
                                  spread[:].rearrange("q j n -> q n j"), ACT.Copy)
+        q_turned = bank("c0", [P, P])
+        nc.tensor.transpose(q_turned[:], q_rows[:], ident[:])
 
         vs_g = sb.tile([P, B * N], F32)
         nc.vector.tensor_copy(vs_g[:], vs_win[:].indirect(offs_t[:]))
@@ -84,9 +91,10 @@ def tile_attend_draft_kernel(tc, qT, k_words, k_scales, vT, vs, pos, qpos, offs,
         nc.vector.tensor_copy(ks_g[:], ks_win[:].bitcast(U8).indirect(offs_t[:]))
         for lo, hi in ((0, 64), (64, 96), (96, 112)):
             nc.sync.dma_start(ks_low[lo:hi, :], ks_g[lo + 16:hi + 16, :].bitcast(I32))
-        v1_raw = arena.tile([P, T], F32, offset=1024)
+        v1_rest = arena.tile([P, 2 * PIECE], F32, offset=3072)
         for h in range(2):
-            nc.sync.dma_start(v1_raw[:, h * T // 2:(h + 1) * T // 2], vT[P:2 * P, h * T // 2:(h + 1) * T // 2])
+            nc.sync.dma_start(v1_rest[:, h * PIECE:(h + 1) * PIECE],
+                              vT[P:2 * P, HEAD + h * PIECE:HEAD + (h + 1) * PIECE])
         v0_win = arena.tile([P, T], F32, offset=9216)
         nc.sync.dma_start(v0_win[:], vT[0:P, :])
         ks_plane = [ks_g[:], ks_low[:].bitcast(U8)]
@@ -99,9 +107,13 @@ def tile_attend_draft_kernel(tc, qT, k_words, k_scales, vT, vs, pos, qpos, offs,
         for b in range(B):
             for g in range(PASSES):
                 nc.scalar.activation(q_bf[b][:, g].rearrange("p (c i) j -> p c j i", i=PACK),
-                                     q_raw[b][:, g].rearrange("p (j c i) -> p c j i", j=PACK, i=PACK), ACT.Copy, scale=-1.0)
-        q_up = sb.tile([P, B], F32)
-        nc.scalar.activation(q_up[:], qpos_t[:], ACT.Copy, scale=FAR * (1.0 + ULP))
+                                     q_raw[b][g][:].rearrange("p (j c i) -> p c j i", j=PACK, i=PACK), ACT.Copy, scale=-1.0)
+        q_step = arena.tile([P, B], F32, offset=63488)
+        nc.scalar.activation(q_step[:], q_turned[:, P - B:P], ACT.Abs, scale=FAR * ULP)
+        q_far = sb.tile([P, B], F32)
+        for b in range(B):
+            nc.scalar.activation(q_far[:, b:b + 1], q_turned[:, P - B + b:P - B + b + 1], ACT.Identity,
+                                 bias=q_step[:, b:b + 1], scale=FAR)
 
         kw_g = [sb.tile([P, N], U32, name="kw_g%d" % b) for b in range(B)]
         for b in range(B):
@@ -134,14 +146,14 @@ def tile_attend_draft_kernel(tc, qT, k_words, k_scales, vT, vs, pos, qpos, offs,
             split(b)
         for b in range(B):
             score(b)
-        q_far = sb.tile([P, B], F32)
-        nc.vector.scalar_tensor_tensor(q_far[:], qpos_t[:], FAR * (1.0 - ULP), q_up[:], ALU.mult, ALU.max)
         for b in range(B):
             places(b)
 
         v1_win = arena.tile([P, T], BF16, offset=20480)
+        nc.scalar.activation(v1_win[:, 0:HEAD], v1_head[:], ACT.Copy)
         for h in range(2):
-            nc.scalar.activation(v1_win[:, h * 1024:(h + 1) * 1024], v1_raw[:, h * 1024:(h + 1) * 1024], ACT.Copy)
+            nc.scalar.activation(v1_win[:, HEAD + h * PIECE:HEAD + (h + 1) * PIECE],
+                                 v1_rest[:, h * PIECE:(h + 1) * PIECE], ACT.Copy)
         v_g1 = [sb.tile([P, N], BF16, name="v_g10"), arena.tile([P, N], BF16, offset=53248, name="v_g11")]
 
         def dealt(gathered):
@@ -170,7 +182,6 @@ def tile_attend_draft_kernel(tc, qT, k_words, k_scales, vT, vs, pos, qpos, offs,
         turned_p = []
         for b in range(B):
             nc.vector.scalar_tensor_tensor(neg[:, b], pos_g[b][:], q_far[:, b:b + 1], scores[b][:], ALU.subtract, ALU.max)
-        for b in range(B):
             nc.vector.tensor_scalar(clamped[:, b], neg[:, b], MASKED, None, ALU.min, ALU.min, accum_out=neg_max[b][:])
             nc.scalar.activation(prob[b][:].rearrange("q t s -> q s t"), clamped[:, b].rearrange("q (s t) -> q s t", t=PACK),
                                  ACT.Exp, bias=neg_max[b][:], scale=-1.0, accum_out=total[:, b:b + 1])
@@ -181,20 +192,20 @@ def tile_attend_draft_kernel(tc, qT, k_words, k_scales, vT, vs, pos, qpos, offs,
         v_bf0 = arena.tile([P, DV, PACK], BF16, align_bytes=64, offset=51200)
         v_bf11 = sb.tile([P, P, PACK], BF16, align_bytes=64)
         v_bf01 = sb.tile([P, P, PACK], BF16, align_bytes=64)
-        lay_values(v_bf0[:, P:DV, :], first_v1)
         nc.scalar.activation(dealt(v_g1[1][:]), v1_win[:].indirect(seq_offs[1]), ACT.Copy)
+        lay_values(v_bf0[:, P:DV, :], first_v1)
 
-        v_g0 = arena.tile([P, B * N], BF16, offset=45056)
-        nc.vector.tensor_copy(v_g0[:].rearrange("f (b u p e) -> f b p u e", b=B, u=2, e=2), v0_win[:].indirect(offs_t[:]))
-        lay_values(v_bf0[:, 0:P, :], turn_values(v_g0[:, 0:N], "d0"))
-        lay_values(v_bf11[:], turn_values(v_g1[1][:], "d1"))
+        v_g0 = [arena.tile([P, N], BF16, offset=45056 + 1024 * b, name="v_g0%d" % b) for b in range(B)]
+        for b in range(B):
+            nc.vector.tensor_copy(dealt(v_g0[b][:]), v0_win[:].indirect(seq_offs[b]))
+        lay_values(v_bf0[:, 0:P, :], turn_values(v_g0[0][:], "d1"))
 
         w_bf = [arena.tile([P, NQ, PACK], BF16, align_bytes=64, offset=12288 + 1024 * b, name="w_bf%d" % b)
                 for b in range(B)]
-        for b in range(B):
+
+        def weigh(b):
             nc.vector.tensor_tensor(w_bf[b][:], turned_p[b][:].rearrange("p t q -> p q t"),
                                     vs_col[b][:].unsqueeze(1).to_broadcast([P, NQ, PACK]), ALU.mult)
-        lay_values(v_bf01[:], turn_values(v_g0[:, N:2 * N], "b0"))
 
         def quantise(name, laid, offset=None):
             width = laid.shape[1]
@@ -210,16 +221,20 @@ def tile_attend_draft_kernel(tc, qT, k_words, k_scales, vT, vs, pos, qpos, offs,
                                 rhs=values[0][:].bitcast(FP8X4), rhs_scale=values[1][:], start=True, stop=True)
             return acc
 
-        w0 = quantise("w0", w_bf[0])
-        sum0 = product(w0, quantise("v0", v_bf0, 37888), "c0")
+        weigh(0)
+        lay_values(v_bf01[:], turn_values(v_g0[1][:], "b0"))
+        lay_values(v_bf11[:], turn_values(v_g1[1][:], "d0"))
         inv = arena.tile([P, B], F32, offset=16384)
         nc.vector.reciprocal(inv[:], total[:])
+        w0 = quantise("w0", w_bf[0])
+        weigh(1)
+        sum0 = product(w0, quantise("v0", v_bf0, 37888), "c0")
         w1 = quantise("w1", w_bf[1])
-        sum11 = product(w1, quantise("v11", v_bf11, 36864), "c1")
         sum01 = product(w1, quantise("v01", v_bf01), "a1")
-        y = [arena.tile([P, DV], F32, offset=45056, name="y0"), sb.tile([P, DV], F32, name="y1")]
+        sum11 = product(w1, quantise("v11", v_bf11), "c1")
+        y = [arena.tile([P, DV], F32, offset=46080, name="y0"), sb.tile([P, DV], F32, name="y1")]
         nc.scalar.activation(y[0][:], sum0[:], ACT.Copy, scale=inv[:, 0:1])
         nc.sync.dma_start(out[0], y[0][:])
-        nc.scalar.activation(y[1][:, P:DV], sum11[:], ACT.Copy, scale=inv[:, 1:2])
-        nc.vector.tensor_scalar(y[1][:, 0:P], sum01[:], inv[:, 1:2], None, ALU.mult)
+        nc.scalar.activation(y[1][:, 0:P], sum01[:], ACT.Copy, scale=inv[:, 1:2])
+        nc.vector.tensor_scalar(y[1][:, P:DV], sum11[:], inv[:, 1:2], None, ALU.mult)
         nc.sync.dma_start(out[1], y[1][:])

@@ -21,13 +21,9 @@ P = 128
 PACK = 4
 PASSES = D // (P * PACK)
 COLS = N // 16
-MASKED = 30000.0
-FAR = float(2 ** 60)
-ULP = float(2 ** -23)
-NEAR = float(2 ** 30)
+FAR = float(2 ** 40)
 ROW = P - 1
-HEAD = 512
-PIECE = (T - HEAD) // 2
+PIECES = ((0, 512), (512, 1280), (1280, T))
 
 
 def tile_attend_draft_kernel(tc, qT, k_words, k_scales, vT, vs, pos, qpos, offs, out):
@@ -46,18 +42,16 @@ def tile_attend_draft_kernel(tc, qT, k_words, k_scales, vT, vs, pos, qpos, offs,
         seq_offs = [offs_t[:, b * COLS:(b + 1) * COLS] for b in range(B)]
 
         ks_win = arena.tile([P, T // 4], I32, offset=8192)
-        nc.vector.memset(ks_win[:], 0)
-        vs_win = sb.tile([P, T], F32)
-        nc.sync.dma_start(vs_win[ROW:P, :], vs[0:1, :])
+        nc.gpsimd.memset(ks_win[:], 0)
         pos_cols = sb.tile([P, T // P], F32)
         nc.sync.dma_start(pos_cols[:], pos[0].rearrange("(p j) -> p j", p=P))
-        kw_win = arena.tile([P, T], I32, offset=24576)
-        kw_rows = k_words[0].rearrange("p t c -> p (t c)").bitcast(I32)
-        nc.sync.dma_start(kw_win[:, 0:T // 2], kw_rows[:, 0:T // 2])
+        vs_win = sb.tile([P, T], F32)
+        nc.sync.dma_start(vs_win[ROW:P, :], vs[0:1, :])
         ks_rows = k_scales.bitcast(I32).rearrange("o f t -> f o t")
         for r in range(4):
             nc.sync.dma_start(ks_win[r:P:16, :], ks_rows[r:16:4, :, :])
-        nc.sync.dma_start(kw_win[:, T // 2:T], kw_rows[:, T // 2:T])
+        kw_win = arena.tile([P, T], I32, offset=24576)
+        nc.sync.dma_start(kw_win[:], k_words[0].rearrange("p t c -> p (t c)").bitcast(I32))
         q_rows = sb.tile([P, NQ], F32)
         nc.sync.dma_start(q_rows[P - B:P, :], qpos.rearrange("b q o -> b (q o)"))
         nc.vector.memset(vs_win[0:ROW, :], 0.0)
@@ -68,8 +62,6 @@ def tile_attend_draft_kernel(tc, qT, k_words, k_scales, vT, vs, pos, qpos, offs,
         for b in range(B):
             for g in range(PASSES):
                 nc.sync.dma_start(q_raw[b][g][:], qT[b].rearrange("(o p j) q -> o p (j q)", p=P, j=PACK)[g])
-        v1_head = sb.tile([P, HEAD], F32)
-        nc.sync.dma_start(v1_head[:], vT[P:2 * P, 0:HEAD])
 
         ident = sb.tile([P, P], F32)
         make_identity(nc, ident[:])
@@ -91,10 +83,9 @@ def tile_attend_draft_kernel(tc, qT, k_words, k_scales, vT, vs, pos, qpos, offs,
         nc.vector.tensor_copy(ks_g[:], ks_win[:].bitcast(U8).indirect(offs_t[:]))
         for lo, hi in ((0, 64), (64, 96), (96, 112)):
             nc.sync.dma_start(ks_low[lo:hi, :], ks_g[lo + 16:hi + 16, :].bitcast(I32))
-        v1_rest = arena.tile([P, 2 * PIECE], F32, offset=3072)
-        for h in range(2):
-            nc.sync.dma_start(v1_rest[:, h * PIECE:(h + 1) * PIECE],
-                              vT[P:2 * P, HEAD + h * PIECE:HEAD + (h + 1) * PIECE])
+        v1_raw = arena.tile([P, T], F32, offset=1024)
+        for lo, hi in PIECES:
+            nc.sync.dma_start(v1_raw[:, lo:hi], vT[P:2 * P, lo:hi])
         v0_win = arena.tile([P, T], F32, offset=9216)
         nc.sync.dma_start(v0_win[:], vT[0:P, :])
         ks_plane = [ks_g[:], ks_low[:].bitcast(U8)]
@@ -107,13 +98,7 @@ def tile_attend_draft_kernel(tc, qT, k_words, k_scales, vT, vs, pos, qpos, offs,
         for b in range(B):
             for g in range(PASSES):
                 nc.scalar.activation(q_bf[b][:, g].rearrange("p (c i) j -> p c j i", i=PACK),
-                                     q_raw[b][g][:].rearrange("p (j c i) -> p c j i", j=PACK, i=PACK), ACT.Copy, scale=-1.0)
-        q_step = arena.tile([P, B], F32, offset=63488)
-        nc.scalar.activation(q_step[:], q_turned[:, P - B:P], ACT.Abs, scale=FAR * ULP)
-        q_far = sb.tile([P, B], F32)
-        for b in range(B):
-            nc.scalar.activation(q_far[:, b:b + 1], q_turned[:, P - B + b:P - B + b + 1], ACT.Identity,
-                                 bias=q_step[:, b:b + 1], scale=FAR)
+                                     q_raw[b][g][:].rearrange("p (j c i) -> p c j i", j=PACK, i=PACK), ACT.Copy, scale=-1.0 / FAR)
 
         kw_g = [sb.tile([P, N], U32, name="kw_g%d" % b) for b in range(B)]
         for b in range(B):
@@ -127,7 +112,7 @@ def tile_attend_draft_kernel(tc, qT, k_words, k_scales, vT, vs, pos, qpos, offs,
             nc.vector.tensor_copy(keys[b][:].bitcast(U16), kw_g[b][:].bitcast(U16).rearrange("p (n o) -> p o n", o=PASSES))
 
         def places(b):
-            nc.vector.tensor_scalar(pos_g[b][:], pos_win[:].indirect(seq_offs[b]), FAR, -NEAR, ALU.mult, ALU.add)
+            nc.vector.tensor_copy(pos_g[b][:], pos_win[:].indirect(seq_offs[b]))
 
         def score(b):
             q_codes = sb.tile([P, PASSES * NQ], U32, align_bytes=64, name="q_codes%d" % b)
@@ -150,10 +135,8 @@ def tile_attend_draft_kernel(tc, qT, k_words, k_scales, vT, vs, pos, qpos, offs,
             places(b)
 
         v1_win = arena.tile([P, T], BF16, offset=20480)
-        nc.scalar.activation(v1_win[:, 0:HEAD], v1_head[:], ACT.Copy)
-        for h in range(2):
-            nc.scalar.activation(v1_win[:, HEAD + h * PIECE:HEAD + (h + 1) * PIECE],
-                                 v1_rest[:, h * PIECE:(h + 1) * PIECE], ACT.Copy)
+        for lo, hi in PIECES:
+            nc.scalar.activation(v1_win[:, lo:hi], v1_raw[:, lo:hi], ACT.Copy)
         v_g1 = [sb.tile([P, N], BF16, name="v_g10"), arena.tile([P, N], BF16, offset=53248, name="v_g11")]
 
         def dealt(gathered):
@@ -181,8 +164,9 @@ def tile_attend_draft_kernel(tc, qT, k_words, k_scales, vT, vs, pos, qpos, offs,
         prob = [arena.tile([P, PACK, P], F32, offset=2048 + 2048 * b, name="prob%d" % b) for b in range(B)]
         turned_p = []
         for b in range(B):
-            nc.vector.scalar_tensor_tensor(neg[:, b], pos_g[b][:], q_far[:, b:b + 1], scores[b][:], ALU.subtract, ALU.max)
-            nc.vector.tensor_scalar(clamped[:, b], neg[:, b], MASKED, None, ALU.min, ALU.min, accum_out=neg_max[b][:])
+            nc.vector.scalar_tensor_tensor(neg[:, b], pos_g[b][:], q_turned[:, P - B + b:P - B + b + 1],
+                                           scores[b][:], ALU.is_gt, ALU.add)
+            nc.vector.tensor_scalar(clamped[:, b], neg[:, b], FAR, None, ALU.mult, ALU.min, accum_out=neg_max[b][:])
             nc.scalar.activation(prob[b][:].rearrange("q t s -> q s t"), clamped[:, b].rearrange("q (s t) -> q s t", t=PACK),
                                  ACT.Exp, bias=neg_max[b][:], scale=-1.0, accum_out=total[:, b:b + 1])
             tp = bank("b%d" % b, [P, PACK, NQ])

@@ -23,7 +23,25 @@ PASSES = D // (P * PACK)
 COLS = N // 16
 FAR = float(2 ** 40)
 ROW = P - 1
-PIECES = ((0, 512), (512, 1280), (1280, T))
+SHIFT = 16
+PIECES = ((0, 768), (768, 1536), (1536, T))
+
+AT_KEY_SCALES = 8192
+AT_UPPER_RAW = AT_KEY_SCALES + 1024 - 4 * T
+AT_LOWER_WIN = AT_KEY_SCALES + 1024
+AT_PROB = 2048
+AT_UPPER_WIN = 20480
+AT_KEY_WORDS = 24576
+AT_SCALE_COLS = 36864
+AT_INV = AT_SCALE_COLS + 1024
+AT_QUERIES = 40960
+AT_PLACES = (AT_QUERIES - 1024, AT_QUERIES + 4096)
+AT_LOWER_G = AT_PLACES[1]
+AT_Y0 = AT_LOWER_G + 1024
+AT_MASKED = 51200
+AT_LAID0 = AT_MASKED
+AT_UPPER_G1 = AT_MASKED + 2048
+AT_RAW_QUERIES = 57344
 
 
 def tile_attend_draft_kernel(tc, qT, k_words, k_scales, vT, vs, pos, qpos, offs, out):
@@ -41,7 +59,7 @@ def tile_attend_draft_kernel(tc, qT, k_words, k_scales, vT, vs, pos, qpos, offs,
         nc.sync.dma_start(offs_t[:], offs)
         seq_offs = [offs_t[:, b * COLS:(b + 1) * COLS] for b in range(B)]
 
-        ks_win = arena.tile([P, T // 4], I32, offset=8192)
+        ks_win = arena.tile([P, T // 4], I32, offset=AT_KEY_SCALES)
         nc.gpsimd.memset(ks_win[:], 0)
         pos_cols = sb.tile([P, T // P], F32)
         nc.sync.dma_start(pos_cols[:], pos[0].rearrange("(p j) -> p j", p=P))
@@ -49,19 +67,19 @@ def tile_attend_draft_kernel(tc, qT, k_words, k_scales, vT, vs, pos, qpos, offs,
         nc.sync.dma_start(vs_win[ROW:P, :], vs[0:1, :])
         ks_rows = k_scales.bitcast(I32).rearrange("o f t -> f o t")
         for r in range(4):
-            nc.sync.dma_start(ks_win[r:P:16, :], ks_rows[r:16:4, :, :])
-        kw_win = arena.tile([P, T], I32, offset=24576)
+            nc.sync.dma_start(ks_win[r:P:SHIFT, :], ks_rows[r:16:4, :, :])
+        kw_win = arena.tile([P, T], I32, offset=AT_KEY_WORDS)
         nc.sync.dma_start(kw_win[:], k_words[0].rearrange("p t c -> p (t c)").bitcast(I32))
         q_rows = sb.tile([P, NQ], F32)
         nc.sync.dma_start(q_rows[P - B:P, :], qpos.rearrange("b q o -> b (q o)"))
         nc.vector.memset(vs_win[0:ROW, :], 0.0)
         ks_low = sb.tile([P, B * N // 4], I32, align_bytes=64)
         nc.vector.memset(ks_low[96:P, :], 0)
-        q_raw = [[arena.tile([P, PACK * NQ], F32, offset=57344 + 2048 * (PASSES * b + g), name="q_raw%d%d" % (b, g))
-                  for g in range(PASSES)] for b in range(B)]
+        q_raw = [[arena.tile([P, PACK * NQ], F32, offset=AT_RAW_QUERIES + 2048 * (PASSES * b + g),
+                             name="q_raw%d%d" % (b, g)) for g in range(PASSES)] for b in range(B)]
         for b in range(B):
             for g in range(PASSES):
-                nc.sync.dma_start(q_raw[b][g][:], qT[b].rearrange("(o p j) q -> o p (j q)", p=P, j=PACK)[g])
+                nc.sync.dma_start(q_raw[b][g][:], qT[b].rearrange("(g p j) q -> g p (j q)", p=P, j=PACK)[g])
 
         ident = sb.tile([P, P], F32)
         make_identity(nc, ident[:])
@@ -74,129 +92,122 @@ def tile_attend_draft_kernel(tc, qT, k_words, k_scales, vT, vs, pos, qpos, offs,
                                     ident[:])
             nc.scalar.activation(pos_win[:].rearrange("q (n j) -> q n j", j=T // P)[:, :, PACK * a:PACK * (a + 1)],
                                  spread[:].rearrange("q j n -> q n j"), ACT.Copy)
-        q_turned = bank("c0", [P, P])
-        nc.tensor.transpose(q_turned[:], q_rows[:], ident[:])
+        q_places = bank("c0", [P, P])
+        nc.tensor.transpose(q_places[:], q_rows[:], ident[:])
 
         vs_g = sb.tile([P, B * N], F32)
         nc.vector.tensor_copy(vs_g[:], vs_win[:].indirect(offs_t[:]))
         ks_g = sb.tile([P, B * N], U8, align_bytes=64)
         nc.vector.tensor_copy(ks_g[:], ks_win[:].bitcast(U8).indirect(offs_t[:]))
-        for lo, hi in ((0, 64), (64, 96), (96, 112)):
-            nc.sync.dma_start(ks_low[lo:hi, :], ks_g[lo + 16:hi + 16, :].bitcast(I32))
-        v1_raw = arena.tile([P, T], F32, offset=1024)
+        for lo, hi in ((0, 64), (64, 96), (96, P - SHIFT)):
+            nc.sync.dma_start(ks_low[lo:hi, :], ks_g[lo + SHIFT:hi + SHIFT, :].bitcast(I32))
+        upper_raw = arena.tile([P, T], F32, offset=AT_UPPER_RAW)
         for lo, hi in PIECES:
-            nc.sync.dma_start(v1_raw[:, lo:hi], vT[P:2 * P, lo:hi])
-        v0_win = arena.tile([P, T], F32, offset=9216)
-        nc.sync.dma_start(v0_win[:], vT[0:P, :])
-        ks_plane = [ks_g[:], ks_low[:].bitcast(U8)]
-        vs_col = [arena.tile([P, PACK], F32, offset=36864 + 1024 * b, name="vs_col%d" % b) for b in range(B)]
+            nc.sync.dma_start(upper_raw[:, lo:hi], vT[P:2 * P, lo:hi])
+        lower_win = arena.tile([P, T], F32, offset=AT_LOWER_WIN)
+        nc.sync.dma_start(lower_win[:], vT[0:P, :])
+        ks_pass = [ks_g[:], ks_low[:].bitcast(U8)]
+        vs_col = [arena.tile([P, PACK], F32, offset=AT_SCALE_COLS + 1024 * b, name="vs_col%d" % b) for b in range(B)]
         for b in range(B):
             nc.sync.dma_start(vs_col[b][:], vs_g[ROW:P, b * N:(b + 1) * N])
 
-        q_bf = [arena.tile([P, PASSES, NQ, PACK], BF16, align_bytes=64, offset=40960 + 4096 * b, name="q_bf%d" % b)
-                for b in range(B)]
+        q_bf = [arena.tile([P, PASSES, NQ, PACK], BF16, align_bytes=64, offset=AT_QUERIES + 4096 * b,
+                           name="q_bf%d" % b) for b in range(B)]
         for b in range(B):
             for g in range(PASSES):
                 nc.scalar.activation(q_bf[b][:, g].rearrange("p (c i) j -> p c j i", i=PACK),
-                                     q_raw[b][g][:].rearrange("p (j c i) -> p c j i", j=PACK, i=PACK), ACT.Copy, scale=-1.0 / FAR)
+                                     q_raw[b][g][:].rearrange("p (j c i) -> p c j i", j=PACK, i=PACK),
+                                     ACT.Copy, scale=-1.0 / FAR)
 
         kw_g = [sb.tile([P, N], U32, name="kw_g%d" % b) for b in range(B)]
         for b in range(B):
             nc.vector.tensor_copy(kw_g[b][:], kw_win[:].bitcast(U32).indirect(seq_offs[b]))
         keys = [sb.tile([P, PASSES, 2 * N], U8, align_bytes=64, name="keys%d" % b) for b in range(B)]
         q_scales = sb.tile([P, B * PASSES * NQ], U8, align_bytes=64)
-        pos_g = [arena.tile([P, N], F32, offset=off, name="pos_g%d" % b) for b, off in enumerate((39936, 45056))]
+        pos_g = [arena.tile([P, N], F32, offset=AT_PLACES[b], name="pos_g%d" % b) for b in range(B)]
+        for b in range(B):
+            nc.vector.tensor_copy(keys[b][:].bitcast(U16),
+                                  kw_g[b][:].bitcast(U16).rearrange("p (n g) -> p g n", g=PASSES))
+
         scores = []
-
-        def split(b):
-            nc.vector.tensor_copy(keys[b][:].bitcast(U16), kw_g[b][:].bitcast(U16).rearrange("p (n o) -> p o n", o=PASSES))
-
-        def places(b):
-            nc.vector.tensor_copy(pos_g[b][:], pos_win[:].indirect(seq_offs[b]))
-
-        def score(b):
+        for b in range(B):
             q_codes = sb.tile([P, PASSES * NQ], U32, align_bytes=64, name="q_codes%d" % b)
-            cols = slice(b * PASSES * NQ, (b + 1) * PASSES * NQ)
-            nc.vector.quantize_mx(q_codes[:].bitcast(FP8X4), q_scales[:, cols],
+            nc.vector.quantize_mx(q_codes[:].bitcast(FP8X4), q_scales[:, b * PASSES * NQ:(b + 1) * PASSES * NQ],
                                   q_bf[b][:].rearrange("p g q j -> p (g q j)"))
             acc = bank("a%d" % b, [P, N])
-            for o in range(PASSES):
-                qc = slice((b * PASSES + o) * NQ, (b * PASSES + o + 1) * NQ)
-                nc.tensor.matmul_mx(acc[:], lhsT=q_codes[:, o * NQ:(o + 1) * NQ].bitcast(FP8X4), lhsT_scale=q_scales[:, qc],
-                                    rhs=keys[b][:, o, :].bitcast(FP4X4), rhs_scale=ks_plane[o][:, b * N:(b + 1) * N],
-                                    start=(o == 0), stop=(o == PASSES - 1))
+            for g in range(PASSES):
+                first = (b * PASSES + g) * NQ
+                nc.tensor.matmul_mx(acc[:], lhsT=q_codes[:, g * NQ:(g + 1) * NQ].bitcast(FP8X4),
+                                    lhsT_scale=q_scales[:, first:first + NQ],
+                                    rhs=keys[b][:, g, :].bitcast(FP4X4), rhs_scale=ks_pass[g][:, b * N:(b + 1) * N],
+                                    start=(g == 0), stop=(g == PASSES - 1))
             scores.append(acc)
+        for b in range(B):
+            nc.vector.tensor_copy(pos_g[b][:], pos_win[:].indirect(seq_offs[b]))
 
-        for b in range(B):
-            split(b)
-        for b in range(B):
-            score(b)
-        for b in range(B):
-            places(b)
-
-        v1_win = arena.tile([P, T], BF16, offset=20480)
+        upper_win = arena.tile([P, T], BF16, offset=AT_UPPER_WIN)
         for lo, hi in PIECES:
-            nc.scalar.activation(v1_win[:, lo:hi], v1_raw[:, lo:hi], ACT.Copy)
-        v_g1 = [sb.tile([P, N], BF16, name="v_g10"), arena.tile([P, N], BF16, offset=53248, name="v_g11")]
+            nc.scalar.activation(upper_win[:, lo:hi], upper_raw[:, lo:hi], ACT.Copy)
+        upper_g = [sb.tile([P, N], BF16, name="upper_g0"),
+                   arena.tile([P, N], BF16, offset=AT_UPPER_G1, name="upper_g1")]
 
         def dealt(gathered):
             return gathered.rearrange("f (u p e) -> f p u e", u=2, e=2)
 
-        nc.scalar.activation(dealt(v_g1[0][:]), v1_win[:].indirect(seq_offs[0]), ACT.Copy)
-
+        nc.scalar.activation(dealt(upper_g[0][:]), upper_win[:].indirect(seq_offs[0]), ACT.Copy)
 
         def turn_values(gathered, tag):
-            words = gathered.bitcast(F32)
+            pairs = gathered.bitcast(F32)
             turned = bank(tag, [P, 2, P])
             for u in range(2):
-                nc.tensor.transpose(turned[:, u, :], words[:, u * P:(u + 1) * P], ident[:])
+                nc.tensor.transpose(turned[:, u, :], pairs[:, u * P:(u + 1) * P], ident[:])
             return turned
 
         def lay_values(laid, turned):
-            nc.scalar.copy(laid.bitcast(F32), turned[:].rearrange("p u e -> p e u"))
+            nc.scalar.copy(laid.bitcast(F32), turned[:].rearrange("p u f -> p f u"))
 
-        first_v1 = turn_values(v_g1[0][:], "d0")
+        upper_turned0 = turn_values(upper_g[0][:], "d0")
 
-        neg = sb.tile([P, B, N], F32)
-        clamped = arena.tile([P, B, N], F32, offset=51200)
+        small = sb.tile([P, B, N], F32)
+        masked = arena.tile([P, B, N], F32, offset=AT_MASKED)
         neg_max = [sb.tile([P, 1], F32, name="neg_max%d" % b) for b in range(B)]
         total = sb.tile([P, B], F32)
-        prob = [arena.tile([P, PACK, P], F32, offset=2048 + 2048 * b, name="prob%d" % b) for b in range(B)]
-        turned_p = []
+        prob = [arena.tile([P, PACK, P], F32, offset=AT_PROB + 2048 * b, name="prob%d" % b) for b in range(B)]
+        prob_turned = []
         for b in range(B):
-            nc.vector.scalar_tensor_tensor(neg[:, b], pos_g[b][:], q_turned[:, P - B + b:P - B + b + 1],
+            nc.vector.scalar_tensor_tensor(small[:, b], pos_g[b][:], q_places[:, P - B + b:P - B + b + 1],
                                            scores[b][:], ALU.is_gt, ALU.add)
-            nc.vector.tensor_scalar(clamped[:, b], neg[:, b], FAR, None, ALU.mult, ALU.min, accum_out=neg_max[b][:])
-            nc.scalar.activation(prob[b][:].rearrange("q t s -> q s t"), clamped[:, b].rearrange("q (s t) -> q s t", t=PACK),
+            nc.vector.tensor_scalar(masked[:, b], small[:, b], FAR, None, ALU.mult, ALU.min, accum_out=neg_max[b][:])
+            nc.scalar.activation(prob[b][:].rearrange("q t s -> q s t"),
+                                 masked[:, b].rearrange("q (s t) -> q s t", t=PACK),
                                  ACT.Exp, bias=neg_max[b][:], scale=-1.0, accum_out=total[:, b:b + 1])
-            tp = bank("b%d" % b, [P, PACK, NQ])
+            turned = bank("b%d" % b, [P, PACK, NQ])
             for t in range(PACK):
-                nc.tensor.transpose(tp[:, t, :], prob[b][:, t, :], ident[:])
-            turned_p.append(tp)
-        v_bf0 = arena.tile([P, DV, PACK], BF16, align_bytes=64, offset=51200)
-        v_bf11 = sb.tile([P, P, PACK], BF16, align_bytes=64)
-        v_bf01 = sb.tile([P, P, PACK], BF16, align_bytes=64)
-        nc.scalar.activation(dealt(v_g1[1][:]), v1_win[:].indirect(seq_offs[1]), ACT.Copy)
-        lay_values(v_bf0[:, P:DV, :], first_v1)
+                nc.tensor.transpose(turned[:, t, :], prob[b][:, t, :], ident[:])
+            prob_turned.append(turned)
 
-        v_g0 = [arena.tile([P, N], BF16, offset=45056 + 1024 * b, name="v_g0%d" % b) for b in range(B)]
+        laid0 = arena.tile([P, DV, PACK], BF16, align_bytes=64, offset=AT_LAID0)
+        laid1_upper = sb.tile([P, P, PACK], BF16, align_bytes=64)
+        laid1_lower = sb.tile([P, P, PACK], BF16, align_bytes=64)
+        nc.scalar.activation(dealt(upper_g[1][:]), upper_win[:].indirect(seq_offs[1]), ACT.Copy)
+        lay_values(laid0[:, P:DV, :], upper_turned0)
+
+        lower_g = [arena.tile([P, N], BF16, offset=AT_LOWER_G + 1024 * b, name="lower_g%d" % b) for b in range(B)]
         for b in range(B):
-            nc.vector.tensor_copy(dealt(v_g0[b][:]), v0_win[:].indirect(seq_offs[b]))
-        lay_values(v_bf0[:, 0:P, :], turn_values(v_g0[0][:], "d1"))
+            nc.vector.tensor_copy(dealt(lower_g[b][:]), lower_win[:].indirect(seq_offs[b]))
+        lay_values(laid0[:, 0:P, :], turn_values(lower_g[0][:], "d1"))
 
-        w_bf = [arena.tile([P, NQ, PACK], BF16, align_bytes=64, offset=12288 + 1024 * b, name="w_bf%d" % b)
-                for b in range(B)]
+        w_bf = [sb.tile([P, NQ, PACK], BF16, align_bytes=64, name="w_bf%d" % b) for b in range(B)]
 
         def weigh(b):
-            nc.vector.tensor_tensor(w_bf[b][:], turned_p[b][:].rearrange("p t q -> p q t"),
+            nc.vector.tensor_tensor(w_bf[b][:], prob_turned[b][:].rearrange("s t q -> s q t"),
                                     vs_col[b][:].unsqueeze(1).to_broadcast([P, NQ, PACK]), ALU.mult)
 
-        def quantise(name, laid, offset=None):
+        def quantise(name, laid):
             width = laid.shape[1]
-            pool = sb if offset is None else arena
-            codes = pool.tile([P, width], U32, align_bytes=64, offset=offset, name=name + "_codes")
+            codes = sb.tile([P, width], U32, align_bytes=64, name=name + "_codes")
             scales = sb.tile([P, width], U8, align_bytes=64, name=name + "_scales")
-            nc.vector.quantize_mx(codes[:].bitcast(FP8X4), scales[:], laid[:].rearrange("p c t -> p (c t)"))
+            nc.vector.quantize_mx(codes[:].bitcast(FP8X4), scales[:], laid[:].rearrange("s c t -> s (c t)"))
             return codes, scales
 
         def product(weights, values, tag):
@@ -206,19 +217,20 @@ def tile_attend_draft_kernel(tc, qT, k_words, k_scales, vT, vs, pos, qpos, offs,
             return acc
 
         weigh(0)
-        lay_values(v_bf01[:], turn_values(v_g0[1][:], "b0"))
-        lay_values(v_bf11[:], turn_values(v_g1[1][:], "d0"))
-        inv = arena.tile([P, B], F32, offset=16384)
-        nc.vector.reciprocal(inv[:], total[:])
-        w0 = quantise("w0", w_bf[0])
+        lay_values(laid1_lower[:], turn_values(lower_g[1][:], "b0"))
+        lay_values(laid1_upper[:], turn_values(upper_g[1][:], "d0"))
         weigh(1)
-        sum0 = product(w0, quantise("v0", v_bf0, 37888), "c0")
+        w0 = quantise("w0", w_bf[0])
+        inv = arena.tile([P, B], F32, offset=AT_INV)
+        nc.vector.reciprocal(inv[:], total[:])
+        sum0 = product(w0, quantise("v0", laid0), "c0")
         w1 = quantise("w1", w_bf[1])
-        sum01 = product(w1, quantise("v01", v_bf01), "a1")
-        sum11 = product(w1, quantise("v11", v_bf11), "c1")
-        y = [arena.tile([P, DV], F32, offset=46080, name="y0"), sb.tile([P, DV], F32, name="y1")]
+        sum1_lower = product(w1, quantise("v1_lower", laid1_lower), "a1")
+        sum1_upper = product(w1, quantise("v1_upper", laid1_upper), "c1")
+
+        y = [arena.tile([P, DV], F32, offset=AT_Y0, name="y0"), sb.tile([P, DV], F32, name="y1")]
         nc.scalar.activation(y[0][:], sum0[:], ACT.Copy, scale=inv[:, 0:1])
         nc.sync.dma_start(out[0], y[0][:])
-        nc.scalar.activation(y[1][:, 0:P], sum01[:], ACT.Copy, scale=inv[:, 1:2])
-        nc.vector.tensor_scalar(y[1][:, P:DV], sum11[:], inv[:, 1:2], None, ALU.mult)
+        nc.scalar.activation(y[1][:, 0:P], sum1_lower[:], ACT.Copy, scale=inv[:, 1:2])
+        nc.vector.tensor_scalar(y[1][:, P:DV], sum1_upper[:], inv[:, 1:2], None, ALU.mult)
         nc.sync.dma_start(out[1], y[1][:])

@@ -35,13 +35,15 @@ AT_KEY_WORDS = 24576
 AT_SCALE_COLS = 36864
 AT_INV = AT_SCALE_COLS + 1024
 AT_QUERIES = 40960
-AT_PLACES = (AT_QUERIES - 1024, AT_QUERIES + 4096)
+AT_RAW_QUERIES = 57344
+AT_KEYS1 = AT_RAW_QUERIES
+AT_PLACES = (AT_RAW_QUERIES + 2048, AT_RAW_QUERIES + 3 * 2048 + 1024)
+AT_SMALL0 = AT_PLACES[1] - 2048
 AT_LOWER_G = AT_PLACES[1]
 AT_Y0 = AT_LOWER_G + 1024
 AT_MASKED = 51200
 AT_LAID0 = AT_MASKED
 AT_UPPER_G1 = AT_MASKED + 2048
-AT_RAW_QUERIES = 57344
 
 
 def tile_attend_draft_kernel(tc, qT, k_words, k_scales, vT, vs, pos, qpos, offs, out):
@@ -111,37 +113,46 @@ def tile_attend_draft_kernel(tc, qT, k_words, k_scales, vT, vs, pos, qpos, offs,
         for b in range(B):
             nc.sync.dma_start(vs_col[b][:], vs_g[ROW:P, b * N:(b + 1) * N])
 
-        q_bf = [arena.tile([P, PASSES, NQ, PACK], BF16, align_bytes=64, offset=AT_QUERIES + 4096 * b,
-                           name="q_bf%d" % b) for b in range(B)]
+        q_bf = [[arena.tile([P, NQ, PACK], BF16, align_bytes=64, offset=AT_QUERIES + 1024 * (PASSES * b + g),
+                            name="q_bf%d%d" % (b, g)) for g in range(PASSES)] for b in range(B)]
         for b in range(B):
             for g in range(PASSES):
-                nc.scalar.activation(q_bf[b][:, g].rearrange("p (c i) j -> p c j i", i=PACK),
+                nc.scalar.activation(q_bf[b][g][:].rearrange("p (c i) j -> p c j i", i=PACK),
                                      q_raw[b][g][:].rearrange("p (j c i) -> p c j i", j=PACK, i=PACK),
                                      ACT.Copy, scale=-1.0 / FAR)
 
         kw_g = [sb.tile([P, N], U32, name="kw_g%d" % b) for b in range(B)]
         for b in range(B):
             nc.vector.tensor_copy(kw_g[b][:], kw_win[:].bitcast(U32).indirect(seq_offs[b]))
-        keys = [sb.tile([P, PASSES, 2 * N], U8, align_bytes=64, name="keys%d" % b) for b in range(B)]
-        q_scales = sb.tile([P, B * PASSES * NQ], U8, align_bytes=64)
+        keys = [sb.tile([P, PASSES, 2 * N], U8, align_bytes=64, name="keys0"),
+                arena.tile([P, PASSES, 2 * N], U8, align_bytes=64, offset=AT_KEYS1, name="keys1")]
         pos_g = [arena.tile([P, N], F32, offset=AT_PLACES[b], name="pos_g%d" % b) for b in range(B)]
-        for b in range(B):
+
+        def split(b):
             nc.vector.tensor_copy(keys[b][:].bitcast(U16),
                                   kw_g[b][:].bitcast(U16).rearrange("p (n g) -> p g n", g=PASSES))
 
-        scores = []
-        for b in range(B):
-            q_codes = sb.tile([P, PASSES * NQ], U32, align_bytes=64, name="q_codes%d" % b)
-            nc.vector.quantize_mx(q_codes[:].bitcast(FP8X4), q_scales[:, b * PASSES * NQ:(b + 1) * PASSES * NQ],
-                                  q_bf[b][:].rearrange("p g q j -> p (g q j)"))
-            acc = bank("a%d" % b, [P, N])
-            for g in range(PASSES):
-                first = (b * PASSES + g) * NQ
-                nc.tensor.matmul_mx(acc[:], lhsT=q_codes[:, g * NQ:(g + 1) * NQ].bitcast(FP8X4),
-                                    lhsT_scale=q_scales[:, first:first + NQ],
-                                    rhs=keys[b][:, g, :].bitcast(FP4X4), rhs_scale=ks_pass[g][:, b * N:(b + 1) * N],
-                                    start=(g == 0), stop=(g == PASSES - 1))
-            scores.append(acc)
+        def quantise(name, laid):
+            width = laid.shape[1]
+            codes = sb.tile([P, width], U32, align_bytes=64, name=name + "_codes")
+            scales = sb.tile([P, width], U8, align_bytes=64, name=name + "_scales")
+            nc.vector.quantize_mx(codes[:].bitcast(FP8X4), scales[:], laid[:].rearrange("s c t -> s (c t)"))
+            return codes, scales
+
+        scores = [bank("a%d" % b, [P, N]) for b in range(B)]
+
+        def score(b, g):
+            codes, scales = quantise("q%d%d" % (b, g), q_bf[b][g])
+            nc.tensor.matmul_mx(scores[b][:], lhsT=codes[:].bitcast(FP8X4), lhsT_scale=scales[:],
+                                rhs=keys[b][:, g, :].bitcast(FP4X4), rhs_scale=ks_pass[g][:, b * N:(b + 1) * N],
+                                start=(g == 0), stop=(g == PASSES - 1))
+
+        split(0)
+        score(0, 0)
+        split(1)
+        score(0, 1)
+        score(1, 0)
+        score(1, 1)
         for b in range(B):
             nc.vector.tensor_copy(pos_g[b][:], pos_win[:].indirect(seq_offs[b]))
 
@@ -168,16 +179,16 @@ def tile_attend_draft_kernel(tc, qT, k_words, k_scales, vT, vs, pos, qpos, offs,
 
         upper_turned0 = turn_values(upper_g[0][:], "d0")
 
-        small = sb.tile([P, B, N], F32)
+        small = [arena.tile([P, N], F32, offset=AT_SMALL0, name="small0"), sb.tile([P, N], F32, name="small1")]
         masked = arena.tile([P, B, N], F32, offset=AT_MASKED)
         neg_max = [sb.tile([P, 1], F32, name="neg_max%d" % b) for b in range(B)]
         total = sb.tile([P, B], F32)
         prob = [arena.tile([P, PACK, P], F32, offset=AT_PROB + 2048 * b, name="prob%d" % b) for b in range(B)]
         prob_turned = []
         for b in range(B):
-            nc.vector.scalar_tensor_tensor(small[:, b], pos_g[b][:], q_places[:, P - B + b:P - B + b + 1],
+            nc.vector.scalar_tensor_tensor(small[b][:], pos_g[b][:], q_places[:, P - B + b:P - B + b + 1],
                                            scores[b][:], ALU.is_gt, ALU.add)
-            nc.vector.tensor_scalar(masked[:, b], small[:, b], FAR, None, ALU.mult, ALU.min, accum_out=neg_max[b][:])
+            nc.vector.tensor_scalar(masked[:, b], small[b][:], FAR, None, ALU.mult, ALU.min, accum_out=neg_max[b][:])
             nc.scalar.activation(prob[b][:].rearrange("q t s -> q s t"),
                                  masked[:, b].rearrange("q (s t) -> q s t", t=PACK),
                                  ACT.Exp, bias=neg_max[b][:], scale=-1.0, accum_out=total[:, b:b + 1])
@@ -203,13 +214,6 @@ def tile_attend_draft_kernel(tc, qT, k_words, k_scales, vT, vs, pos, qpos, offs,
             nc.vector.tensor_tensor(w_bf[b][:], prob_turned[b][:].rearrange("s t q -> s q t"),
                                     vs_col[b][:].unsqueeze(1).to_broadcast([P, NQ, PACK]), ALU.mult)
 
-        def quantise(name, laid):
-            width = laid.shape[1]
-            codes = sb.tile([P, width], U32, align_bytes=64, name=name + "_codes")
-            scales = sb.tile([P, width], U8, align_bytes=64, name=name + "_scales")
-            nc.vector.quantize_mx(codes[:].bitcast(FP8X4), scales[:], laid[:].rearrange("s c t -> s (c t)"))
-            return codes, scales
-
         def product(weights, values, tag):
             acc = bank(tag, [P, values[0].shape[1]])
             nc.tensor.matmul_mx(acc[:], lhsT=weights[0][:].bitcast(FP8X4), lhsT_scale=weights[1][:],
@@ -217,15 +221,15 @@ def tile_attend_draft_kernel(tc, qT, k_words, k_scales, vT, vs, pos, qpos, offs,
             return acc
 
         weigh(0)
-        lay_values(laid1_lower[:], turn_values(lower_g[1][:], "b0"))
-        lay_values(laid1_upper[:], turn_values(upper_g[1][:], "d0"))
+        lay_values(laid1_lower[:], turn_values(lower_g[1][:], "a0"))
+        lay_values(laid1_upper[:], turn_values(upper_g[1][:], "a1"))
         weigh(1)
         w0 = quantise("w0", w_bf[0])
         inv = arena.tile([P, B], F32, offset=AT_INV)
         nc.vector.reciprocal(inv[:], total[:])
         sum0 = product(w0, quantise("v0", laid0), "c0")
         w1 = quantise("w1", w_bf[1])
-        sum1_lower = product(w1, quantise("v1_lower", laid1_lower), "a1")
+        sum1_lower = product(w1, quantise("v1_lower", laid1_lower), "b0")
         sum1_upper = product(w1, quantise("v1_upper", laid1_upper), "c1")
 
         y = [arena.tile([P, DV], F32, offset=AT_Y0, name="y0"), sb.tile([P, DV], F32, name="y1")]

@@ -22,6 +22,7 @@ PACK = 4
 PASSES = D // (P * PACK)
 COLS = N // 16
 FAR = float(2 ** 40)
+STEP = 2.0 ** -12
 ROW = P - 1
 SHIFT = 16
 PIECES = ((0, 768), (768, 1536), (1536, T))
@@ -37,8 +38,9 @@ AT_INV = AT_SCALE_COLS + 1024
 AT_QUERIES = 40960
 AT_RAW_QUERIES = 57344
 AT_KEYS1 = AT_RAW_QUERIES
-AT_PLACES = (AT_RAW_QUERIES + 2048, AT_RAW_QUERIES + 3 * 2048 + 1024)
-AT_SMALL0 = AT_PLACES[1] - 2048
+AT_PLACES = (AT_RAW_QUERIES + 3072, AT_RAW_QUERIES + 5120)
+AT_RAW = tuple(AT_RAW_QUERIES + 2048 * i for i in (0, 1, 2, 4))
+AT_WORDS1 = AT_QUERIES + 3072
 AT_LOWER_G = AT_PLACES[1]
 AT_Y0 = AT_LOWER_G + 1024
 AT_MASKED = 51200
@@ -77,7 +79,7 @@ def tile_attend_draft_kernel(tc, qT, k_words, k_scales, vT, vs, pos, qpos, offs,
         nc.vector.memset(vs_win[0:ROW, :], 0.0)
         ks_low = sb.tile([P, B * N // 4], I32, align_bytes=64)
         nc.vector.memset(ks_low[96:P, :], 0)
-        q_raw = [[arena.tile([P, PACK * NQ], F32, offset=AT_RAW_QUERIES + 2048 * (PASSES * b + g),
+        q_raw = [[arena.tile([P, PACK * NQ], F32, offset=AT_RAW[PASSES * b + g],
                              name="q_raw%d%d" % (b, g)) for g in range(PASSES)] for b in range(B)]
         for b in range(B):
             for g in range(PASSES):
@@ -96,6 +98,8 @@ def tile_attend_draft_kernel(tc, qT, k_words, k_scales, vT, vs, pos, qpos, offs,
                                  spread[:].rearrange("q j n -> q n j"), ACT.Copy)
         q_places = bank("c0", [P, P])
         nc.tensor.transpose(q_places[:], q_rows[:], ident[:])
+        q_key = sb.tile([P, B], F32)
+        nc.scalar.activation(q_key[:], q_places[:, P - B:P], ACT.Exp, scale=STEP)
 
         vs_g = sb.tile([P, B * N], F32)
         nc.vector.tensor_copy(vs_g[:], vs_win[:].indirect(offs_t[:]))
@@ -115,13 +119,14 @@ def tile_attend_draft_kernel(tc, qT, k_words, k_scales, vT, vs, pos, qpos, offs,
 
         q_bf = [[arena.tile([P, NQ, PACK], BF16, align_bytes=64, offset=AT_QUERIES + 1024 * (PASSES * b + g),
                             name="q_bf%d%d" % (b, g)) for g in range(PASSES)] for b in range(B)]
-        for b in range(B):
-            for g in range(PASSES):
-                nc.scalar.activation(q_bf[b][g][:].rearrange("p (c i) j -> p c j i", i=PACK),
-                                     q_raw[b][g][:].rearrange("p (j c i) -> p c j i", j=PACK, i=PACK),
-                                     ACT.Copy, scale=-1.0 / FAR)
+        def query_views(b, g):
+            return (q_bf[b][g][:].rearrange("p (c i) j -> p c j i", i=PACK),
+                    q_raw[b][g][:].rearrange("p (j c i) -> p c j i", j=PACK, i=PACK))
 
-        kw_g = [sb.tile([P, N], U32, name="kw_g%d" % b) for b in range(B)]
+        for b, g in ((0, 0), (0, 1), (1, 0)):
+            nc.scalar.activation(*query_views(b, g), ACT.Copy, scale=-1.0 / FAR)
+
+        kw_g = [sb.tile([P, N], U32, name="kw_g0"), arena.tile([P, N], U32, offset=AT_WORDS1, name="kw_g1")]
         for b in range(B):
             nc.vector.tensor_copy(kw_g[b][:], kw_win[:].bitcast(U32).indirect(seq_offs[b]))
         keys = [sb.tile([P, PASSES, 2 * N], U8, align_bytes=64, name="keys0"),
@@ -151,10 +156,11 @@ def tile_attend_draft_kernel(tc, qT, k_words, k_scales, vT, vs, pos, qpos, offs,
         score(0, 0)
         split(1)
         score(0, 1)
+        nc.vector.tensor_scalar(*query_views(1, 1), -1.0 / FAR, None, ALU.mult)
         score(1, 0)
         score(1, 1)
         for b in range(B):
-            nc.vector.tensor_copy(pos_g[b][:], pos_win[:].indirect(seq_offs[b]))
+            nc.scalar.activation(pos_g[b][:], pos_win[:].indirect(seq_offs[b]), ACT.Exp, scale=STEP)
 
         upper_win = arena.tile([P, T], BF16, offset=AT_UPPER_WIN)
         for lo, hi in PIECES:
@@ -179,15 +185,14 @@ def tile_attend_draft_kernel(tc, qT, k_words, k_scales, vT, vs, pos, qpos, offs,
 
         upper_turned0 = turn_values(upper_g[0][:], "d0")
 
-        small = [arena.tile([P, N], F32, offset=AT_SMALL0, name="small0"), sb.tile([P, N], F32, name="small1")]
+        small = [sb.tile([P, N], F32, name="small%d" % b) for b in range(B)]
         masked = arena.tile([P, B, N], F32, offset=AT_MASKED)
         neg_max = [sb.tile([P, 1], F32, name="neg_max%d" % b) for b in range(B)]
         total = sb.tile([P, B], F32)
         prob = [arena.tile([P, PACK, P], F32, offset=AT_PROB + 2048 * b, name="prob%d" % b) for b in range(B)]
         prob_turned = []
         for b in range(B):
-            nc.vector.scalar_tensor_tensor(small[b][:], pos_g[b][:], q_places[:, P - B + b:P - B + b + 1],
-                                           scores[b][:], ALU.is_gt, ALU.add)
+            nc.vector.scalar_tensor_tensor(small[b][:], pos_g[b][:], q_key[:, b:b + 1], scores[b][:], ALU.is_gt, ALU.add)
             nc.vector.tensor_scalar(masked[:, b], small[b][:], FAR, None, ALU.mult, ALU.min, accum_out=neg_max[b][:])
             nc.scalar.activation(prob[b][:].rearrange("q t s -> q s t"),
                                  masked[:, b].rearrange("q (s t) -> q s t", t=PACK),

@@ -27,11 +27,13 @@ ROW = P - 1
 SHIFT = 16
 PIECES = ((0, 768), (768, 1536), (1536, T))
 
+CAST_V = 512
+
 AT_KEY_SCALES = 8192
 AT_UPPER_RAW = AT_KEY_SCALES + 1024 - 4 * T
 AT_LOWER_WIN = AT_KEY_SCALES + 1024
 AT_PROB = 2048
-AT_UPPER_WIN = 20480
+AT_UPPER_WIN = 65536
 AT_KEY_WORDS = 24576
 AT_SCALE_COLS = 36864
 AT_INV = AT_SCALE_COLS + 1024
@@ -163,7 +165,8 @@ def tile_attend_draft_kernel(tc, qT, k_words, k_scales, vT, vs, pos, qpos, offs,
             nc.scalar.activation(pos_g[b][:], pos_win[:].indirect(seq_offs[b]), ACT.Exp, scale=STEP)
 
         upper_win = arena.tile([P, T], BF16, offset=AT_UPPER_WIN)
-        for lo, hi in PIECES:
+        nc.vector.tensor_copy(upper_win[:, 0:CAST_V], upper_raw[:, 0:CAST_V])
+        for lo, hi in ((CAST_V, PIECES[0][1]),) + PIECES[1:]:
             nc.scalar.activation(upper_win[:, lo:hi], upper_raw[:, lo:hi], ACT.Copy)
         upper_g = [sb.tile([P, N], BF16, name="upper_g0"),
                    arena.tile([P, N], BF16, offset=AT_UPPER_G1, name="upper_g1")]

@@ -22,18 +22,13 @@ PACK = 4
 PASSES = D // (P * PACK)
 COLS = N // 16
 FAR = float(2 ** 40)
-STEP = 2.0 ** -12
 ROW = P - 1
 SHIFT = 16
-PIECES = ((0, 768), (768, 1536), (1536, T))
-
-CAST_V = 512
 
 AT_KEY_SCALES = 8192
-AT_UPPER_RAW = AT_KEY_SCALES + 1024 - 4 * T
+AT_UPPER_WIN = AT_KEY_SCALES + 1024 - 4 * T
 AT_LOWER_WIN = AT_KEY_SCALES + 1024
 AT_PROB = 2048
-AT_UPPER_WIN = 65536
 AT_KEY_WORDS = 24576
 AT_SCALE_COLS = 36864
 AT_INV = AT_SCALE_COLS + 1024
@@ -47,7 +42,6 @@ AT_LOWER_G = AT_PLACES[1]
 AT_Y0 = AT_LOWER_G + 1024
 AT_MASKED = 51200
 AT_LAID0 = AT_MASKED
-AT_UPPER_G1 = AT_MASKED + 2048
 
 
 def tile_attend_draft_kernel(tc, qT, k_words, k_scales, vT, vs, pos, qpos, offs, out):
@@ -100,8 +94,6 @@ def tile_attend_draft_kernel(tc, qT, k_words, k_scales, vT, vs, pos, qpos, offs,
                                  spread[:].rearrange("q j n -> q n j"), ACT.Copy)
         q_places = bank("c0", [P, P])
         nc.tensor.transpose(q_places[:], q_rows[:], ident[:])
-        q_key = sb.tile([P, B], F32)
-        nc.scalar.activation(q_key[:], q_places[:, P - B:P], ACT.Exp, scale=STEP)
 
         vs_g = sb.tile([P, B * N], F32)
         nc.vector.tensor_copy(vs_g[:], vs_win[:].indirect(offs_t[:]))
@@ -109,9 +101,8 @@ def tile_attend_draft_kernel(tc, qT, k_words, k_scales, vT, vs, pos, qpos, offs,
         nc.vector.tensor_copy(ks_g[:], ks_win[:].bitcast(U8).indirect(offs_t[:]))
         for lo, hi in ((0, 64), (64, 96), (96, P - SHIFT)):
             nc.sync.dma_start(ks_low[lo:hi, :], ks_g[lo + SHIFT:hi + SHIFT, :].bitcast(I32))
-        upper_raw = arena.tile([P, T], F32, offset=AT_UPPER_RAW)
-        for lo, hi in PIECES:
-            nc.sync.dma_start(upper_raw[:, lo:hi], vT[P:2 * P, lo:hi])
+        upper_win = arena.tile([P, T], F32, offset=AT_UPPER_WIN)
+        nc.sync.dma_start(upper_win[:], vT[P:2 * P, :])
         lower_win = arena.tile([P, T], F32, offset=AT_LOWER_WIN)
         nc.sync.dma_start(lower_win[:], vT[0:P, :])
         ks_pass = [ks_g[:], ks_low[:].bitcast(U8)]
@@ -162,31 +153,29 @@ def tile_attend_draft_kernel(tc, qT, k_words, k_scales, vT, vs, pos, qpos, offs,
         score(1, 0)
         score(1, 1)
         for b in range(B):
-            nc.scalar.activation(pos_g[b][:], pos_win[:].indirect(seq_offs[b]), ACT.Exp, scale=STEP)
+            nc.scalar.activation(pos_g[b][:], pos_win[:].indirect(seq_offs[b]), ACT.Copy)
 
-        upper_win = arena.tile([P, T], BF16, offset=AT_UPPER_WIN)
-        nc.vector.tensor_copy(upper_win[:, 0:CAST_V], upper_raw[:, 0:CAST_V])
-        for lo, hi in ((CAST_V, PIECES[0][1]),) + PIECES[1:]:
-            nc.scalar.activation(upper_win[:, lo:hi], upper_raw[:, lo:hi], ACT.Copy)
-        upper_g = [sb.tile([P, N], BF16, name="upper_g0"),
-                   arena.tile([P, N], BF16, offset=AT_UPPER_G1, name="upper_g1")]
+        upper_g = [sb.tile([P, N], BF16, name="upper_g%d" % b) for b in range(B)]
 
         def dealt(gathered):
             return gathered.rearrange("f (u p e) -> f p u e", u=2, e=2)
 
-        nc.scalar.activation(dealt(upper_g[0][:]), upper_win[:].indirect(seq_offs[0]), ACT.Copy)
+        for b in range(B):
+            nc.scalar.activation(upper_g[b][:], upper_win[:].indirect(seq_offs[b]), ACT.Copy)
 
-        def turn_values(gathered, tag):
-            pairs = gathered.bitcast(F32)
+        def turn_values(halves, tag):
             turned = bank(tag, [P, 2, P])
             for u in range(2):
-                nc.tensor.transpose(turned[:, u, :], pairs[:, u * P:(u + 1) * P], ident[:])
+                nc.tensor.transpose(turned[:, u, :], halves[:, u, :], ident[:])
             return turned
+
+        def listed_halves(gathered):
+            return gathered.bitcast(F32).rearrange("f (p u) -> f u p", u=2)
 
         def lay_values(laid, turned):
             nc.scalar.copy(laid.bitcast(F32), turned[:].rearrange("p u f -> p f u"))
 
-        upper_turned0 = turn_values(upper_g[0][:], "d0")
+        upper_turned = [turn_values(listed_halves(upper_g[b][:]), tag) for b, tag in enumerate(("d0", "c1"))]
 
         small = [sb.tile([P, N], F32, name="small%d" % b) for b in range(B)]
         masked = arena.tile([P, B, N], F32, offset=AT_MASKED)
@@ -195,7 +184,8 @@ def tile_attend_draft_kernel(tc, qT, k_words, k_scales, vT, vs, pos, qpos, offs,
         prob = [arena.tile([P, PACK, P], F32, offset=AT_PROB + 2048 * b, name="prob%d" % b) for b in range(B)]
         prob_turned = []
         for b in range(B):
-            nc.vector.scalar_tensor_tensor(small[b][:], pos_g[b][:], q_key[:, b:b + 1], scores[b][:], ALU.is_gt, ALU.add)
+            nc.vector.scalar_tensor_tensor(small[b][:], pos_g[b][:], q_places[:, P - B + b:P - B + b + 1], scores[b][:],
+                                           ALU.is_gt, ALU.add)
             nc.vector.tensor_scalar(masked[:, b], small[b][:], FAR, None, ALU.mult, ALU.min, accum_out=neg_max[b][:])
             nc.scalar.activation(prob[b][:].rearrange("q t s -> q s t"),
                                  masked[:, b].rearrange("q (s t) -> q s t", t=PACK),
@@ -208,13 +198,12 @@ def tile_attend_draft_kernel(tc, qT, k_words, k_scales, vT, vs, pos, qpos, offs,
         laid0 = arena.tile([P, DV, PACK], BF16, align_bytes=64, offset=AT_LAID0)
         laid1_upper = sb.tile([P, P, PACK], BF16, align_bytes=64)
         laid1_lower = sb.tile([P, P, PACK], BF16, align_bytes=64)
-        nc.scalar.activation(dealt(upper_g[1][:]), upper_win[:].indirect(seq_offs[1]), ACT.Copy)
-        lay_values(laid0[:, P:DV, :], upper_turned0)
-
         lower_g = [arena.tile([P, N], BF16, offset=AT_LOWER_G + 1024 * b, name="lower_g%d" % b) for b in range(B)]
-        for b in range(B):
-            nc.vector.tensor_copy(dealt(lower_g[b][:]), lower_win[:].indirect(seq_offs[b]))
-        lay_values(laid0[:, 0:P, :], turn_values(lower_g[0][:], "d1"))
+        nc.vector.tensor_copy(dealt(lower_g[0][:]), lower_win[:].indirect(seq_offs[0]))
+        nc.scalar.activation(lower_g[1][:], lower_win[:].indirect(seq_offs[1]), ACT.Copy)
+        lay_values(laid0[:, P:DV, :], upper_turned[0])
+        lay_values(laid1_upper[:], upper_turned[1])
+        lay_values(laid0[:, 0:P, :], turn_values(lower_g[0][:].bitcast(F32).rearrange("f (u p) -> f u p", u=2), "d1"))
 
         w_bf = [sb.tile([P, NQ, PACK], BF16, align_bytes=64, name="w_bf%d" % b) for b in range(B)]
 
@@ -229,20 +218,19 @@ def tile_attend_draft_kernel(tc, qT, k_words, k_scales, vT, vs, pos, qpos, offs,
             return acc
 
         weigh(0)
-        lay_values(laid1_lower[:], turn_values(lower_g[1][:], "a0"))
-        lay_values(laid1_upper[:], turn_values(upper_g[1][:], "a1"))
+        lay_values(laid1_lower[:], turn_values(listed_halves(lower_g[1][:]), "a0"))
         weigh(1)
         w0 = quantise("w0", w_bf[0])
         inv = arena.tile([P, B], F32, offset=AT_INV)
         nc.vector.reciprocal(inv[:], total[:])
         sum0 = product(w0, quantise("v0", laid0), "c0")
         w1 = quantise("w1", w_bf[1])
-        sum1_lower = product(w1, quantise("v1_lower", laid1_lower), "b0")
         sum1_upper = product(w1, quantise("v1_upper", laid1_upper), "c1")
+        sum1_lower = product(w1, quantise("v1_lower", laid1_lower), "b0")
 
         y = [arena.tile([P, DV], F32, offset=AT_Y0, name="y0"), sb.tile([P, DV], F32, name="y1")]
         nc.scalar.activation(y[0][:], sum0[:], ACT.Copy, scale=inv[:, 0:1])
         nc.sync.dma_start(out[0], y[0][:])
-        nc.scalar.activation(y[1][:, 0:P], sum1_lower[:], ACT.Copy, scale=inv[:, 1:2])
-        nc.vector.tensor_scalar(y[1][:, P:DV], sum1_upper[:], inv[:, 1:2], None, ALU.mult)
+        nc.scalar.activation(y[1][:, P:DV], sum1_upper[:], ACT.Copy, scale=inv[:, 1:2])
+        nc.vector.tensor_scalar(y[1][:, 0:P], sum1_lower[:], inv[:, 1:2], None, ALU.mult)
         nc.sync.dma_start(out[1], y[1][:])

@@ -28,7 +28,8 @@ SHIFT = 16
 AT_KEY_SCALES = 8192
 AT_UPPER_WIN = AT_KEY_SCALES + 1024 - 4 * T
 AT_LOWER_WIN = AT_KEY_SCALES + 1024
-AT_PROB = 2048
+AT_UPPER_G0 = 0
+AT_PROB = (512, 4096)
 AT_KEY_WORDS = 24576
 AT_SCALE_COLS = 36864
 AT_INV = AT_SCALE_COLS + 1024
@@ -41,7 +42,7 @@ AT_WORDS1 = AT_QUERIES + 3072
 AT_LOWER_G = AT_PLACES[1]
 AT_Y0 = AT_LOWER_G + 1024
 AT_MASKED = 51200
-AT_LAID0 = AT_MASKED
+AT_LAID = AT_MASKED
 
 
 def tile_attend_draft_kernel(tc, qT, k_words, k_scales, vT, vs, pos, qpos, offs, out):
@@ -130,12 +131,17 @@ def tile_attend_draft_kernel(tc, qT, k_words, k_scales, vT, vs, pos, qpos, offs,
             nc.vector.tensor_copy(keys[b][:].bitcast(U16),
                                   kw_g[b][:].bitcast(U16).rearrange("p (n g) -> p g n", g=PASSES))
 
+        def operand(name, width):
+            return (sb.tile([P, width], U32, align_bytes=64, name=name + "_codes"),
+                    sb.tile([P, width], U8, align_bytes=64, name=name + "_scales"))
+
+        def quantise_into(into, at, laid):
+            nc.vector.quantize_mx(into[0][:, at:at + P].bitcast(FP8X4), into[1][:, at:at + P],
+                                  laid[:].rearrange("s c t -> s (c t)"))
+            return into
+
         def quantise(name, laid):
-            width = laid.shape[1]
-            codes = sb.tile([P, width], U32, align_bytes=64, name=name + "_codes")
-            scales = sb.tile([P, width], U8, align_bytes=64, name=name + "_scales")
-            nc.vector.quantize_mx(codes[:].bitcast(FP8X4), scales[:], laid[:].rearrange("s c t -> s (c t)"))
-            return codes, scales
+            return quantise_into(operand(name, P), 0, laid)
 
         scores = [bank("a%d" % b, [P, N]) for b in range(B)]
 
@@ -155,7 +161,7 @@ def tile_attend_draft_kernel(tc, qT, k_words, k_scales, vT, vs, pos, qpos, offs,
         for b in range(B):
             nc.scalar.activation(pos_g[b][:], pos_win[:].indirect(seq_offs[b]), ACT.Copy)
 
-        upper_g = [sb.tile([P, N], BF16, name="upper_g%d" % b) for b in range(B)]
+        upper_g = [arena.tile([P, N], BF16, offset=AT_UPPER_G0, name="upper_g0"), sb.tile([P, N], BF16, name="upper_g1")]
 
         def dealt(gathered):
             return gathered.rearrange("f (u p e) -> f p u e", u=2, e=2)
@@ -176,12 +182,14 @@ def tile_attend_draft_kernel(tc, qT, k_words, k_scales, vT, vs, pos, qpos, offs,
             nc.scalar.copy(laid.bitcast(F32), turned[:].rearrange("p u f -> p f u"))
 
         upper_turned = [turn_values(listed_halves(upper_g[b][:]), tag) for b, tag in enumerate(("d0", "c1"))]
+        laid0_upper = sb.tile([P, P, PACK], BF16, align_bytes=64)
+        lay_values(laid0_upper[:], upper_turned[0])
 
         small = [sb.tile([P, N], F32, name="small%d" % b) for b in range(B)]
         masked = arena.tile([P, B, N], F32, offset=AT_MASKED)
         neg_max = [sb.tile([P, 1], F32, name="neg_max%d" % b) for b in range(B)]
         total = sb.tile([P, B], F32)
-        prob = [arena.tile([P, PACK, P], F32, offset=AT_PROB + 2048 * b, name="prob%d" % b) for b in range(B)]
+        prob = [arena.tile([P, PACK, P], F32, offset=AT_PROB[b], name="prob%d" % b) for b in range(B)]
         prob_turned = []
         for b in range(B):
             nc.vector.scalar_tensor_tensor(small[b][:], pos_g[b][:], q_places[:, P - B + b:P - B + b + 1], scores[b][:],
@@ -195,15 +203,14 @@ def tile_attend_draft_kernel(tc, qT, k_words, k_scales, vT, vs, pos, qpos, offs,
                 nc.tensor.transpose(turned[:, t, :], prob[b][:, t, :], ident[:])
             prob_turned.append(turned)
 
-        laid0 = arena.tile([P, DV, PACK], BF16, align_bytes=64, offset=AT_LAID0)
-        laid1_upper = sb.tile([P, P, PACK], BF16, align_bytes=64)
+        laid0_lower = arena.tile([P, P, PACK], BF16, align_bytes=64, offset=AT_LAID)
+        laid1_upper = arena.tile([P, P, PACK], BF16, align_bytes=64, offset=AT_LAID + 1024)
         laid1_lower = sb.tile([P, P, PACK], BF16, align_bytes=64)
         lower_g = [arena.tile([P, N], BF16, offset=AT_LOWER_G + 1024 * b, name="lower_g%d" % b) for b in range(B)]
         nc.vector.tensor_copy(dealt(lower_g[0][:]), lower_win[:].indirect(seq_offs[0]))
         nc.scalar.activation(lower_g[1][:], lower_win[:].indirect(seq_offs[1]), ACT.Copy)
-        lay_values(laid0[:, P:DV, :], upper_turned[0])
+        lay_values(laid0_lower[:], turn_values(lower_g[0][:].bitcast(F32).rearrange("f (u p) -> f u p", u=2), "d1"))
         lay_values(laid1_upper[:], upper_turned[1])
-        lay_values(laid0[:, 0:P, :], turn_values(lower_g[0][:].bitcast(F32).rearrange("f (u p) -> f u p", u=2), "d1"))
 
         w_bf = [sb.tile([P, NQ, PACK], BF16, align_bytes=64, name="w_bf%d" % b) for b in range(B)]
 
@@ -218,13 +225,14 @@ def tile_attend_draft_kernel(tc, qT, k_words, k_scales, vT, vs, pos, qpos, offs,
             return acc
 
         weigh(0)
+        v0 = quantise_into(operand("v0", DV), P, laid0_upper)
+        w0 = quantise("w0", w_bf[0])
         lay_values(laid1_lower[:], turn_values(listed_halves(lower_g[1][:]), "a0"))
         weigh(1)
-        w0 = quantise("w0", w_bf[0])
+        sum0 = product(w0, quantise_into(v0, 0, laid0_lower), "c0")
+        w1 = quantise("w1", w_bf[1])
         inv = arena.tile([P, B], F32, offset=AT_INV)
         nc.vector.reciprocal(inv[:], total[:])
-        sum0 = product(w0, quantise("v0", laid0), "c0")
-        w1 = quantise("w1", w_bf[1])
         sum1_upper = product(w1, quantise("v1_upper", laid1_upper), "c1")
         sum1_lower = product(w1, quantise("v1_lower", laid1_lower), "b0")
 

@@ -28,8 +28,7 @@ SHIFT = 16
 AT_KEY_SCALES = 8192
 AT_UPPER_WIN = AT_KEY_SCALES + 1024 - 4 * T
 AT_LOWER_WIN = AT_KEY_SCALES + 1024
-AT_UPPER_G0 = 0
-AT_PROB = (512, 4096)
+AT_PROB = (2048, 4096)
 AT_KEY_WORDS = 24576
 AT_SCALE_COLS = 36864
 AT_INV = AT_SCALE_COLS + 1024
@@ -161,7 +160,7 @@ def tile_attend_draft_kernel(tc, qT, k_words, k_scales, vT, vs, pos, qpos, offs,
         for b in range(B):
             nc.scalar.activation(pos_g[b][:], pos_win[:].indirect(seq_offs[b]), ACT.Copy)
 
-        upper_g = [arena.tile([P, N], BF16, offset=AT_UPPER_G0, name="upper_g0"), sb.tile([P, N], BF16, name="upper_g1")]
+        upper_g = [sb.tile([P, N], BF16, name="upper_g%d" % b) for b in range(B)]
 
         def dealt(gathered):
             return gathered.rearrange("f (u p e) -> f p u e", u=2, e=2)
@@ -178,13 +177,10 @@ def tile_attend_draft_kernel(tc, qT, k_words, k_scales, vT, vs, pos, qpos, offs,
         def listed_halves(gathered):
             return gathered.bitcast(F32).rearrange("f (p u) -> f u p", u=2)
 
-        def lay_values(laid, turned):
-            nc.scalar.copy(laid.bitcast(F32), turned[:].rearrange("p u f -> p f u"))
+        def lay_values(laid, turned, copy=nc.scalar.copy):
+            copy(laid.bitcast(F32), turned[:].rearrange("p u f -> p f u"))
 
         upper_turned = [turn_values(listed_halves(upper_g[b][:]), tag) for b, tag in enumerate(("d0", "c1"))]
-        laid0_upper = sb.tile([P, P, PACK], BF16, align_bytes=64)
-        lay_values(laid0_upper[:], upper_turned[0])
-
         small = [sb.tile([P, N], F32, name="small%d" % b) for b in range(B)]
         masked = arena.tile([P, B, N], F32, offset=AT_MASKED)
         neg_max = [sb.tile([P, 1], F32, name="neg_max%d" % b) for b in range(B)]
@@ -209,6 +205,8 @@ def tile_attend_draft_kernel(tc, qT, k_words, k_scales, vT, vs, pos, qpos, offs,
         lower_g = [arena.tile([P, N], BF16, offset=AT_LOWER_G + 1024 * b, name="lower_g%d" % b) for b in range(B)]
         nc.vector.tensor_copy(dealt(lower_g[0][:]), lower_win[:].indirect(seq_offs[0]))
         nc.scalar.activation(lower_g[1][:], lower_win[:].indirect(seq_offs[1]), ACT.Copy)
+        laid0_upper = sb.tile([P, P, PACK], BF16, align_bytes=64)
+        lay_values(laid0_upper[:], upper_turned[0], nc.vector.tensor_copy)
         lay_values(laid0_lower[:], turn_values(lower_g[0][:].bitcast(F32).rearrange("f (u p) -> f u p", u=2), "d1"))
         lay_values(laid1_upper[:], upper_turned[1])
 

@@ -27,21 +27,20 @@ SHIFT = 16
 
 AT_KEY_SCALES = 8192
 AT_UPPER_WIN = AT_KEY_SCALES + 1024 - 4 * T
-AT_LOWER_WIN = AT_KEY_SCALES + 1024
+AT_SCALES0 = AT_KEY_SCALES + 1024
 AT_PROB = (2048, 4096)
-AT_KEY_WORDS = 24576
+AT_SCALE_WIN = 12288
+AT_LOWER_WIN = AT_SCALE_WIN
+AT_WEIGHTS1 = AT_LOWER_WIN
 AT_SCALE_COLS = 36864
-AT_INV = AT_SCALE_COLS + 1024
-AT_QUERIES = 40960
-AT_RAW_QUERIES = 57344
-AT_KEYS1 = AT_RAW_QUERIES
-AT_PLACES = (AT_RAW_QUERIES + 3072, AT_RAW_QUERIES + 5120)
-AT_RAW = tuple(AT_RAW_QUERIES + 2048 * i for i in (0, 1, 2, 4))
-AT_WORDS1 = AT_QUERIES + 3072
-AT_LOWER_G = AT_PLACES[1]
-AT_Y0 = AT_LOWER_G + 1024
-AT_MASKED = 51200
-AT_LAID = AT_MASKED
+AT_INV = AT_SCALE_COLS
+AT_RAW = (40960, 43008, 49152, 45056)
+AT_KEYS1 = AT_RAW[1]
+AT_PLACES = (AT_RAW[2] - 1024, AT_RAW[2] + 1024)
+AT_SMALL1 = AT_PLACES[0]
+AT_LOWER_G0 = AT_PLACES[1]
+AT_MASKED = 53248
+AT_AFTER_EXP = AT_MASKED
 
 
 def tile_attend_draft_kernel(tc, qT, k_words, k_scales, vT, vs, pos, qpos, offs, out):
@@ -63,22 +62,22 @@ def tile_attend_draft_kernel(tc, qT, k_words, k_scales, vT, vs, pos, qpos, offs,
         nc.gpsimd.memset(ks_win[:], 0)
         pos_cols = sb.tile([P, T // P], F32)
         nc.sync.dma_start(pos_cols[:], pos[0].rearrange("(p j) -> p j", p=P))
-        vs_win = sb.tile([P, T], F32)
+        vs_win = arena.tile([P, T], F32, offset=AT_SCALE_WIN)
         nc.sync.dma_start(vs_win[ROW:P, :], vs[0:1, :])
         ks_rows = k_scales.bitcast(I32).rearrange("o f t -> f o t")
         for r in range(4):
             nc.sync.dma_start(ks_win[r:P:SHIFT, :], ks_rows[r:16:4, :, :])
-        kw_win = arena.tile([P, T], I32, offset=AT_KEY_WORDS)
+        kw_win = sb.tile([P, T], I32)
         nc.sync.dma_start(kw_win[:], k_words[0].rearrange("p t c -> p (t c)").bitcast(I32))
         q_rows = sb.tile([P, NQ], F32)
         nc.sync.dma_start(q_rows[P - B:P, :], qpos.rearrange("b q o -> b (q o)"))
         nc.vector.memset(vs_win[0:ROW, :], 0.0)
         ks_low = sb.tile([P, B * N // 4], I32, align_bytes=64)
-        nc.vector.memset(ks_low[96:P, :], 0)
+        nc.vector.memset(ks_low[:], 0)
         q_raw = [[arena.tile([P, PACK * NQ], F32, offset=AT_RAW[PASSES * b + g],
                              name="q_raw%d%d" % (b, g)) for g in range(PASSES)] for b in range(B)]
         for b in range(B):
-            for g in range(PASSES):
+            for g in ((0, 1), (1, 0))[b]:
                 nc.sync.dma_start(q_raw[b][g][:], qT[b].rearrange("(g p j) q -> g p (j q)", p=P, j=PACK)[g])
 
         ident = sb.tile([P, P], F32)
@@ -92,79 +91,61 @@ def tile_attend_draft_kernel(tc, qT, k_words, k_scales, vT, vs, pos, qpos, offs,
                                     ident[:])
             nc.scalar.activation(pos_win[:].rearrange("q (n j) -> q n j", j=T // P)[:, :, PACK * a:PACK * (a + 1)],
                                  spread[:].rearrange("q j n -> q n j"), ACT.Copy)
-        q_places = bank("c0", [P, P])
-        nc.tensor.transpose(q_places[:], q_rows[:], ident[:])
 
-        vs_g = sb.tile([P, B * N], F32)
-        nc.vector.tensor_copy(vs_g[:], vs_win[:].indirect(offs_t[:]))
+        vs_g = [arena.tile([P, PACK, P], F32, offset=AT_SCALES0, name="vs_g0"), sb.tile([P, PACK, P], F32, name="vs_g1")]
         ks_g = sb.tile([P, B * N], U8, align_bytes=64)
+        nc.vector.tensor_copy(vs_g[1][:].rearrange("p t s -> p s t"), vs_win[:].indirect(seq_offs[1]))
         nc.vector.tensor_copy(ks_g[:], ks_win[:].bitcast(U8).indirect(offs_t[:]))
-        for lo, hi in ((0, 64), (64, 96), (96, P - SHIFT)):
-            nc.sync.dma_start(ks_low[lo:hi, :], ks_g[lo + SHIFT:hi + SHIFT, :].bitcast(I32))
+        nc.vector.tensor_copy(vs_g[0][:].rearrange("p t s -> p s t"), vs_win[:].indirect(seq_offs[0]))
+        for r in range(4):
+            nc.sync.dma_start(ks_low[r:P:32, :], ks_g[SHIFT + r:P:32, :].bitcast(I32))
         upper_win = arena.tile([P, T], F32, offset=AT_UPPER_WIN)
         nc.sync.dma_start(upper_win[:], vT[P:2 * P, :])
         lower_win = arena.tile([P, T], F32, offset=AT_LOWER_WIN)
         nc.sync.dma_start(lower_win[:], vT[0:P, :])
         ks_pass = [ks_g[:], ks_low[:].bitcast(U8)]
-        vs_col = [arena.tile([P, PACK], F32, offset=AT_SCALE_COLS + 1024 * b, name="vs_col%d" % b) for b in range(B)]
+        scale_bank = bank("c1", [P, N])
+        for m in reversed(range(B * PACK)):
+            nc.tensor.transpose(scale_bank[:, 2 * m:2 * m + P], vs_g[m // PACK][:, m % PACK, :], ident[:])
+        q_places = bank("c0", [P, P])
+        nc.tensor.transpose(q_places[:], q_rows[:], ident[:])
+
+        q_bf = [[sb.tile([P, NQ, PACK], BF16, align_bytes=64, name="q_bf%d%d" % (b, g)) for g in range(PASSES)]
+                for b in range(B)]
         for b in range(B):
-            nc.sync.dma_start(vs_col[b][:], vs_g[ROW:P, b * N:(b + 1) * N])
+            for g in ((0, 1), (1, 0))[b]:
+                nc.scalar.activation(q_bf[b][g][:].rearrange("p (c i) j -> p c j i", i=PACK),
+                                     q_raw[b][g][:].rearrange("p (j c i) -> p c j i", j=PACK, i=PACK),
+                                     ACT.Copy, scale=-1.0 / FAR)
+        vs_col = arena.tile([P, B * PACK], F32, offset=AT_SCALE_COLS)
+        nc.scalar.copy(vs_col[:], scale_bank[:, ROW:ROW + 2 * B * PACK:2])
 
-        q_bf = [[arena.tile([P, NQ, PACK], BF16, align_bytes=64, offset=AT_QUERIES + 1024 * (PASSES * b + g),
-                            name="q_bf%d%d" % (b, g)) for g in range(PASSES)] for b in range(B)]
-        def query_views(b, g):
-            return (q_bf[b][g][:].rearrange("p (c i) j -> p c j i", i=PACK),
-                    q_raw[b][g][:].rearrange("p (j c i) -> p c j i", j=PACK, i=PACK))
-
-        for b, g in ((0, 0), (0, 1), (1, 0)):
-            nc.scalar.activation(*query_views(b, g), ACT.Copy, scale=-1.0 / FAR)
-
-        kw_g = [sb.tile([P, N], U32, name="kw_g0"), arena.tile([P, N], U32, offset=AT_WORDS1, name="kw_g1")]
+        kw_g = [sb.tile([P, N], U32, name="kw_g%d" % b) for b in range(B)]
         for b in range(B):
             nc.vector.tensor_copy(kw_g[b][:], kw_win[:].bitcast(U32).indirect(seq_offs[b]))
         keys = [sb.tile([P, PASSES, 2 * N], U8, align_bytes=64, name="keys0"),
                 arena.tile([P, PASSES, 2 * N], U8, align_bytes=64, offset=AT_KEYS1, name="keys1")]
         pos_g = [arena.tile([P, N], F32, offset=AT_PLACES[b], name="pos_g%d" % b) for b in range(B)]
 
-        def split(b):
-            nc.vector.tensor_copy(keys[b][:].bitcast(U16),
-                                  kw_g[b][:].bitcast(U16).rearrange("p (n g) -> p g n", g=PASSES))
-
-        def operand(name, width):
-            return (sb.tile([P, width], U32, align_bytes=64, name=name + "_codes"),
-                    sb.tile([P, width], U8, align_bytes=64, name=name + "_scales"))
-
-        def quantise_into(into, at, laid):
-            nc.vector.quantize_mx(into[0][:, at:at + P].bitcast(FP8X4), into[1][:, at:at + P],
-                                  laid[:].rearrange("s c t -> s (c t)"))
-            return into
-
         def quantise(name, laid):
-            return quantise_into(operand(name, P), 0, laid)
+            codes = sb.tile([P, P], U32, align_bytes=64, name=name + "_codes")
+            scales = sb.tile([P, P], U8, align_bytes=64, name=name + "_scales")
+            nc.vector.quantize_mx(codes[:].bitcast(FP8X4), scales[:], laid[:].rearrange("s c t -> s (c t)"))
+            return codes, scales
 
         scores = [bank("a%d" % b, [P, N]) for b in range(B)]
-
-        def score(b, g):
-            codes, scales = quantise("q%d%d" % (b, g), q_bf[b][g])
-            nc.tensor.matmul_mx(scores[b][:], lhsT=codes[:].bitcast(FP8X4), lhsT_scale=scales[:],
-                                rhs=keys[b][:, g, :].bitcast(FP4X4), rhs_scale=ks_pass[g][:, b * N:(b + 1) * N],
-                                start=(g == 0), stop=(g == PASSES - 1))
-
-        split(0)
-        score(0, 0)
-        split(1)
-        score(0, 1)
-        nc.vector.tensor_scalar(*query_views(1, 1), -1.0 / FAR, None, ALU.mult)
-        score(1, 0)
-        score(1, 1)
+        for b in range(B):
+            nc.vector.tensor_copy(keys[b][:].bitcast(U16),
+                                  kw_g[b][:].bitcast(U16).rearrange("p (n g) -> p g n", g=PASSES))
+            for g in ((0, 1), (1, 0))[b]:
+                codes, scales = quantise("q%d%d" % (b, g), q_bf[b][g])
+                nc.tensor.matmul_mx(scores[b][:], lhsT=codes[:].bitcast(FP8X4), lhsT_scale=scales[:],
+                                    rhs=keys[b][:, g, :].bitcast(FP4X4), rhs_scale=ks_pass[g][:, b * N:(b + 1) * N],
+                                    start=(g == b), stop=(g != b))
         for b in range(B):
             nc.scalar.activation(pos_g[b][:], pos_win[:].indirect(seq_offs[b]), ACT.Copy)
 
         upper_g = [sb.tile([P, N], BF16, name="upper_g%d" % b) for b in range(B)]
-
-        def dealt(gathered):
-            return gathered.rearrange("f (u p e) -> f p u e", u=2, e=2)
-
         for b in range(B):
             nc.scalar.activation(upper_g[b][:], upper_win[:].indirect(seq_offs[b]), ACT.Copy)
 
@@ -177,19 +158,21 @@ def tile_attend_draft_kernel(tc, qT, k_words, k_scales, vT, vs, pos, qpos, offs,
         def listed_halves(gathered):
             return gathered.bitcast(F32).rearrange("f (p u) -> f u p", u=2)
 
-        def lay_values(laid, turned, copy=nc.scalar.copy):
-            copy(laid.bitcast(F32), turned[:].rearrange("p u f -> p f u"))
+        def lay_values(laid, turned, copy):
+            copy(laid[:].bitcast(F32), turned[:].rearrange("p u f -> p f u"))
+            return laid
 
-        upper_turned = [turn_values(listed_halves(upper_g[b][:]), tag) for b, tag in enumerate(("d0", "c1"))]
-        small = [sb.tile([P, N], F32, name="small%d" % b) for b in range(B)]
+        small = [sb.tile([P, N], F32, name="small0"), arena.tile([P, N], F32, offset=AT_SMALL1, name="small1")]
         masked = arena.tile([P, B, N], F32, offset=AT_MASKED)
         neg_max = [sb.tile([P, 1], F32, name="neg_max%d" % b) for b in range(B)]
         total = sb.tile([P, B], F32)
         prob = [arena.tile([P, PACK, P], F32, offset=AT_PROB[b], name="prob%d" % b) for b in range(B)]
         prob_turned = []
+        upper_turned = []
         for b in range(B):
             nc.vector.scalar_tensor_tensor(small[b][:], pos_g[b][:], q_places[:, P - B + b:P - B + b + 1], scores[b][:],
                                            ALU.is_gt, ALU.add)
+            upper_turned.append(turn_values(listed_halves(upper_g[b][:]), "a%d" % b))
             nc.vector.tensor_scalar(masked[:, b], small[b][:], FAR, None, ALU.mult, ALU.min, accum_out=neg_max[b][:])
             nc.scalar.activation(prob[b][:].rearrange("q t s -> q s t"),
                                  masked[:, b].rearrange("q (s t) -> q s t", t=PACK),
@@ -199,44 +182,46 @@ def tile_attend_draft_kernel(tc, qT, k_words, k_scales, vT, vs, pos, qpos, offs,
                 nc.tensor.transpose(turned[:, t, :], prob[b][:, t, :], ident[:])
             prob_turned.append(turned)
 
-        laid0_lower = arena.tile([P, P, PACK], BF16, align_bytes=64, offset=AT_LAID)
-        laid1_upper = arena.tile([P, P, PACK], BF16, align_bytes=64, offset=AT_LAID + 1024)
-        laid1_lower = sb.tile([P, P, PACK], BF16, align_bytes=64)
-        lower_g = [arena.tile([P, N], BF16, offset=AT_LOWER_G + 1024 * b, name="lower_g%d" % b) for b in range(B)]
-        nc.vector.tensor_copy(dealt(lower_g[0][:]), lower_win[:].indirect(seq_offs[0]))
-        nc.scalar.activation(lower_g[1][:], lower_win[:].indirect(seq_offs[1]), ACT.Copy)
-        laid0_upper = sb.tile([P, P, PACK], BF16, align_bytes=64)
-        lay_values(laid0_upper[:], upper_turned[0], nc.vector.tensor_copy)
-        lay_values(laid0_lower[:], turn_values(lower_g[0][:].bitcast(F32).rearrange("f (u p) -> f u p", u=2), "d1"))
-        lay_values(laid1_upper[:], upper_turned[1])
+        laid_u0 = arena.tile([P, P, PACK], BF16, align_bytes=64, offset=AT_LOWER_G0 + 1024)
+        laid_u1 = arena.tile([P, P, PACK], BF16, align_bytes=64, offset=AT_AFTER_EXP + 1024)
+        laid_l0 = arena.tile([P, P, PACK], BF16, align_bytes=64, offset=AT_AFTER_EXP + 2048)
+        laid_l1 = sb.tile([P, P, PACK], BF16, align_bytes=64)
+        lower_g0 = arena.tile([P, N], BF16, offset=AT_LOWER_G0)
+        lower_g1 = arena.tile([P, N], BF16, offset=AT_AFTER_EXP)
+        lay_values(laid_u0, upper_turned[0], nc.vector.tensor_copy)
+        nc.vector.tensor_copy(lower_g0[:].rearrange("f (u p e) -> f p u e", u=2, e=2), lower_win[:].indirect(seq_offs[0]))
+        nc.scalar.activation(lower_g1[:], lower_win[:].indirect(seq_offs[1]), ACT.Copy)
+        lay_values(laid_u1, upper_turned[1], nc.scalar.copy)
+        lay_values(laid_l0, turn_values(lower_g0[:].bitcast(F32).rearrange("f (u p) -> f u p", u=2), "c1"), nc.scalar.copy)
+        lay_values(laid_l1, turn_values(listed_halves(lower_g1[:]), "d0"), nc.scalar.copy)
 
-        w_bf = [sb.tile([P, NQ, PACK], BF16, align_bytes=64, name="w_bf%d" % b) for b in range(B)]
-
-        def weigh(b):
+        w_bf = [sb.tile([P, NQ, PACK], BF16, align_bytes=64, name="w_bf0"),
+                arena.tile([P, NQ, PACK], BF16, align_bytes=64, offset=AT_WEIGHTS1, name="w_bf1")]
+        for b in range(B):
             nc.vector.tensor_tensor(w_bf[b][:], prob_turned[b][:].rearrange("s t q -> s q t"),
-                                    vs_col[b][:].unsqueeze(1).to_broadcast([P, NQ, PACK]), ALU.mult)
+                                    vs_col[:, PACK * b:PACK * (b + 1)].unsqueeze(1).to_broadcast([P, NQ, PACK]), ALU.mult)
 
         def product(weights, values, tag):
-            acc = bank(tag, [P, values[0].shape[1]])
+            acc = bank(tag, [P, P])
             nc.tensor.matmul_mx(acc[:], lhsT=weights[0][:].bitcast(FP8X4), lhsT_scale=weights[1][:],
                                 rhs=values[0][:].bitcast(FP8X4), rhs_scale=values[1][:], start=True, stop=True)
             return acc
 
-        weigh(0)
-        v0 = quantise_into(operand("v0", DV), P, laid0_upper)
         w0 = quantise("w0", w_bf[0])
-        lay_values(laid1_lower[:], turn_values(listed_halves(lower_g[1][:]), "a0"))
-        weigh(1)
-        sum0 = product(w0, quantise_into(v0, 0, laid0_lower), "c0")
+        sum_u0 = product(w0, quantise("u0", laid_u0), "c1")
         w1 = quantise("w1", w_bf[1])
+        sum_u1 = product(w1, quantise("u1", laid_u1), "a1")
         inv = arena.tile([P, B], F32, offset=AT_INV)
         nc.vector.reciprocal(inv[:], total[:])
-        sum1_upper = product(w1, quantise("v1_upper", laid1_upper), "c1")
-        sum1_lower = product(w1, quantise("v1_lower", laid1_lower), "b0")
+        sum_l0 = product(w0, quantise("l0", laid_l0), "a0")
+        sum_l1 = product(w1, quantise("l1", laid_l1), "d1")
 
-        y = [arena.tile([P, DV], F32, offset=AT_Y0, name="y0"), sb.tile([P, DV], F32, name="y1")]
-        nc.scalar.activation(y[0][:], sum0[:], ACT.Copy, scale=inv[:, 0:1])
-        nc.sync.dma_start(out[0], y[0][:])
-        nc.scalar.activation(y[1][:, P:DV], sum1_upper[:], ACT.Copy, scale=inv[:, 1:2])
-        nc.vector.tensor_scalar(y[1][:, 0:P], sum1_lower[:], inv[:, 1:2], None, ALU.mult)
-        nc.sync.dma_start(out[1], y[1][:])
+        y_upper = sb.tile([P, B, P], F32)
+        y_lower = sb.tile([P, B, P], F32)
+        by_query = out.rearrange("b q e -> q b e")
+        nc.scalar.activation(y_upper[:, 0, :], sum_u0[:], ACT.Copy, scale=inv[:, 0:1])
+        nc.scalar.activation(y_upper[:, 1, :], sum_u1[:], ACT.Copy, scale=inv[:, 1:2])
+        nc.sync.dma_start(by_query[:, :, P:DV], y_upper[:])
+        nc.scalar.activation(y_lower[:, 0, :], sum_l0[:], ACT.Copy, scale=inv[:, 0:1])
+        nc.vector.tensor_scalar(y_lower[:, 1, :], sum_l1[:], inv[:, 1:2], None, ALU.mult)
+        nc.sync.dma_start(by_query[:, :, 0:P], y_lower[:])

@@ -36,7 +36,7 @@ AT_SCALE_COLS = 36864
 AT_INV = AT_SCALE_COLS
 AT_RAW = (40960, 43008, 49152, 45056)
 AT_KEYS1 = AT_RAW[1]
-AT_PLACES = (AT_RAW[2] - 1024, AT_RAW[2] + 1024)
+AT_PLACES = (57344, AT_RAW[2] + 1024)
 AT_SMALL1 = AT_PLACES[0]
 AT_LOWER_G0 = AT_PLACES[1]
 AT_MASKED = 53248
@@ -58,7 +58,7 @@ def tile_attend_draft_kernel(tc, qT, k_words, k_scales, vT, vs, pos, qpos, offs,
         nc.sync.dma_start(offs_t[:], offs)
         seq_offs = [offs_t[:, b * COLS:(b + 1) * COLS] for b in range(B)]
 
-        ks_win = arena.tile([P, T // 4], I32, offset=AT_KEY_SCALES)
+        ks_win = arena.tile([P, T // 4], I32, align_bytes=256, offset=AT_KEY_SCALES)
         nc.gpsimd.memset(ks_win[:], 0)
         pos_cols = sb.tile([P, T // P], F32)
         nc.sync.dma_start(pos_cols[:], pos[0].rearrange("(p j) -> p j", p=P))
@@ -67,13 +67,13 @@ def tile_attend_draft_kernel(tc, qT, k_words, k_scales, vT, vs, pos, qpos, offs,
         ks_rows = k_scales.bitcast(I32).rearrange("o f t -> f o t")
         for r in range(4):
             nc.sync.dma_start(ks_win[r:P:SHIFT, :], ks_rows[r:16:4, :, :])
-        kw_win = sb.tile([P, T], I32)
+        kw_win = sb.tile([P, T], I32, align_bytes=256)
         nc.sync.dma_start(kw_win[:], k_words[0].rearrange("p t c -> p (t c)").bitcast(I32))
         q_rows = sb.tile([P, NQ], F32)
         nc.sync.dma_start(q_rows[P - B:P, :], qpos.rearrange("b q o -> b (q o)"))
         nc.vector.memset(vs_win[0:ROW, :], 0.0)
-        ks_low = sb.tile([P, B * N // 4], I32, align_bytes=64)
-        nc.vector.memset(ks_low[:], 0)
+        ks_low = sb.tile([P, B * N // 4], I32, align_bytes=256)
+        nc.vector.memset(ks_low[64:P, :], 0)
         q_raw = [[arena.tile([P, PACK * NQ], F32, offset=AT_RAW[PASSES * b + g],
                              name="q_raw%d%d" % (b, g)) for g in range(PASSES)] for b in range(B)]
         for b in range(B):
@@ -93,12 +93,12 @@ def tile_attend_draft_kernel(tc, qT, k_words, k_scales, vT, vs, pos, qpos, offs,
                                  spread[:].rearrange("q j n -> q n j"), ACT.Copy)
 
         vs_g = [arena.tile([P, PACK, P], F32, offset=AT_SCALES0, name="vs_g0"), sb.tile([P, PACK, P], F32, name="vs_g1")]
-        ks_g = sb.tile([P, B * N], U8, align_bytes=64)
+        ks_g = sb.tile([P, B * N], U8, align_bytes=256)
         nc.vector.tensor_copy(vs_g[1][:].rearrange("p t s -> p s t"), vs_win[:].indirect(seq_offs[1]))
         nc.vector.tensor_copy(ks_g[:], ks_win[:].bitcast(U8).indirect(offs_t[:]))
         nc.vector.tensor_copy(vs_g[0][:].rearrange("p t s -> p s t"), vs_win[:].indirect(seq_offs[0]))
-        for r in range(4):
-            nc.sync.dma_start(ks_low[r:P:32, :], ks_g[SHIFT + r:P:32, :].bitcast(I32))
+        for lo, hi in ((0, 64), (64, 68), (96, 100)):
+            nc.sync.dma_start(ks_low[lo:hi, :], ks_g[lo + SHIFT:hi + SHIFT, :].bitcast(I32))
         upper_win = arena.tile([P, T], F32, offset=AT_UPPER_WIN)
         nc.sync.dma_start(upper_win[:], vT[P:2 * P, :])
         lower_win = arena.tile([P, T], F32, offset=AT_LOWER_WIN)
@@ -216,8 +216,8 @@ def tile_attend_draft_kernel(tc, qT, k_words, k_scales, vT, vs, pos, qpos, offs,
         sum_l0 = product(w0, quantise("l0", laid_l0), "a0")
         sum_l1 = product(w1, quantise("l1", laid_l1), "d1")
 
-        y_upper = sb.tile([P, B, P], F32)
-        y_lower = sb.tile([P, B, P], F32)
+        y_upper = sb.tile([P, B, P], F32, align_bytes=256)
+        y_lower = sb.tile([P, B, P], F32, align_bytes=256)
         by_query = out.rearrange("b q e -> q b e")
         nc.scalar.activation(y_upper[:, 0, :], sum_u0[:], ACT.Copy, scale=inv[:, 0:1])
         nc.scalar.activation(y_upper[:, 1, :], sum_u1[:], ACT.Copy, scale=inv[:, 1:2])

@@ -31,7 +31,6 @@ AT_SCALES0 = AT_KEY_SCALES + 1024
 AT_PROB = (2048, 4096)
 AT_SCALE_WIN = 12288
 AT_LOWER_WIN = AT_SCALE_WIN
-AT_WEIGHTS1 = AT_LOWER_WIN
 AT_SCALE_COLS = 36864
 AT_INV = AT_SCALE_COLS
 AT_RAW = (40960, 43008, 49152, 45056)
@@ -127,8 +126,9 @@ def tile_attend_draft_kernel(tc, qT, k_words, k_scales, vT, vs, pos, qpos, offs,
                 arena.tile([P, PASSES, 2 * N], U8, align_bytes=64, offset=AT_KEYS1, name="keys1")]
         pos_g = [arena.tile([P, N], F32, offset=AT_PLACES[b], name="pos_g%d" % b) for b in range(B)]
 
-        def quantise(name, laid):
-            codes = sb.tile([P, P], U32, align_bytes=64, name=name + "_codes")
+        def quantise(name, laid, at=None):
+            codes = (sb.tile([P, P], U32, align_bytes=64, name=name + "_codes") if at is None else
+                     arena.tile([P, P], U32, align_bytes=64, offset=at, name=name + "_codes"))
             scales = sb.tile([P, P], U8, align_bytes=64, name=name + "_scales")
             nc.vector.quantize_mx(codes[:].bitcast(FP8X4), scales[:], laid[:].rearrange("s c t -> s (c t)"))
             return codes, scales
@@ -145,18 +145,19 @@ def tile_attend_draft_kernel(tc, qT, k_words, k_scales, vT, vs, pos, qpos, offs,
         for b in range(B):
             nc.scalar.activation(pos_g[b][:], pos_win[:].indirect(seq_offs[b]), ACT.Copy)
 
+        def dealt(gathered):
+            return gathered[:].rearrange("f (u p e) -> f p u e", u=2, e=2)
+
         upper_g = [sb.tile([P, N], BF16, name="upper_g%d" % b) for b in range(B)]
         for b in range(B):
-            nc.scalar.activation(upper_g[b][:], upper_win[:].indirect(seq_offs[b]), ACT.Copy)
+            nc.scalar.activation(dealt(upper_g[b]), upper_win[:].indirect(seq_offs[b]), ACT.Copy)
 
-        def turn_values(halves, tag):
+        def turn_values(gathered, tag):
+            halves = gathered[:].bitcast(F32).rearrange("f (u p) -> f u p", u=2)
             turned = bank(tag, [P, 2, P])
             for u in range(2):
                 nc.tensor.transpose(turned[:, u, :], halves[:, u, :], ident[:])
             return turned
-
-        def listed_halves(gathered):
-            return gathered.bitcast(F32).rearrange("f (p u) -> f u p", u=2)
 
         def lay_values(laid, turned, copy):
             copy(laid[:].bitcast(F32), turned[:].rearrange("p u f -> p f u"))
@@ -172,7 +173,7 @@ def tile_attend_draft_kernel(tc, qT, k_words, k_scales, vT, vs, pos, qpos, offs,
         for b in range(B):
             nc.vector.scalar_tensor_tensor(small[b][:], pos_g[b][:], q_places[:, P - B + b:P - B + b + 1], scores[b][:],
                                            ALU.is_gt, ALU.add)
-            upper_turned.append(turn_values(listed_halves(upper_g[b][:]), "a%d" % b))
+            upper_turned.append(turn_values(upper_g[b], "a%d" % b))
             nc.vector.tensor_scalar(masked[:, b], small[b][:], FAR, None, ALU.mult, ALU.min, accum_out=neg_max[b][:])
             nc.scalar.activation(prob[b][:].rearrange("q t s -> q s t"),
                                  masked[:, b].rearrange("q (s t) -> q s t", t=PACK),
@@ -189,14 +190,13 @@ def tile_attend_draft_kernel(tc, qT, k_words, k_scales, vT, vs, pos, qpos, offs,
         lower_g0 = arena.tile([P, N], BF16, offset=AT_LOWER_G0)
         lower_g1 = arena.tile([P, N], BF16, offset=AT_AFTER_EXP)
         lay_values(laid_u0, upper_turned[0], nc.vector.tensor_copy)
-        nc.vector.tensor_copy(lower_g0[:].rearrange("f (u p e) -> f p u e", u=2, e=2), lower_win[:].indirect(seq_offs[0]))
-        nc.scalar.activation(lower_g1[:], lower_win[:].indirect(seq_offs[1]), ACT.Copy)
+        nc.vector.tensor_copy(dealt(lower_g0), lower_win[:].indirect(seq_offs[0]))
+        nc.scalar.activation(dealt(lower_g1), lower_win[:].indirect(seq_offs[1]), ACT.Copy)
         lay_values(laid_u1, upper_turned[1], nc.scalar.copy)
-        lay_values(laid_l0, turn_values(lower_g0[:].bitcast(F32).rearrange("f (u p) -> f u p", u=2), "c1"), nc.scalar.copy)
-        lay_values(laid_l1, turn_values(listed_halves(lower_g1[:]), "d0"), nc.scalar.copy)
+        lay_values(laid_l0, turn_values(lower_g0, "c1"), nc.scalar.copy)
+        lay_values(laid_l1, turn_values(lower_g1, "d0"), nc.scalar.copy)
 
-        w_bf = [sb.tile([P, NQ, PACK], BF16, align_bytes=64, name="w_bf0"),
-                arena.tile([P, NQ, PACK], BF16, align_bytes=64, offset=AT_WEIGHTS1, name="w_bf1")]
+        w_bf = [sb.tile([P, NQ, PACK], BF16, align_bytes=64, name="w_bf%d" % b) for b in range(B)]
         for b in range(B):
             nc.vector.tensor_tensor(w_bf[b][:], prob_turned[b][:].rearrange("s t q -> s q t"),
                                     vs_col[:, PACK * b:PACK * (b + 1)].unsqueeze(1).to_broadcast([P, NQ, PACK]), ALU.mult)
@@ -207,7 +207,7 @@ def tile_attend_draft_kernel(tc, qT, k_words, k_scales, vT, vs, pos, qpos, offs,
                                 rhs=values[0][:].bitcast(FP8X4), rhs_scale=values[1][:], start=True, stop=True)
             return acc
 
-        w0 = quantise("w0", w_bf[0])
+        w0 = quantise("w0", w_bf[0], AT_PROB[1])
         sum_u0 = product(w0, quantise("u0", laid_u0), "c1")
         w1 = quantise("w1", w_bf[1])
         sum_u1 = product(w1, quantise("u1", laid_u1), "a1")

@@ -58,7 +58,7 @@ def tile_attend_draft_kernel(tc, qT, k_words, k_scales, vT, vs, pos, qpos, offs,
         seq_offs = [offs_t[:, b * COLS:(b + 1) * COLS] for b in range(B)]
 
         ks_win = arena.tile([P, T // 4], I32, align_bytes=256, offset=AT_KEY_SCALES)
-        nc.gpsimd.memset(ks_win[:], 0)
+        nc.vector.memset(ks_win[:], 0)
         pos_cols = sb.tile([P, T // P], F32)
         nc.sync.dma_start(pos_cols[:], pos[0].rearrange("(p j) -> p j", p=P))
         vs_win = arena.tile([P, T], F32, offset=AT_SCALE_WIN)

@@ -1,7 +1,6 @@
 from contextlib import ExitStack
 
 import concourse.mybir as mybir
-from concourse.masks import make_identity
 
 B, N, T, D, DV, NQ = 2, 512, 2048, 1024, 256, 128
 FLOPS = 2 * B * NQ * N * (D + DV)
@@ -27,10 +26,10 @@ SHIFT = 16
 
 AT_KEY_SCALES = 8192
 AT_UPPER_WIN = AT_KEY_SCALES + 1024 - 4 * T
-AT_SCALES0 = AT_KEY_SCALES + 1024
 AT_PROB = (2048, 4096)
-AT_SCALE_WIN = 12288
-AT_LOWER_WIN = AT_SCALE_WIN
+AT_SCALE_WIN = 20480
+AT_LOWER_WIN = AT_KEY_SCALES + 1024
+AT_ZEROS = 32768
 AT_SCALE_COLS = 36864
 AT_INV = AT_SCALE_COLS
 AT_RAW = (40960, 43008, 49152, 45056)
@@ -80,8 +79,13 @@ def tile_attend_draft_kernel(tc, qT, k_words, k_scales, vT, vs, pos, qpos, offs,
                 nc.sync.dma_start(q_raw[b][g][:], qT[b].rearrange("(g p j) q -> g p (j q)", p=P, j=PACK)[g])
 
         ident = sb.tile([P, P], F32)
-        make_identity(nc, ident[:])
-        nc.gpsimd.memset(q_rows[0:P - B, :], 0.0)
+        zeros = arena.tile([P, P], F32, offset=AT_ZEROS)
+        nc.gpsimd.memset(zeros[:], 0.0)
+        nc.gpsimd.affine_select(out=ident[:], in_=zeros[:], compare_op=ALU.not_equal, fill=1.0, base=0,
+                                pattern=[[-1, P]], channel_multiplier=1)
+        nc.scalar.activation(q_rows[0:P - B, :], zeros[0:P - B, :], ACT.Copy)
+        vs_g1 = arena.tile([P, N], F32, offset=AT_ZEROS)
+        nc.scalar.activation(vs_g1[:], vs_win[:].indirect(seq_offs[1]), ACT.Copy)
         pos_win = sb.tile([P, T], F32)
         for a, tag in enumerate(("a0", "a1", "b0", "b1")):
             spread = bank(tag, [P, PACK, P])
@@ -91,11 +95,11 @@ def tile_attend_draft_kernel(tc, qT, k_words, k_scales, vT, vs, pos, qpos, offs,
             nc.scalar.activation(pos_win[:].rearrange("q (n j) -> q n j", j=T // P)[:, :, PACK * a:PACK * (a + 1)],
                                  spread[:].rearrange("q j n -> q n j"), ACT.Copy)
 
-        vs_g = [arena.tile([P, PACK, P], F32, offset=AT_SCALES0, name="vs_g0"), sb.tile([P, PACK, P], F32, name="vs_g1")]
+        vs_g0 = sb.tile([P, PACK, P], F32)
+        vs_g = [vs_g0[:], vs_g1[:].rearrange("p (s t) -> p t s", t=PACK)]
         ks_g = sb.tile([P, B * N], U8, align_bytes=256)
-        nc.vector.tensor_copy(vs_g[1][:].rearrange("p t s -> p s t"), vs_win[:].indirect(seq_offs[1]))
+        nc.vector.tensor_copy(vs_g0[:].rearrange("p t s -> p s t"), vs_win[:].indirect(seq_offs[0]))
         nc.vector.tensor_copy(ks_g[:], ks_win[:].bitcast(U8).indirect(offs_t[:]))
-        nc.vector.tensor_copy(vs_g[0][:].rearrange("p t s -> p s t"), vs_win[:].indirect(seq_offs[0]))
         for lo, hi in ((0, 64), (64, 68), (96, 100)):
             nc.sync.dma_start(ks_low[lo:hi, :], ks_g[lo + SHIFT:hi + SHIFT, :].bitcast(I32))
         upper_win = arena.tile([P, T], F32, offset=AT_UPPER_WIN)

from contextlib import ExitStack

import concourse.mybir as mybir

B, N, T, D, DV, NQ = 2, 512, 2048, 1024, 256, 128
FLOPS = 2 * B * NQ * N * (D + DV)

F32 = mybir.dt.float32
BF16 = mybir.dt.bfloat16
I32 = mybir.dt.int32
U32 = mybir.dt.uint32
U16 = mybir.dt.uint16
U8 = mybir.dt.uint8
FP8X4 = mybir.dt.float8_e4m3fn_x4
FP4X4 = mybir.dt.float4_e2m1fn_x4
ALU = mybir.AluOpType
ACT = mybir.ActivationFunctionType

P = 128
PACK = 4
PASSES = D // (P * PACK)
COLS = N // 16
FAR = float(2 ** 40)
ROW = P - 1
SHIFT = 16

AT_KEY_SCALES = 8192
AT_UPPER_WIN = AT_KEY_SCALES + 1024 - 4 * T
AT_PROB = (2048, 4096)
AT_SCALE_WIN = 20480
AT_LOWER_WIN = AT_KEY_SCALES + 1024
AT_ZEROS = 32768
AT_SCALE_COLS = 36864
AT_INV = AT_SCALE_COLS
AT_RAW = (40960, 43008, 49152, 45056)
AT_KEYS1 = AT_RAW[1]
AT_PLACES = (57344, AT_RAW[2] + 1024)
AT_SMALL1 = AT_PLACES[0]
AT_LOWER_G0 = AT_PLACES[1]
AT_MASKED = 53248
AT_AFTER_EXP = AT_MASKED


def tile_attend_draft_kernel(tc, qT, k_words, k_scales, vT, vs, pos, qpos, offs, out):
    nc = tc.nc
    with ExitStack() as ctx:
        lists = ctx.enter_context(tc.tile_pool(name="lists", bufs=1))
        sb = ctx.enter_context(tc.tile_pool(name="sb", bufs=1))
        arena = ctx.enter_context(tc.tile_pool(name="arena", bufs=1))
        ps = ctx.enter_context(tc.psum_pool(name="ps", bufs=1))

        def bank(tag, shape):
            return ps.tile(shape, F32, name=tag, tag=tag)

        offs_t = lists.tile([P, B * COLS], U16)
        nc.sync.dma_start(offs_t[:], offs)
        seq_offs = [offs_t[:, b * COLS:(b + 1) * COLS] for b in range(B)]

        ks_win = arena.tile([P, T // 4], I32, align_bytes=256, offset=AT_KEY_SCALES)
        nc.vector.memset(ks_win[:], 0)
        pos_cols = sb.tile([P, T // P], F32)
        nc.sync.dma_start(pos_cols[:], pos[0].rearrange("(p j) -> p j", p=P))
        vs_win = arena.tile([P, T], F32, offset=AT_SCALE_WIN)
        nc.sync.dma_start(vs_win[ROW:P, :], vs[0:1, :])
        ks_rows = k_scales.bitcast(I32).rearrange("o f t -> f o t")
        for r in range(4):
            nc.sync.dma_start(ks_win[r:P:SHIFT, :], ks_rows[r:16:4, :, :])
        kw_win = sb.tile([P, T], I32, align_bytes=256)
        nc.sync.dma_start(kw_win[:], k_words[0].rearrange("p t c -> p (t c)").bitcast(I32))
        q_rows = sb.tile([P, NQ], F32)
        nc.sync.dma_start(q_rows[P - B:P, :], qpos.rearrange("b q o -> b (q o)"))
        nc.vector.memset(vs_win[0:ROW, :], 0.0)
        ks_low = sb.tile([P, B * N // 4], I32, align_bytes=256)
        nc.vector.memset(ks_low[64:P, :], 0)
        q_raw = [[arena.tile([P, PACK * NQ], F32, offset=AT_RAW[PASSES * b + g],
                             name="q_raw%d%d" % (b, g)) for g in range(PASSES)] for b in range(B)]
        for b in range(B):
            for g in ((0, 1), (1, 0))[b]:
                nc.sync.dma_start(q_raw[b][g][:], qT[b].rearrange("(g p j) q -> g p (j q)", p=P, j=PACK)[g])

        ident = sb.tile([P, P], F32)
        zeros = arena.tile([P, P], F32, offset=AT_ZEROS)
        nc.gpsimd.memset(zeros[:], 0.0)
        nc.gpsimd.affine_select(out=ident[:], in_=zeros[:], compare_op=ALU.not_equal, fill=1.0, base=0,
                                pattern=[[-1, P]], channel_multiplier=1)
        nc.scalar.activation(q_rows[0:P - B, :], zeros[0:P - B, :], ACT.Copy)
        vs_g1 = arena.tile([P, N], F32, offset=AT_ZEROS)
        nc.scalar.activation(vs_g1[:], vs_win[:].indirect(seq_offs[1]), ACT.Copy)
        pos_win = sb.tile([P, T], F32)
        for a, tag in enumerate(("a0", "a1", "b0", "b1")):
            spread = bank(tag, [P, PACK, P])
            for j in range(PACK):
                nc.tensor.transpose(spread[:, j, :], pos_cols[:, PACK * a + j:PACK * a + j + 1].to_broadcast([P, P]),
                                    ident[:])
            nc.scalar.activation(pos_win[:].rearrange("q (n j) -> q n j", j=T // P)[:, :, PACK * a:PACK * (a + 1)],
                                 spread[:].rearrange("q j n -> q n j"), ACT.Copy)

        vs_g0 = sb.tile([P, PACK, P], F32)
        vs_g = [vs_g0[:], vs_g1[:].rearrange("p (s t) -> p t s", t=PACK)]
        ks_g = sb.tile([P, B * N], U8, align_bytes=256)
        nc.vector.tensor_copy(vs_g0[:].rearrange("p t s -> p s t"), vs_win[:].indirect(seq_offs[0]))
        nc.vector.tensor_copy(ks_g[:], ks_win[:].bitcast(U8).indirect(offs_t[:]))
        for lo, hi in ((0, 64), (64, 68), (96, 100)):
            nc.sync.dma_start(ks_low[lo:hi, :], ks_g[lo + SHIFT:hi + SHIFT, :].bitcast(I32))
        upper_win = arena.tile([P, T], F32, offset=AT_UPPER_WIN)
        nc.sync.dma_start(upper_win[:], vT[P:2 * P, :])
        lower_win = arena.tile([P, T], F32, offset=AT_LOWER_WIN)
        nc.sync.dma_start(lower_win[:], vT[0:P, :])
        ks_pass = [ks_g[:], ks_low[:].bitcast(U8)]
        scale_bank = bank("c1", [P, N])
        for m in reversed(range(B * PACK)):
            nc.tensor.transpose(scale_bank[:, 2 * m:2 * m + P], vs_g[m // PACK][:, m % PACK, :], ident[:])
        q_places = bank("c0", [P, P])
        nc.tensor.transpose(q_places[:], q_rows[:], ident[:])

        q_bf = [[sb.tile([P, NQ, PACK], BF16, align_bytes=64, name="q_bf%d%d" % (b, g)) for g in range(PASSES)]
                for b in range(B)]
        for b in range(B):
            for g in ((0, 1), (1, 0))[b]:
                nc.scalar.activation(q_bf[b][g][:].rearrange("p (c i) j -> p c j i", i=PACK),
                                     q_raw[b][g][:].rearrange("p (j c i) -> p c j i", j=PACK, i=PACK),
                                     ACT.Copy, scale=-1.0 / FAR)
        vs_col = arena.tile([P, B * PACK], F32, offset=AT_SCALE_COLS)
        nc.scalar.copy(vs_col[:], scale_bank[:, ROW:ROW + 2 * B * PACK:2])

        kw_g = [sb.tile([P, N], U32, name="kw_g%d" % b) for b in range(B)]
        for b in range(B):
            nc.vector.tensor_copy(kw_g[b][:], kw_win[:].bitcast(U32).indirect(seq_offs[b]))
        keys = [sb.tile([P, PASSES, 2 * N], U8, align_bytes=64, name="keys0"),
                arena.tile([P, PASSES, 2 * N], U8, align_bytes=64, offset=AT_KEYS1, name="keys1")]
        pos_g = [arena.tile([P, N], F32, offset=AT_PLACES[b], name="pos_g%d" % b) for b in range(B)]

        def quantise(name, laid, at=None):
            codes = (sb.tile([P, P], U32, align_bytes=64, name=name + "_codes") if at is None else
                     arena.tile([P, P], U32, align_bytes=64, offset=at, name=name + "_codes"))
            scales = sb.tile([P, P], U8, align_bytes=64, name=name + "_scales")
            nc.vector.quantize_mx(codes[:].bitcast(FP8X4), scales[:], laid[:].rearrange("s c t -> s (c t)"))
            return codes, scales

        scores = [bank("a%d" % b, [P, N]) for b in range(B)]
        for b in range(B):
            nc.vector.tensor_copy(keys[b][:].bitcast(U16),
                                  kw_g[b][:].bitcast(U16).rearrange("p (n g) -> p g n", g=PASSES))
            for g in ((0, 1), (1, 0))[b]:
                codes, scales = quantise("q%d%d" % (b, g), q_bf[b][g])
                nc.tensor.matmul_mx(scores[b][:], lhsT=codes[:].bitcast(FP8X4), lhsT_scale=scales[:],
                                    rhs=keys[b][:, g, :].bitcast(FP4X4), rhs_scale=ks_pass[g][:, b * N:(b + 1) * N],
                                    start=(g == b), stop=(g != b))
        for b in range(B):
            nc.scalar.activation(pos_g[b][:], pos_win[:].indirect(seq_offs[b]), ACT.Copy)

        def dealt(gathered):
            return gathered[:].rearrange("f (u p e) -> f p u e", u=2, e=2)

        upper_g = [sb.tile([P, N], BF16, name="upper_g%d" % b) for b in range(B)]
        for b in range(B):
            nc.scalar.activation(dealt(upper_g[b]), upper_win[:].indirect(seq_offs[b]), ACT.Copy)

        def turn_values(gathered, tag):
            halves = gathered[:].bitcast(F32).rearrange("f (u p) -> f u p", u=2)
            turned = bank(tag, [P, 2, P])
            for u in range(2):
                nc.tensor.transpose(turned[:, u, :], halves[:, u, :], ident[:])
            return turned

        def lay_values(laid, turned, copy):
            copy(laid[:].bitcast(F32), turned[:].rearrange("p u f -> p f u"))
            return laid

        small = [sb.tile([P, N], F32, name="small0"), arena.tile([P, N], F32, offset=AT_SMALL1, name="small1")]
        masked = arena.tile([P, B, N], F32, offset=AT_MASKED)
        neg_max = [sb.tile([P, 1], F32, name="neg_max%d" % b) for b in range(B)]
        total = sb.tile([P, B], F32)
        prob = [arena.tile([P, PACK, P], F32, offset=AT_PROB[b], name="prob%d" % b) for b in range(B)]
        prob_turned = []
        upper_turned = []
        for b in range(B):
            nc.vector.scalar_tensor_tensor(small[b][:], pos_g[b][:], q_places[:, P - B + b:P - B + b + 1], scores[b][:],
                                           ALU.is_gt, ALU.add)
            upper_turned.append(turn_values(upper_g[b], "a%d" % b))
            nc.vector.tensor_scalar(masked[:, b], small[b][:], FAR, None, ALU.mult, ALU.min, accum_out=neg_max[b][:])
            nc.scalar.activation(prob[b][:].rearrange("q t s -> q s t"),
                                 masked[:, b].rearrange("q (s t) -> q s t", t=PACK),
                                 ACT.Exp, bias=neg_max[b][:], scale=-1.0, accum_out=total[:, b:b + 1])
            turned = bank("b%d" % b, [P, PACK, NQ])
            for t in range(PACK):
                nc.tensor.transpose(turned[:, t, :], prob[b][:, t, :], ident[:])
            prob_turned.append(turned)

        laid_u0 = arena.tile([P, P, PACK], BF16, align_bytes=64, offset=AT_LOWER_G0 + 1024)
        laid_u1 = arena.tile([P, P, PACK], BF16, align_bytes=64, offset=AT_AFTER_EXP + 1024)
        laid_l0 = arena.tile([P, P, PACK], BF16, align_bytes=64, offset=AT_AFTER_EXP + 2048)
        laid_l1 = sb.tile([P, P, PACK], BF16, align_bytes=64)
        lower_g0 = arena.tile([P, N], BF16, offset=AT_LOWER_G0)
        lower_g1 = arena.tile([P, N], BF16, offset=AT_AFTER_EXP)
        lay_values(laid_u0, upper_turned[0], nc.vector.tensor_copy)
        nc.vector.tensor_copy(dealt(lower_g0), lower_win[:].indirect(seq_offs[0]))
        nc.scalar.activation(dealt(lower_g1), lower_win[:].indirect(seq_offs[1]), ACT.Copy)
        lay_values(laid_u1, upper_turned[1], nc.scalar.copy)
        lay_values(laid_l0, turn_values(lower_g0, "c1"), nc.scalar.copy)
        lay_values(laid_l1, turn_values(lower_g1, "d0"), nc.scalar.copy)

        w_bf = [sb.tile([P, NQ, PACK], BF16, align_bytes=64, name="w_bf%d" % b) for b in range(B)]
        for b in range(B):
            nc.vector.tensor_tensor(w_bf[b][:], prob_turned[b][:].rearrange("s t q -> s q t"),
                                    vs_col[:, PACK * b:PACK * (b + 1)].unsqueeze(1).to_broadcast([P, NQ, PACK]), ALU.mult)

        def product(weights, values, tag):
            acc = bank(tag, [P, P])
            nc.tensor.matmul_mx(acc[:], lhsT=weights[0][:].bitcast(FP8X4), lhsT_scale=weights[1][:],
                                rhs=values[0][:].bitcast(FP8X4), rhs_scale=values[1][:], start=True, stop=True)
            return acc

        w0 = quantise("w0", w_bf[0], AT_PROB[1])
        sum_u0 = product(w0, quantise("u0", laid_u0), "c1")
        w1 = quantise("w1", w_bf[1])
        sum_u1 = product(w1, quantise("u1", laid_u1), "a1")
        inv = arena.tile([P, B], F32, offset=AT_INV)
        nc.vector.reciprocal(inv[:], total[:])
        sum_l0 = product(w0, quantise("l0", laid_l0), "a0")
        sum_l1 = product(w1, quantise("l1", laid_l1), "d1")

        y_upper = sb.tile([P, B, P], F32, align_bytes=256)
        y_lower = sb.tile([P, B, P], F32, align_bytes=256)
        by_query = out.rearrange("b q e -> q b e")
        nc.scalar.activation(y_upper[:, 0, :], sum_u0[:], ACT.Copy, scale=inv[:, 0:1])
        nc.scalar.activation(y_upper[:, 1, :], sum_u1[:], ACT.Copy, scale=inv[:, 1:2])
        nc.sync.dma_start(by_query[:, :, P:DV], y_upper[:])
        nc.scalar.activation(y_lower[:, 0, :], sum_l0[:], ACT.Copy, scale=inv[:, 0:1])
        nc.vector.tensor_scalar(y_lower[:, 1, :], sum_l1[:], inv[:, 1:2], None, ALU.mult)
        nc.sync.dma_start(by_query[:, :, 0:P], y_lower[:])
